import numpy as np, ml_dtypes
CORES = [9,25,41,57]
N = 4
BF = ml_dtypes.bfloat16
V, H, M, CAP, R = 2560, 160, 1, 64, 5
L = M * H
def lanes(t, r):
    c = (M * (N * t + r) + np.arange(M)) & 15
    return (16 * np.arange(H)[None, :] + c[:, None]).reshape(-1)
def pack(b, x, lm):
    return {"nb": np.ascontiguousarray(b.reshape(N, 128, V)).astype(np.float32), "xs": np.ascontiguousarray(x.reshape(N, 128, V)).astype(np.float32).astype(BF),
            "lim": np.ascontiguousarray(lm.reshape(N, 128, 1)).astype(np.int32)}
def parts(rng):
    dens = rng.choice(np.array([0.08, 0.25, 0.5, 0.8]), (N, 8, 1, V)); u = rng.random((N, 8, 16, V))
    h = np.minimum((V * u * u).astype(np.int64), V - 1)
    pool = rng.integers(V // 4, V, (8, 12)); known = pool[np.arange(8)[None, :, None, None], rng.integers(0, 12, (N, 8, 16, V))]
    h = np.where(rng.random((N, 8, 16, V)) < 0.35, known, h)
    b = np.where(rng.random((N, 8, 16, V)) < dens, h, V)
    top = np.where(rng.random((N, 8, 1, V)) < 0.02, 256, rng.choice(np.array([4, 16, 40, 64]), (N, 8, 1, V)))
    x = (top * rng.random((N, 8, 16, V))).astype(np.int64)
    lm = rng.permutation(np.array([6, 16, 28, 45, 70, 110, 180, 300]))[None, :, None] + rng.integers(0, 8, (N, 8, 16))
    return b, x, lm
def late(rng, b, x, lm, g):
    E = np.stack([np.append(rng.permutation(lanes(0, r)[:-1]), lanes(0, r)[-1])[-26:] for r in range(N)])
    C = np.stack([np.append(rng.permutation(lanes(1, r)[:-1]), lanes(1, r)[-1])[-14:] for r in range(N)])
    D = np.stack([rng.permutation(np.setdiff1d(lanes(2, r), E[r]))[:4] for r in range(N)])
    low = E[:, :12]; own = E[:, 12:18]; top = E[:, 18:]; lows = low.reshape(-1)
    pool = np.setdiff1d(np.arange(V), np.concatenate([E.reshape(-1), C.reshape(-1), D.reshape(-1)]))
    b[:, g] = rng.choice(pool, (N, 16, V)); x[:, g] = rng.integers(128, 256, (N, 16, V)); lm[:, g] = rng.integers(600, 1600, (N, 16))
    for r in range(N):
        b[r, g][:, E[r]] = V; b[r, g][:, C[r, :3]] = V
    for r in range(N):
        z = rng.permutation(pool)[:12]; x[r, g][:, z] = 255; x[r, g][rng.integers(0, 16, 12), z] = 254
        b[r, g][rng.integers(0, 16, 12), low[r]] = z
        p = rng.integers(0, 16, 8); b[r, g][p, top[r]] = rng.choice(pool, 8); b[r, g][(p + rng.integers(1, 16, 8)) & 15, top[r]] = rng.choice(pool, 8)
        q = (r + 1) % N; s = C[r, :6]; k = rng.integers(0, 16, 6); j = (k + rng.integers(1, 16, 6)) & 15
        b[q, g][k, own[q]] = s; b[r, g][k, s] = s; b[r, g][j, s] = own[q]
        for i in range(8):
            n = rng.permutation(lows)[:16]; n[12 + (i & 3)] = top[q, i] if i < 4 else top[0, i]
            b[r, g][:, C[r, 6 + i]] = n
        if r < N - 1:
            for i in range(4):
                n = rng.permutation(lows)[:16]; n[int(rng.integers(0, 16))] = top[0, 4 + i]
                b[r, g][:, D[r, i]] = n
def setup_inputs(rng):
    return pack(*parts(rng))
def setup_inputs_spread(rng):
    d = rng.random((N, 8, 1, V))
    b = np.where(rng.random((N, 8, 16, V)) < d * d * d, rng.integers(0, V, (N, 8, 16, V)), V)
    x = np.minimum((np.exp2(8 * rng.random((N, 8, 1, V))) * rng.random((N, 8, 16, V))).astype(np.int64), 255)
    lm = np.minimum((np.exp2(3 + 9 * rng.random((N, 8, 1))) * (0.5 + 0.5 * rng.random((N, 8, 16)))).astype(np.int64), 4079)
    return pack(b, x, lm)
def setup_inputs_ends(rng):
    x = 255 * np.where(rng.random((N, 8, 1, V)) < 0.5, rng.integers(0, 2, (N, 8, 1, V)), rng.integers(0, 2, (N, 8, 16, V)))
    x[:, 1::2, :, :16] = 255; x[:, 1::2, :, V - 1] = 255
    mode = rng.choice(np.array([0, 0, 1, 2, 2, 2, 3, 4]), (N, 8, 1, V)); coin = rng.integers(0, 2, (N, 8, 16, V))
    v = np.arange(V)[None, :]; p = np.arange(16)[:, None]
    b = np.where(mode == 0, 0, np.where(mode == 1, V, np.where(mode == 2, coin * V, np.where(mode == 3, np.where(coin == 1, p, V - 1), rng.integers(0, V + 1, (N, 8, 16, V))))))
    b[:, 0:6:2, :, 0:16:2] = V
    b[:, 3:6:2, :, 0:16] = V; b[:, 3:6:2, 5, 0:16] = 0
    b[N - 1, 7] = np.where((v >= V - 192) & (p == ((v >> 4) & 15)), V, 0)
    big = np.array([9, 16, 8, 16, 0, 9, 12, 16])[None, :, None]
    lm = np.where(np.argsort(rng.random((N, 8, 16)), axis=2) < big, 4079, 0)
    return pack(b, x, lm)
def setup_inputs_corners(rng):
    x = rng.integers(16, 32, (N, 8, 16, V)); x[..., V - 80:V - 16] = 255; x[..., V - 16:] = 0
    pos = np.argsort(rng.random((N, 8, 16, V)), axis=2)
    many = np.where((rng.random((N, 8, 16, V)) < 0.4) | (pos < 4), rng.integers(0, V - 16, (N, 8, 16, V)), V)
    one = np.where(pos == 0, rng.integers(0, V - 80, (N, 8, 16, V)), V)
    kind = rng.choice(np.array([0, 1, 2, 2]), (N, 8, 1, V)); counts = (CAP, CAP + 1, L, CAP - 1, 1, 0, CAP, 2)
    for q in range(N):
        v = lanes(0, q)
        for g in range(8):
            n = counts[(g + 3 * q) % 8]; o = rng.permutation(L)
            kind[q, g, 0, v[o[:n]]] = 0 if g % 4 == 2 else rng.integers(0, 2, n)
            kind[q, g, 0, v[o[n:]]] = rng.integers(1, 3, L - n) if g % 4 == 2 else 2
    b = np.where(kind == 0, V, np.where(kind == 1, one, many))
    lm = 40 + rng.integers(0, 8, (N, 8, 16)); o = np.argsort(rng.random((N, 8, 16)), axis=2)
    lm[:, 1::2] = np.where(o[:, 1::2] < 9, lm[:, 1::2], 0); lm[:, 2::4] = np.where(o[:, 2::4] < 8, lm[:, 2::4], 0)
    return pack(b, x, lm)
def setup_inputs_crowd(rng):
    b, x, lm = parts(rng)
    b[:, :4] = np.where(rng.random((N, 4, 16, V)) < 0.1, rng.integers(V - 128, V, (N, 4, 16, V)), V); b[:, :4, 0, :] = 0
    v = np.arange(V)
    for t in range(16 // (N * M)):
        c = (M * (N * t + N - 1)) & 15
        b[:, 1:4:2, 0, np.flatnonzero(((v & 15) == c) & ((v >> 4) % CAP == CAP - 1))] = V
    lm[:, :4] = 4079; x[:, :2] = 255
    b[:, 4:] = np.where(b[:, 4:] < V, rng.choice(np.array([0, 1, 18, 40, V - 1]), (N, 4, 16, V)), V); b[:, 4:, :, :48] = V
    return pack(b, x, lm)
def setup_inputs_alike(rng):
    b, x, lm = parts(rng)
    u = rng.random((N, 8, 3, V)); few = np.minimum((V * u * u).astype(np.int64), V - 1)
    few[:, :, 0] = np.where(rng.random((N, 8, V)) < 0.15, np.arange(V), few[:, :, 0])
    pool = rng.integers(V // 2, V, (8, 4)); few[:, :, 2] = pool[np.arange(8)[None, :, None], rng.integers(0, 4, (N, 8, V))]
    which = np.minimum(rng.integers(0, 3, (N, 8, 16, V)), rng.integers(0, 3, (N, 8, 1, V)))
    b = np.where(rng.random((N, 8, 16, V)) < rng.choice(np.array([0.4, 0.8, 1.0]), (N, 8, 1, V)), np.take_along_axis(few, which, 2), V)
    lm = np.minimum(4 * lm, 4079)
    late(rng, b, x, lm, int(rng.integers(0, 8)))
    return pack(b, x, lm)
def check_inputs(d):
    bad = []
    for k, lo, hi in (("nb", 0, V), ("xs", 0, 255), ("lim", 0, 4079)):
        a = np.asarray(d[k]).astype(np.float64)
        if not np.all((a >= lo) & (a <= hi)): bad.append("range of " + k)
        elif not np.all(a == np.floor(a)): bad.append("whole numbers in " + k)
    return bad
def reference(nb, xs, lim):
    b = nb.astype(np.int32).reshape(N, 8, 16, V); x = xs.astype(np.float32).astype(np.int32).reshape(N, 8, 16, V)
    lm = lim.astype(np.int64).reshape(N, 8, 16, 1)
    J = np.tile(np.arange(V), (8, 1)); gone = np.zeros((8, V), bool)
    A = [0] * N; g8 = np.arange(8)[:, None, None]
    for t in range(R):
        new = []
        for r in range(N):
            v = lanes(t, r); q = b[r][:, :, v]
            has = q < V; u = np.where(has, q, 0)
            n = J[g8, u]; elem = has & gone[g8, u]; var = has & ~elem
            at = n.reshape(8, 1, 16 * L)
            Q = np.take_along_axis(b[r], at, 2).reshape(8, 16, 16, L); X = np.take_along_axis(x[r], at, 2).reshape(8, 16, 16, L)
            ek = elem[:, None]
            cov = var & np.any((Q == q[:, :, None, :]) & ek, axis=2)
            unc = var & ~cov
            deg = np.sum(np.where(unc[:, None], X, 0), axis=2) + np.max(np.where(ek, X, 0), axis=2)
            live = ~gone[:, v]
            hit = live & (np.sum(deg <= lm[r] + (A[r] & 7), axis=1) >= 9)
            piv = hit & (np.add.accumulate(hit.astype(np.int64), axis=1) <= CAP)
            col = np.minimum(np.where(unc & (q != v), q, V), np.min(np.where(ek & (Q != v), Q, V), axis=2))
            S = np.where(elem, np.sum(X, axis=1), -1); k = np.argmax(S, axis=1)
            e = np.take_along_axis(n, k[:, None, :], 1)[:, 0, :]
            b[r][:, :, v] = np.where(cov & (live & ~piv)[:, None, :], V, q)
            new.append((v, piv, col, np.minimum(deg, 255), e, piv & np.any(elem, axis=1)))
        for g in range(8):
            es = []; vs = []
            for v, piv, col, sz, e, cl in new:
                w = np.flatnonzero(piv[g]); b[:, g][:, :, v[w]] = col[g][:, w]; x[:, g][:, :, v[w]] = sz[g][:, w]; gone[g, v[w]] = True
                w = np.flatnonzero(cl[g]); es.append(e[g][w]); vs.append(v[w])
            ue, ui = np.unique(np.concatenate(es), return_index=True)
            J[g, ue] = np.concatenate(vs)[ui]
            J[g] = J[g][J[g]]
        A = [int(np.sum(a[1])) for a in new]
    return {"yn": b.reshape(N, 128, V).astype(np.float32), "yx": x.reshape(N, 128, V).astype(np.float32).astype(BF), "yj": np.stack([J] * N).astype(np.float32)}

@@ -1,0 +1,526 @@
+from concourse.bass import DstId, RemoteDMATransfer
+from concourse.mybir import AluOpType, ActivationFunctionType
+
+A = AluOpType
+F = ActivationFunctionType
+V, N, R = 2560, 4, 5
+W = 2640
+NT, XT = 3600, 3616
+EPS = 2.0 ** -10
+SL = 72
+LL = 24
+
+SCRATCH = {}
+for _d, _spec in (
+    ("float32", "NBN:3600 NU:3600 LIMF:1 THR:1 FNA:2640 FNB:2640 L1:1440 L2:1440 QF:640 QN16:640 QM:640 PREA:640 SG:640 VN:640 "
+     "QD:160 QPF:160 NE:160 QA:160 QE:2560 QE2:2560 QL:160 OC:160 CODB:160 CODA:160 DEG:160 D1:160 SD:160 U1:10 U2:10 U3:10 "
+     "THA:10 THW:10 CW:10 CW1:10 LV:64 LVM:64 LVS:64 DM64:64 TS:1024 EW:4 EO:24 TR4:4 QG:1024 NS:1024 XSA:288 XSS:288 ZERO:64 "
+     "YJ:2560 MASKI:256 LANE:160 PREB:160 I16:10 TC:64 IDF:128"),
+    ("bfloat16", "XSN:3616 XEA:2640 XEB:2640 SGN:2560 EQ:2560 UNC:2560 XEG:2560 MXS:2560 XVG:2560 NONEL:160 WW:160 CV:160 CV2:160 "
+     "AXR:160 LIVE:160 MP:160 OK:160 HX:12 XSC:12 ONES:128 TM:1 AXC:1024 SGC:1024 TF:64 DC:256 DS:256 MM:1024 RM:2560 RN:2560 "
+     "R64:256 BIAS:512 MASKJ:256 G1:128 GG:128 TRI:128 ID:128 IDB:128 GS:128 GJ:128 GN:128 BM:2048 JM:2048 DM:2048"),
+    ("int32", "LIMI:1 AI:1 AJ:1 QI:160 QI2:160 QI3:160 CA:320 CB:320 CBI:64 C1:64 C2:64 C3:64 C4:64 TI:64 TB:64 EXPI:160 TCI:16"),
+    ("uint16", "JL:160 L3:480 QPU:640 QLU:160 SLU:10 QCU:64 EXPL:160"),
+):
+    for _e in _spec.split():
+        SCRATCH[_e.split(":")[0]] = ("sbuf", [128, int(_e.split(":")[1])], _d)
+for _e in "pD pE pC pM pW pN0 pN1".split():
+    SCRATCH[_e] = ("psum", [128, 512], "float32")
+SEMAPHORES = ["v", "s", "t", "p", "lo", "d_nb0", "d_nb1", "d_xs", "d_lim", "d_yn", "d_yx", "d_yj"] + [
+    "a%d_%d_%d" % (k, t, q) for k in (1, 2, 3) for t in range(R) for q in range(N)]
+
+
+def queues(g, T):
+    eng = {"v": g.vector, "s": g.scalar, "t": g.tensor, "p": g, "y": g.sync}
+    cnt = {"v": 0, "s": 0, "t": 0, "p": 0}
+    know = {q: {} for q in eng}
+    lastw, readers, dmas = {}, {}, {}
+
+    def wait(q, tok):
+        sem, val, clock, _ = tok
+        if know[q].get(sem, 0) < val:
+            eng[q].wait_ge(T.sem[sem], val)
+            know[q][sem] = val
+        for k, n in clock.items():
+            if know[q].get(k, 0) < n:
+                know[q][k] = n
+
+    def before(q, R_, W_):
+        toks = [lastw[k] for k in R_ if k in lastw]
+        for k in W_:
+            toks += [x for x in list(readers.get(k, {}).values()) + ([lastw[k]] if k in lastw else [])
+                     if not (x[3] == q and q == "t")]
+        for tok in sorted(toks, key=lambda x: -x[1]):
+            wait(q, tok)
+
+    def after(tok, R_, W_):
+        for k in W_:
+            lastw[k] = tok
+            readers[k] = {}
+        for k in R_:
+            readers.setdefault(k, {})[tok[0]] = tok
+
+    def op(q, fns, R_=(), W_=()):
+        before(q, R_, W_)
+        for f in (fns if isinstance(fns, list) else [fns]):
+            ins = f()
+        cnt[q] += 1
+        ins.then_inc(T.sem[q], 1)
+        after((q, cnt[q], dict(know[q]), q), R_, W_)
+
+    def dma(q, sem, fns, R_=(), W_=()):
+        before(q, R_, W_)
+        for f in fns:
+            dmas[sem] = dmas.get(sem, 0) + 16
+            f().then_inc(T.sem[sem], 16)
+        after((sem, dmas[sem], dict(know[q]), "dma"), R_, W_)
+
+    def arrive(sem, n, W_):
+        dmas[sem] = n
+        after((sem, n, {}, "far"), (), W_)
+
+    def finish(extra):
+        for sem, n in list(cnt.items()) + list(dmas.items()) + extra:
+            if n and know["y"].get(sem, 0) < n:
+                g.sync.wait_ge(T.sem[sem], n)
+
+    return op, dma, arrive, finish, before
+
+
+def rank_program(g, core, T, topo):
+    r = T.rank_of(core)
+    if r is None:
+        return
+    vec, sca, ten = g.vector, g.scalar, g.tensor
+    op, dma, arrive, finish, before = queues(g, T)
+    others = [d for d in T.cores if d != core]
+
+    def cp(out, in_, R_, W_):
+        op("v", lambda: vec.tensor_copy(out=out, in_=in_), R_, W_)
+
+    def tt(out, a, b, o, R_, W_):
+        op("v", lambda: vec.tensor_tensor(out=out, in0=a, in1=b, op=o), R_, W_)
+
+    def ts(out, a, s1, o1, s2, o2, R_, W_):
+        if o2 is None:
+            op("v", lambda: vec.tensor_scalar(out=out, in0=a, scalar1=s1, scalar2=None, op0=o1), R_, W_)
+        else:
+            op("v", lambda: vec.tensor_scalar(out=out, in0=a, scalar1=s1, scalar2=s2, op0=o1, op1=o2), R_, W_)
+
+    def scan(out, d0, d1, o0, o1, R_, W_):
+        op("v", lambda: vec.tensor_tensor_scan(out=out, data0=d0, data1=d1, initial=0.0, op0=o0, op1=o1), R_, W_)
+
+    def fill(ap, x, W_):
+        op("v", lambda: vec.memset(ap, x), (), W_)
+
+    def act(out, in_, R_, W_, func=F.Copy, **kw):
+        op("s", lambda: sca.activation(out, in_, func, **kw), R_, W_)
+
+    def iota(out, pattern, base, cm, W_):
+        op("p", lambda: g.iota(out, pattern, base, cm, allow_small_or_imprecise_dtypes=True), (), W_)
+
+    def mm(out, l, rr, st, sp):
+        return lambda: ten.matmul(out, l, rr, st, sp)
+
+    def tab(name, a, b, *more):
+        return [(name, x) for x in range(a, b)] + [(name, x) for x in more]
+
+    def whole(name):
+        return tab(name, 0, 16, "n")
+    M16 = range(16)
+    NB, XS = ["NB0", "NB1"], ["XS", "XS0"]
+    BMk, DMk = [("BM", m) for m in M16], [("DM", m) for m in M16]
+
+    dma("y", "d_nb0", [lambda: g.sync.dma_start(T.NBN[:, 0:1280], T.nb[:, 0:1280])], (), ["NB0"])
+    dma("s", "d_nb1", [lambda: g.scalar.dma_start(T.NBN[:, 1280:2560], T.nb[:, 1280:2560])], (), ["NB1"])
+    dma("y", "d_xs", [lambda: g.sync.dma_start(T.XSN[:, 16:2576], T.xs[:])], (), ["XS"])
+    dma("s", "d_lim", [lambda: g.scalar.dma_start(T.LIMI[:], T.lim[:])], (), ["LIMI"])
+
+    iota(T.TCI[:, 0:1], [[1, 1]], 0, 1, ["TCI"])
+    iota(T.LANE[:], [[1, 160]], 0, 0, ["LANE"])
+    fill(T.ONES[:], 1.0, ["ONES"])
+    ones = T.ONES[:]
+    op("p", lambda: g.affine_select(T.ID[:], ones, [[-1, 128]], A.is_equal, 0.0, 0, 1), ["ONES"], ["ID"])
+    op("p", lambda: g.affine_select(T.G1[:], ones, [[-16, 8], [0, 16]], A.is_ge, 0.0, 0, 1), ["ONES"], ["G1"])
+    op("p", lambda: g.affine_select(T.GG[:], T.G1[:], [[16, 8], [0, 16]], A.is_ge, 0.0, 15, -1), ["G1"], ["GG"])
+    iota(T.I16[:], [[16, 10]], 0, 0, ["I16"])
+    op("p", lambda: g.affine_select(T.TRI[:], T.GG[:], [[1, 128]], A.is_ge, 0.0, 0, -1), ["GG"], ["TRI"])
+    iota(T.EXPI[:], [[1, 160]], 0, 0, ["EXPI"])
+    iota(T.CBI[:], [[1, 64]], 2560 * 256 + 161, 0, ["CBI"])
+    iota(T.TC[:, 40:44], [[16, 4]], 2576, 0, ["T40"])
+    iota(T.LVM[:], [[0, 4], [1, 16]], 0, 0, ["LVM"])
+    iota(T.MASKI[:], [[-16, 4], [1, 64]], 0, 0, ["MASKI"])
+    iota(T.BIAS[:], [[0, 32], [-4, 16]], 61, 0, ["BIAS"])
+    iota(T.FNA[:], [[0, W]], V, 0, whole("FNA"))
+    iota(T.NU[:, 0:V], [[1, V]], 0, 0, ["NU"])
+    fill(T.XSN[:, 0:16], 0.0, ["XS0"])
+    fill(T.XSN[:, 2576:2592], 0.0, ["XS0"])
+    fill(T.BM[:], 0.0, BMk)
+    fill(T.DM[:], 0.0, DMk)
+    for m in M16:
+        act(T.BM[:, 128 * m + m:128 * m + 128:16], T.GG[:, m:128:16], ["GG"], [("BM", m)])
+    for m in M16:
+        act(T.DM[:, 128 * m + m:128 * m + 128:16], T.ID[:, m:128:16], ["ID"], [("DM", m)])
+    ts(T.TCI[:, 1:2], T.TCI[:, 0:1], 15, A.bitwise_and, None, None, ["TCI"], ["TCI1"])
+    for b in range(4):
+        ts(T.TCI[:, 4 + b:5 + b], T.TCI[:, 1:2], b, A.logical_shift_right, 1, A.bitwise_and, ["TCI1"], ["TCB%d" % b])
+    cp(T.TC[:, 0:1], T.TCI[:, 1:2], ["TCI1"], ["PM"])
+    for b in range(4):
+        up = float(2 ** (2 ** b))
+        ts(T.TC[:, 12 + b:13 + b], T.TCI[:, 4 + b:5 + b], up - 1.0, A.mult, 1.0, A.add, ["TCB%d" % b], ["UP%d" % b])
+        ts(T.TC[:, 16 + b:17 + b], T.TCI[:, 4 + b:5 + b], 1.0 / up - 1.0, A.mult, 1.0, A.add, ["TCB%d" % b], ["DN%d" % b])
+    for nm, c0, d in (("UP", 12, 1), ("DN", 16, 2)):
+        tt(T.TC[:, 20 + d:21 + d], T.TC[:, c0:c0 + 1], T.TC[:, c0 + 1:c0 + 2], A.mult, [nm + "0", nm + "1"], [nm + "a"])
+        tt(T.TC[:, 24 + d:25 + d], T.TC[:, c0 + 2:c0 + 3], T.TC[:, c0 + 3:c0 + 4], A.mult, [nm + "2", nm + "3"], [nm + "b"])
+        tt(T.TC[:, d:d + 1], T.TC[:, 20 + d:21 + d], T.TC[:, 24 + d:25 + d], A.mult, [nm + "a", nm + "b"], [nm])
+    pm, up, dn = T.TC[:, 0:1], T.TC[:, 1:2], T.TC[:, 2:3]
+    cp(T.EXPL[:], T.EXPI[:], ["EXPI"], ["EXPL"])
+    ts(T.PREB[:], T.LANE[:], float(2560 * 256), A.add, None, None, ["LANE"], ["PREB"])
+
+    def signs(k):
+        c = 4 * k + r
+        s = slice(160 * k, 160 * k + 160)
+        ts(T.QD[:], T.LANE[:], float(256 * (15 - c)), A.add, None, None, ["LANE"], ["QD"])
+        ts(T.VN[:, s], T.LANE[:], 16.0, A.mult, float(c), A.add, ["LANE"], ["VN%d" % k])
+        ts(T.QPF[:], T.QD[:], dn, A.mult, -0.495, A.add, ["QD", "DN"], ["QPF"])
+        cp(T.QI[:], T.QPF[:], ["QPF"], ["QI"])
+        ts(T.QI2[:], T.QI[:], 1, A.bitwise_and, None, None, ["QI"], ["QI2"])
+        ts(T.SG[:, s], T.QI2[:], 2.0, A.mult, -1.0, A.add, ["QI2"], ["SG%d" % k])
+    for k in range(4):
+        signs(k)
+    ts(T.TC[:, 8:9], pm, 7.5, A.is_lt, 0.5, A.mult, ["PM"], ["W0"])
+    ts(T.TC[:, 9:10], pm, 11.5, A.is_lt, 0.5, A.mult, ["PM"], ["W1"])
+    ts(T.TC[:, 10:11], pm, 12.0, A.is_equal, None, None, ["PM"], ["W2"])
+    ts(T.TC[:, 11:12], pm, 13.0, A.is_equal, -2040.0, A.mult, ["PM"], ["W3"])
+    tt(T.TC[:, 28:29], T.TC[:, 8:9], up, A.mult, ["W0", "UP"], ["W4"])
+    tt(T.TC[:, 29:30], T.TC[:, 9:10], up, A.mult, ["W1", "UP"], ["W5"])
+    ts(T.TC[:, 45:46], T.TC[:, 10:11], 2.0 * EPS, A.mult, -EPS, A.add, ["W2"], ["NX"])
+    ts(T.TC[:, 32:33], T.TC[:, 10:11], 1280.0, A.mult, None, None, ["W2"], ["W8"])
+    tt(T.TC[:, 30:31], T.TC[:, 29:30], T.TC[:, 28:29], A.subtract, ["W4", "W5"], ["W6"])
+    ts(T.TC[:, 37:38], T.TC[:, 10:11], -7.5, A.mult, None, None, ["W2"], ["WC"])
+    ts(T.TC[:, 35:36], T.TC[:, 28:29], 16.0, A.mult, None, None, ["W4"], ["WA"])
+    ts(T.TC[:, 31:32], T.TC[:, 30:31], 160.0 / 256.0, A.mult, None, None, ["W6"], ["W7"])
+    ts(T.TC[:, 36:37], T.TC[:, 30:31], -1.0 / 256.0, A.mult, None, None, ["W6"], ["WB"])
+    tt(T.TC[:, 39:40], T.TC[:, 37:38], T.TC[:, 11:12], A.add, ["WC", "W3"], ["WE"])
+    tt(T.TC[:, 33:34], T.TC[:, 31:32], T.TC[:, 28:29], A.add, ["W7", "W4"], ["W9"])
+    tt(T.TC[:, 38:39], T.TC[:, 35:36], T.TC[:, 36:37], A.add, ["WA", "WB"], ["WD"])
+    tt(T.TC[:, 34:35], T.TC[:, 33:34], T.TC[:, 32:33], A.add, ["W8", "W9"], ["WJ"])
+    tt(T.TC[:, 44:45], T.TC[:, 38:39], T.TC[:, 39:40], A.add, ["WD", "WE"], ["WN"])
+    nx = T.TC[:, 45:46]
+    ts(T.CW1[:], T.I16[:], pm, A.add, 160.0, A.add, ["I16", "PM"], ["CW1"])
+    ts(T.CW[:], T.CW1[:], 1.0, A.add, None, None, ["CW1"], ["CW"])
+    fill(T.HX[:], 0.0, ["HX"])
+    fill(T.RM[:], 1.0, ["RM"])
+    fill(T.RM[:, 0:2560:16], 0.0, ["RM"])
+    fill(T.CA[:, 0:64], V * 1024 + 512, ["CA"])
+    cp(T.CB[:, 0:64], T.CBI[:], ["CBI"], ["CB"])
+    cp(T.LIMF[:], T.LIMI[:], ["LIMI"], ["LIMF"])
+    cp(T.THR[:], T.LIMF[:], ["LIMF"], ["THR"])
+
+    made = []
+
+    def own_s1(k):
+        s = slice(160 * k, 160 * k + 160)
+        if k not in made:
+            act(T.QF[:, s], T.NBN[:, 4 * k + r:V:16], NB, ["QF%d" % k])
+            act(T.QA[:], T.QF[:, s], ["QF%d" % k], ["QA"], scale=256.0, bias=-655360.0)
+        made.append(k)
+
+    def own_v1(k):
+        s = slice(160 * k, 160 * k + 160)
+        tt(T.NE[:], T.QF[:, s], T.VN[:, s], A.not_equal, ["QF%d" % k, "VN%d" % k], ["NE"])
+        tt(T.QM[:, s], T.QA[:], T.NE[:], A.mult, ["QA", "NE"], ["QM%d" % k])
+
+    def own_v2(k):
+        s = slice(160 * k, 160 * k + 160)
+        cp(T.QI[:], T.QF[:, s], ["QF%d" % k], ["QI"])
+        ts(T.QI2[:], T.QI[:], 15, A.bitwise_and, None, None, ["QI"], ["QI2"])
+        ts(T.QI3[:], T.QI[:], 4, A.logical_shift_right, None, None, ["QI"], ["QI3"])
+        ts(T.QD[:], T.QI2[:], -160.0, A.mult, 2400.0, A.add, ["QI2"], ["QD"])
+        tt(T.QPF[:], T.QD[:], T.QI3[:], A.add, ["QD", "QI3"], ["QPF"])
+        cp(T.QPU[:, s], T.QPF[:], ["QPF"], ["QPU%d" % k])
+
+    def own_s2(k):
+        s = slice(160 * k, 160 * k + 160)
+        act(T.QN16[:, s], T.QF[:, s], ["QF%d" % k], ["QN%d" % k], bias=16.0)
+        act(T.PREA[:, s], T.QPF[:], ["QPF"], ["PREA%d" % k], scale=1024.0, bias=512.0)
+
+    def expand(k, name, h):
+        act(T[name][:, 1280 * h:1280 * h + 1280], T.QF[:, 160 * k:160 * k + 160].indirect(T.EXPL[:, 80 * h:80 * h + 80]),
+            ["QF%d" % k, "EXPL"], [name + str(h)])
+
+    mask = topo.mask(core, others[0])
+    for d in others:
+        mask &= topo.mask(core, d)
+    neng = len([e for e in topo.engines(core, others[0]) if mask >> e & 1])
+    ids = [DstId(rid=topo.addr(d)[0], pnc=topo.addr(d)[1]) for d in others]
+    nsend = [0]
+
+    def send(kind, t, buf, w, n):
+        ap = T[buf][:, (4 * t + r) * w:(4 * t + r) * w + n]
+        before("p", [(buf, t, r)], ())
+        g.remote_dma_fused([RemoteDMATransfer(dst_ids=ids, dma_engine_mask=mask, remote_sem=T.sem["a%d_%d_%d" % (kind, t, r)],
+                                              srcs=[ap], dsts=[ap for d in others])], local_sem=T.sem["lo"])
+        nsend[0] += neng
+    for t in range(R):
+        for q in range(N):
+            if q != r:
+                for kind, buf in ((1, "L1"), (2, "L2"), (3, "L3")):
+                    arrive("a%d_%d_%d" % (kind, t, q), neng, [(buf, t, q)])
+
+    def l1(t, q, a=0, b=64):
+        return T.L1[:, (4 * t + q) * SL + a:(4 * t + q) * SL + b]
+
+    def l2(t, q, a=0, b=64):
+        return T.L2[:, (4 * t + q) * SL + a:(4 * t + q) * SL + b]
+
+    def l3(t, q, a, b):
+        return T.L3[:, (4 * t + q) * LL + a:(4 * t + q) * LL + b]
+
+    def keep_sizes(t):
+        act(T.XSA[:], T.L1[:, 4 * t * SL:4 * (t + 1) * SL], [("L1", t, q) for q in range(N)], ["XSA"], func=F.Abs)
+        act(T.XSS[:], T.XSA[:], ["XSA"], ["XSS"], bias=-1.0)
+
+    def store_sizes(t):
+        for q in range(N):
+            cp(T.XSN[:, 16:XT].indirect(l3(t, q, 14, 18)), T.XSS[:, SL * q:SL * q + 64], ["XSS", ("L3", t, q)], XS)
+
+    def store_names(t):
+        for q in range(N):
+            cp(T.NBN[:, 0:NT].indirect(l3(t, q, 14, 18)), l2(t, q), [("L2", t, q), ("L3", t, q)], NB)
+
+    def store_gone(t):
+        for q in range(N):
+            cp(T.NU[:, 0:NT].indirect(l3(t, q, 14, 18)), T.ZERO[:], ["ZERO", ("L3", t, q)], ["NU"])
+
+    PARTS = ((0, 48, "s"), (48, 96, "s"), (96, 160, "v"))
+    ts(T.QLU[:], T.NBN[:, r:V:16], 16.0, A.add, None, None, NB, ["QLU"])
+
+    cur, nxt = "A", "B"
+    for t in range(R):
+        k = t % 4
+        k1 = (t + 1) % 4
+        ks = slice(160 * k, 160 * k + 160)
+        lo = 640 * (4 - t)
+        n = V - lo
+        fn, xe = T["FN" + cur], T["XE" + cur]
+        qe, qe1 = ("QE", "QE2") if t % 2 else ("QE2", "QE")
+        FNk, XEk = whole("FN" + cur), whole("XE" + cur)
+        if t:
+            for h in range(2):
+                s, l = slice(1280 * h, 1280 * h + 1280), T.QPU[:, 160 * k + 80 * h:160 * k + 80 * h + 80]
+                act(T.XEG[:, s], xe[:, 0:2576].indirect(l), XEk + ["QPU%d" % k], ["XEG%d" % h], func=F.Abs)
+                tt(T.EQ[:, s], fn[:, 0:2576].indirect(l), T[qe][:, s], A.not_equal, FNk + ["QPU%d" % k, qe + str(h)], ["EQ%d" % h])
+                op("t", [mm(T.pE[:, 80 * h:80 * h + 80], T.DM[:, 128 * j:128 * j + 128], T.XEG[:, 1280 * h + j:1280 * h + 1280:16],
+                            j == 0, j == 15) for j in M16], DMk + ["XEG%d" % h], ["pE"])
+            scan(T.UNC[:], T.RN[:], T.EQ[:], A.max, A.min, ["RN", "EQ0", "EQ1"], ["UNC"])
+            ts(T.NONEL[:], T.pE[:, 0:160], 0.5, A.is_lt, None, None, ["pE"], ["NONEL"])
+            tt(T.WW[:], T.UNC[:, 15:V:16], T.NONEL[:], A.mult, ["UNC", "NONEL"], ["WW"])
+            tt(T.QL[:], T.QN16[:, ks], T.WW[:], A.mult, ["QN%d" % k, "WW"], ["QL"])
+            cp(T.QLU[:], T.QL[:], ["QL"], ["QLU"])
+        for a, b, q in PARTS:
+            o, i = T.XVG[:, 16 * a:16 * b], T.XSN[:, 0:2592].indirect(T.QLU[:, a:b])
+            if q == "s":
+                act(o, i, XS + ["QLU"], ["XVG%d" % a])
+            else:
+                cp(o, i, XS + ["QLU"], ["XVG%d" % a])
+        for a, b, q in (PARTS[0], PARTS[2], PARTS[1]):
+            op("t", [mm(T.pD[:, a:b], T.ID[:], T.XVG[:, 16 * a + j:16 * b:16], j == 0, j == 15) for j in M16],
+               ["ID", "XVG%d" % a], ["pD"])
+        if t:
+            scan(T.MXS[:], T.RM[:], T.XEG[:], A.mult, A.max, ["RM", "XEG0", "XEG1"], ["MXS"])
+            tt(T.OC[:], T.QM[:, ks], T.WW[:], A.mult, ["QM%d" % k, "WW"], ["OC"])
+            ts(T.MP[:], T.MXS[:, 15:V:16], 1.0, A.max, 1.0, A.subtract, ["MXS"], ["MP"])
+            tt(T.CODB[:], T.OC[:], T.PREB[:], A.add, ["OC", "PREB"], ["CODB"])
+            if t >= 2:
+                act(T.SGN[:, lo:V], xe[:, lo:V], tab("XE" + cur, lo // 160, 16), ["SGN"], func=F.Sign)
+            if t < 4:
+                own_s1(k1)
+                expand(k1, qe1, 0)
+            tt(T.DEG[:], T.pD[:, 0:160], T.MP[:], A.add, ["pD", "MP"], ["DEG"])
+        else:
+            own_s1(0)
+            own_v1(0)
+            tt(T.CODB[:], T.QM[:, ks], T.PREB[:], A.add, ["QM0", "PREB"], ["CODB"])
+            act(T.XEA[:], T.FNA[:], whole("FNA") + ["NX"], whole("XEA"), func=F.Identity, scale=0.0, bias=nx)
+            own_s1(1)
+            expand(1, qe1, 0)
+            expand(1, qe1, 1)
+            ts(T.DM64[:], T.LVM[:], pm, A.is_equal, None, None, ["LVM", "PM"], ["DM64"])
+            ts(T.TR4[:], T.TC[:, 40:44], pm, A.add, None, None, ["T40", "PM"], ["TR4"])
+            fill(T.ZERO[:], 0.0, ["ZERO"])
+            cp(T.DEG[:], T.pD[:, 0:160], ["pD"], ["DEG"])
+        ts(T.OK[:], T.DEG[:], T.THR[:], A.is_le, None, None, ["DEG", "THR"], ["OK"])
+        op("t", [mm(T.pC[:, 0:10], T.BM[:, 128 * m:128 * m + 128], T.OK[:, m:160:16], m == 0, m == 15) for m in M16], BMk + ["OK"], ["pC"])
+        ts(T.D1[:], T.DEG[:], 255.0, A.min, 1.0, A.add, ["DEG"], ["D1"])
+        tt(T.SD[:], T.D1[:], T.SG[:, ks], A.mult, ["D1", "SG%d" % k], ["SD"])
+        if t:
+            tt(T.CODA[:], T.SD[:], T.PREA[:, ks], A.add, ["SD", "PREA%d" % k], ["CODA"])
+        else:
+            ts(T.CODA[:], T.SD[:], 512.0, A.add, None, None, ["SD"], ["CODA"])
+        if t < 4:
+            ts(T.HX[:, 1:11], T.pC[:, 0:10], 8.5, A.is_ge, None, None, ["pC"], ["HX"])
+        else:
+            tt(T.HX[:, 1:11], T.pC[:, 0:10], T.THW[:], A.is_ge, ["pC", "THW"], ["HX"])
+        scan(T.XSC[:, 0:11], T.ONES[:, 0:11], T.HX[:, 0:11], A.mult, A.add, ["ONES", "HX"], ["XSC"])
+        op("t", [mm(T.pC[:, 16:26], T.TRI[:], T.HX[:, 1:11], True, False), mm(T.pC[:, 16:26], T.GG[:], T.XSC[:, 0:10], False, True),
+                 mm(T.pC[:, 32:33], T.GG[:], T.XSC[:, 10:11], True, True)], ["TRI", "GG", "HX", "XSC"], ["pC"])
+        tt(T.U1[:], T.pC[:, 16:26], T.CW[:], A.subtract, ["pC", "CW"], ["U1"])
+        tt(T.U2[:], T.U1[:], T.HX[:, 1:11], A.mult, ["U1", "HX"], ["U2"])
+        tt(T.U3[:], T.U2[:], T.CW1[:], A.add, ["U2", "CW1"], ["U3"])
+        cp(T.SLU[:], T.U3[:], ["U3"], ["SLU"])
+        L1k, L2k, L3k = ("L1", t, r), ("L2", t, r), ("L3", t, r)
+        cp(T.CA[:, 0:320].indirect(T.SLU[:]), T.CODA[:], ["SLU", "CODA"], ["CA"])
+        if t:
+            if t >= 2:
+                op("t", [mm(T.pW[:, 16:16 + n // 16], T.JM[:, 128 * m:128 * m + 128], T.SGN[:, lo + m:V:16], m == 0, m == 15) for m in M16],
+                   ["JM", "SGN"], ["pW"])
+            ts(T.C1[:], T.CA[:, 0:64], 10, A.logical_shift_right, None, None, ["CA"], ["C1"])
+            cp(T.QCU[:], T.C1[:], ["C1"], ["QCU"])
+            hs = [(b, slice(512 * b, 512 * b + 512), T.QCU[:, 32 * b:32 * b + 32]) for b in range(2)]
+            for b, s, l in hs:
+                act(T.QG[:, s], fn[:, 0:2576].indirect(l), FNk + ["QCU"], ["QG%d" % b])
+                op("t", mm(T["pN%d" % b][:], T.IDF[:], T.QG[:, s], True, False), ["IDF", "QG%d" % b], ["pN%d" % b])
+            for b, s, l in hs:
+                bank = ("pD", "pE")[b]
+                act(T.AXC[:, s], xe[:, 0:2576].indirect(l), XEk + ["QCU"], ["AXC%d" % b], func=F.Abs)
+                act(T.SGC[:, s], xe[:, 0:2576].indirect(l), XEk + ["QCU"], ["SGC%d" % b], func=F.Sign)
+                op("t", [mm(T[bank][:], T.ID[:], T.BIAS[:], True, False), mm(T[bank][:], T.GS[:], T.AXC[:, s], False, False),
+                         mm(T[bank][:], T.ID[:], T.SGC[:, s], False, True)], ["ID", "BIAS", "SGC%d" % b, "GS", "AXC%d" % b], [bank])
+        ts(T.C2[:], T.CA[:, 0:64], 1023, A.bitwise_and, None, None, ["CA"], ["C2"])
+        ts(l1(t, r), T.C2[:], 512.0, A.subtract, None, None, ["C2"], [L1k])
+        ts(l1(t, r, 64, SL), T.BIAS[:, 0:8], 0.0, A.mult, nx, A.add, ["BIAS", "NX"], [L1k])
+        send(1, t, "L1", SL, SL)
+        cp(T.CB[:, 0:320].indirect(T.SLU[:]), T.CODB[:], ["SLU", "CODB"], ["CB"])
+        fill(l2(t, r, 64, SL), float(V), [L2k])
+        ts(T.C3[:], T.CB[:, 0:64], 8, A.logical_shift_right, None, None, ["CB"], ["C3"])
+        ts(T.C4[:], T.CB[:, 0:64], 255, A.bitwise_and, None, None, ["CB"], ["C4"])
+        if t == 0:
+            cp(l2(t, r), T.C3[:], ["C3"], [L2k])
+            send(2, t, "L2", SL, SL)
+        ts(T.LV[:], T.C4[:], 16.0, A.mult, float(4 * k + r), A.add, ["C4"], ["LV"])
+        ts(l3(t, r, 4, 14), T.U3[:], 64.0, A.min, None, None, ["U3"], [L3k])
+        if t:
+            for b, s, l in hs:
+                tt(T.MM[:, s], T.LV[:, 0:64].indirect(T.EXPL[:, 32 * b:32 * b + 32]), T.QG[:, s], A.is_equal, ["LV", "EXPL", "QG%d" % b], ["MM%d" % b])
+                op("t", mm(T["pN%d" % b][:], T.IDB[:], T.MM[:, s], False, True), ["IDB", "MM%d" % b], ["pN%d" % b])
+        tt(T.LVM[:], T.LV[:], T.DM64[:], A.mult, ["LV", "DM64"], ["LVM"])
+        scan(T.LVS[:], T.RM[:, 0:64], T.LVM[:], A.mult, A.add, ["RM", "LVM"], ["LVS"])
+        cp(l3(t, r, 14, 18), T.LVS[:, 15:64:16], ["LVS"], [L3k])
+        if t == 0:
+            ts(l3(t, r, 0, 4), T.TR4[:], 0.0, A.mult, None, None, ["TR4"], [L3k])
+            send(3, t, "L3", LL, 18)
+        else:
+            if t < 4:
+                if k1:
+                    own_v1(k1)
+                own_v2(k1)
+            store_gone(t - 1)
+            for b in range(2):
+                bank = ("pD", "pE")[b]
+                scan(T.TS[:, 512 * b:512 * b + 512], T.RM[:, 0:512], T[bank][:], A.mult, A.max, ["RM", bank], ["TS%d" % b])
+            cp(T.TI[:], T.TS[:, 15:1024:16], ["TS0", "TS1"], ["TI"])
+            ts(T.TB[:], T.TI[:], 2, A.bitwise_and, None, None, ["TI"], ["TB"])
+            cp(T.TF[:], T.TB[:], ["TB"], ["TF"])
+            op("t", [mm(T.pC[:, 48:52], T.JM[:, 128 * m:128 * m + 128], T.TF[:, m:64:16], m == 0, m == 15) for m in M16], ["JM", "TF"], ["pC"])
+            op("t", [mm(T.pM[:, 0:256], T.ID[:], T.MASKJ[:], True, False)] +
+               [mm(T.pM[:, 64 * s:64 * s + 64], T.GJ[:], T.TF[:], False, s == 3) for s in range(4)], ["ID", "MASKJ", "GJ", "TF"], ["pM"])
+            for b in range(2):
+                scan(T.NS[:, 512 * b:512 * b + 512], T.RN[:, 0:512], T["pN%d" % b][:], A.max, A.min, ["RN", "pN%d" % b], ["NS%d" % b])
+            tt(l2(t, r), T.NS[:, 15:1024:16], T.C3[:], A.min, ["NS0", "NS1", "C3"], [L2k])
+            send(2, t, "L2", SL, SL)
+            tt(T.CV[:], T.NONEL[:], T.WW[:], A.subtract, ["NONEL", "WW"], ["CV"])
+            cp(T.EW[:], T.pC[:, 48:52], ["pC"], ["EW"])
+            for s in range(4):
+                ts(T.DC[:, 64 * s:64 * s + 64], T.pM[:, 64 * s:64 * s + 64], T.EW[:, s:s + 1], A.is_equal, 4096.0, A.mult, ["pM", "EW"], ["DC%d" % s])
+            scan(T.DS[:], T.R64[:], T.DC[:], A.mult, A.max, ["R64"] + ["DC%d" % s for s in range(4)], ["DS"])
+            tt(T.EO[:, 0:4], T.DS[:, 63:256:64], T.EW[:], A.add, ["DS", "EW"], ["EO0"])
+            ts(T.EO[:, 4:8], T.EO[:, 0:4], 2559.5, A.is_lt, None, None, ["EO0"], ["EO1"])
+            tt(T.EO[:, 8:12], T.EO[:, 0:4], T.TR4[:], A.subtract, ["EO0", "TR4"], ["EO2"])
+            tt(T.EO[:, 12:16], T.EO[:, 8:12], T.EO[:, 4:8], A.mult, ["EO1", "EO2"], ["EO3"])
+            tt(T.EO[:, 16:20], T.EO[:, 12:16], T.TR4[:], A.add, ["EO3", "TR4"], ["EO4"])
+            ts(l3(t, r, 0, 4), T.EO[:, 16:20], float(lo), A.subtract, None, None, ["EO4"], [L3k])
+            send(3, t, "L3", LL, 18)
+        if t < 4:
+            ts(T.TM[:], T.pC[:, 32:33], 64.0, A.min, None, None, ["pC"], ["TM"])
+            op("t", mm(T.pC[:, 40:41], T.ONES[:], T.TM[:], True, True), ["ONES", "TM"], ["pC"])
+            if t == 0:
+                own_v1(1)
+                own_v2(1)
+            own_s2(k1)
+            ts(T.AI[:], T.pC[:, 40:41], 1.0 / 16.0, A.mult, None, None, ["pC"], ["AI"])
+            ts(T.AJ[:], T.AI[:], 7, A.bitwise_and, None, None, ["AI"], ["AJ"])
+            tt(T.THR[:], T.LIMF[:], T.AJ[:], A.add, ["LIMF", "AJ"], ["THR"])
+            fill(T.CA[:, 0:64], V * 1024 + 512, ["CA"])
+            cp(T.CB[:, 0:64], T.CBI[:], ["CBI"], ["CB"])
+        if t == 0:
+            ts(T.THA[:], T.U3[:], 63.5, A.is_lt, 100.0, A.mult, ["U3"], ["THA"])
+            ts(T.THW[:], T.THA[:], 8.5, A.max, None, None, ["THA"], ["THW"])
+            iota(T.FNB[:], [[0, W]], V, 0, whole("FNB"))
+            fill(T.RN[:], 0.0, ["RN"])
+            fill(T.RN[:, 0:2560:16], 8192.0, ["RN"])
+            ts(T.JM[:], T.BM[:], T.TC[:, 34:35], A.mult, None, None, BMk + ["WJ"], ["JM"])
+            ts(T.GJ[:], T.GG[:], T.TC[:, 34:35], A.mult, None, None, ["GG", "WJ"], ["GJ"])
+            ts(T.GN[:], T.GG[:], T.TC[:, 44:45], A.mult, None, None, ["GG", "WN"], ["GN"])
+            ts(T.GS[:], T.GG[:], 64.0, A.mult, None, None, ["GG"], ["GS"])
+            ts(T.IDB[:], T.ID[:], 4096.0, A.mult, None, None, ["ID"], ["IDB"])
+            cp(T.IDF[:], T.ID[:], ["ID"], ["IDF"])
+            ts(T.MASKJ[:], T.MASKI[:], pm, A.is_ge, 8192.0, A.mult, ["MASKI", "PM"], ["MASKJ"])
+            fill(T.R64[:], 1.0, ["R64"])
+            fill(T.R64[:, 0:256:64], 0.0, ["R64"])
+        else:
+            if t < 4:
+                expand(k1, qe1, 1)
+            if t == 1:
+                act(T.XEB[:], T.FNB[:], whole("FNB") + ["NX"], whole("XEB"), func=F.Identity, scale=0.0, bias=nx)
+            if t >= 2:
+                ts(T.JL[:, lo // 16:160], T.pW[:, 16:16 + n // 16], 2607.5, A.add, None, None, ["pW"], ["JL"])
+            if t == 4:
+                cl = 160 * (15 - r)
+                act(T.AXR[:], xe[:, cl:cl + 160], [("XE" + cur, 15 - r)], ["AXR"], func=F.Abs)
+                ts(T.LIVE[:], T.AXR[:], 0.5, A.is_lt, None, None, ["AXR"], ["LIVE"])
+                tt(T.CV[:], T.CV[:], T.LIVE[:], A.mult, ["CV", "LIVE"], ["CV"])
+            ts(T.CV2[:], T.CV[:], float(V), A.mult, None, None, ["CV"], ["CV2"])
+            col = T.NBN[:, 4 * k + r:V:16]
+            tt(col, col, T.CV2[:], A.max, NB + ["CV2"], NB)
+            keep_sizes(t - 1)
+            store_sizes(t - 1)
+            store_names(t - 1)
+        b0 = lo // 160
+        wx, wf = tab("XE" + cur, b0, 16, "n"), tab("FN" + cur, b0, 16, "n")
+        if t < 4:
+            to = nxt if t >= 2 else cur
+            if t:
+                for q in (3, 2, 1, 0):
+                    cp(xe[:, lo:W].indirect(l3(t, q, 0, 4)), l1(t, q), [("L1", t, q), ("L3", t, q)], wx)
+            for buf, nm, ld in (("L1", "XE", l1), ("L2", "FN", l2)):
+                for q in range(N):
+                    bk = 15 - 4 * t - q
+                    act(T[nm + to][:, 160 * bk:160 * bk + 160], ld(t, q, 0, SL).indirect(l3(t, q, 4, 14)), [(buf, t, q), ("L3", t, q)], [(nm + to, bk)])
+            if t:
+                for q in (3, 2, 1, 0):
+                    cp(fn[:, lo:W].indirect(l3(t, q, 0, 4)), l2(t, q), [("L2", t, q), ("L3", t, q)], wf)
+            if t >= 2:
+                act(T["XE" + to][:, lo:V], xe[:, 0:2576].indirect(T.JL[:, lo // 16:160]), XEk + ["JL"], tab("XE" + to, b0, 16))
+                cp(T["FN" + to][:, lo:V], fn[:, 0:2576].indirect(T.JL[:, lo // 16:160]), FNk + ["JL"], tab("FN" + to, b0, 16))
+                cur, nxt = nxt, cur
+        else:
+            for q in (3, 2, 1, 0):
+                cp(xe[:, lo:W].indirect(l3(t, q, 0, 4)), l1(t, q), [("L1", t, q), ("L3", t, q)], wx)
+            keep_sizes(t)
+            store_names(t)
+            dma("y", "d_yn", [lambda: g.sync.dma_start(T.yn[:], T.NBN[:, 0:V])], NB, ())
+            store_sizes(t)
+            dma("y", "d_yx", [lambda: g.sync.dma_start(T.yx[:], T.XSN[:, 16:2576])], XS, ())
+            xo, xk = T["XE" + nxt], "XE" + nxt
+            act(xo[:, 0:1280], xe[:, 0:2576].indirect(T.JL[:, 0:80]), XEk + ["JL"], tab(xk, 0, 8))
+            cp(xo[:, 1280:V], xe[:, 0:2576].indirect(T.JL[:, 80:160]), XEk + ["JL"], tab(xk, 8, 16))
+            for j, (a, b) in enumerate(((0, 480), (480, 960), (960, 1280), (1280, 1760), (1760, 2240), (2240, 2560))):
+                bank = ("pN0", "pN1", "pM", "pW", "pD", "pE")[j]
+                act(T.SGN[:, a:b], xo[:, a:b], tab(xk, a // 160, b // 160), [("SGN", j)] + (["SGN"] if j == 0 else []), func=F.Sign)
+                op("t", mm(T[bank][:, 0:b - a], T.GN[:], T.SGN[:, a:b], True, True), ["GN", ("SGN", j)], [bank])
+                for p in range(a, b, 160):
+                    c = 15 - p // 160
+                    tt(T.YJ[:, c:V:16], T[bank][:, p - a:p - a + 160], T.NU[:, c:V:16], A.max, [bank, "NU"], [("YJ", c)])
+            dma("y", "d_yj", [lambda i=i: g.sync.dma_start(T.yj[i:i + 1, :], T.YJ[16 * i:16 * i + 1, :]) for i in range(8)], [("YJ", c) for c in M16], ())
+    finish([("lo", nsend[0])])

@@ -4,83 +4,93 @@ from concourse.mybir import AluOpType, ActivationFunctionType
 A = AluOpType
 F = ActivationFunctionType
 V, N, R = 2560, 4, 5
-W = 2640
-NT, XT = 3600, 3616
-EPS = 2.0 ** -10
-SL = 72
-LL = 24
+NAT, DUMP, B0 = 16, 2592, 2688
+TW = B0 + 64 * N * R
+SM, SC = 320, 72
+MAGIC = 1.5 * 2.0 ** 23
+MAGIC128 = 1.5 * 2.0 ** 30
+TINY = 2.0 ** -14
+COVER = ((0, 64), (64, 128), (128, 160))
+SIZES = (((0, 64, "s"),), ((64, 128, "s"),), ((128, 160, "v"),))
+LISTS = ((0, 96, "s"), (96, 160, "v"))
+SIZES0 = ((0, 40, "s"), (40, 80, "v"), (80, 120, "s"), (120, 160, "v"))
 
 SCRATCH = {}
 for _d, _spec in (
-    ("float32", "NBN:3600 NU:3600 LIMF:1 THR:1 FNA:2640 FNB:2640 L1:1440 L2:1440 QF:640 QN16:640 QM:640 PREA:640 SG:640 VN:640 "
-     "QD:160 QPF:160 NE:160 QA:160 QE:2560 QE2:2560 QL:160 OC:160 CODB:160 CODA:160 DEG:160 D1:160 SD:160 U1:10 U2:10 U3:10 "
-     "THA:10 THW:10 CW:10 CW1:10 LV:64 LVM:64 LVS:64 DM64:64 TS:1024 EW:4 EO:24 TR4:4 QG:1024 NS:1024 XSA:288 XSS:288 ZERO:64 "
-     "YJ:2560 MASKI:256 LANE:160 PREB:160 I16:10 TC:64 IDF:128"),
-    ("bfloat16", "XSN:3616 XEA:2640 XEB:2640 SGN:2560 EQ:2560 UNC:2560 XEG:2560 MXS:2560 XVG:2560 NONEL:160 WW:160 CV:160 CV2:160 "
-     "AXR:160 LIVE:160 MP:160 OK:160 HX:12 XSC:12 ONES:128 TM:1 AXC:1024 SGC:1024 TF:64 DC:256 DS:256 MM:1024 RM:2560 RN:2560 "
-     "R64:256 BIAS:512 MASKJ:256 G1:128 GG:128 TRI:128 ID:128 IDB:128 GS:128 GJ:128 GN:128 BM:2048 JM:2048 DM:2048"),
-    ("int32", "LIMI:1 AI:1 AJ:1 QI:160 QI2:160 QI3:160 CA:320 CB:320 CBI:64 C1:64 C2:64 C3:64 C4:64 TI:64 TB:64 EXPI:160 TCI:16"),
-    ("uint16", "JL:160 L3:480 QPU:640 QLU:160 SLU:10 QCU:64 EXPL:160"),
+    ("float32", "NB:%d KT:%d YN:2560 YJ:2560 QEA:2560 QEB:2560 QF:640 QN:640 QM:704 QL4:176 QX:160 XL4:160 CV:160 QM2:160 OC:176 D1:176 "
+     "LANE:176 ACC:4 LV:64 OCC:64 KG:1024 QG:1024 TS:1024 NS:1024 RK1:64 EWS:64 DC:160 DS:160 ST:72 TR:4 CC:80 LO4:80 UU:160 OL4:160 "
+     "LIMF:1 THR:1 TC:48 IDF:128 NE:160 QA:160 QB:160 SCR:160" % (TW, TW)),
+    ("bfloat16", "XB:%d MB:%d YX:2560 EQ:2560 XG:2560 MXS:2560 GM:2560 RM:2560 RK:1024 RN:1024 RD:160 MM:1024 JM:2048 ELB:160 OK:160 "
+     "HH:160 RR:160 YY:160 ZERO:160 DEAD:160 LIVE:160 TF:64 TM:1 ONES:128 O16:128 ID:128 G1:128 GG:128 GW:128 IDN:128 IDX:128 IDB:128 GJ:128 "
+     "W1:128 W2:128 CST:256 MSK:224 MK1:224" % (TW, SM * N * R)),
+    ("int32", "LIMI:1 AI:1 AJ:1 QI:160 QI2:160 TCI:2 EXPI:64"),
+    ("uint16", "CU:%d QL:160 XL:160 QP:160 LN:4 QC:64 EXPL:64 JL:240 LO:80 OL:160" % (SC * N * R)),
 ):
     for _e in _spec.split():
         SCRATCH[_e.split(":")[0]] = ("sbuf", [128, int(_e.split(":")[1])], _d)
-for _e in "pD pE pC pM pW pN0 pN1".split():
+for _e in "pZ pD pC pL pN0 pN1 pM pK".split():
     SCRATCH[_e] = ("psum", [128, 512], "float32")
 SEMAPHORES = ["v", "s", "t", "p", "lo", "d_nb0", "d_nb1", "d_xs", "d_lim", "d_yn", "d_yx", "d_yj"] + [
-    "a%d_%d_%d" % (k, t, q) for k in (1, 2, 3) for t in range(R) for q in range(N)]
+    "a%d_%d_%d" % (k, t, q) for k in (1, 2) for t in range(R) for q in range(N)]
 
 
 def queues(g, T):
     eng = {"v": g.vector, "s": g.scalar, "t": g.tensor, "p": g, "y": g.sync}
     cnt = {"v": 0, "s": 0, "t": 0, "p": 0}
     know = {q: {} for q in eng}
-    lastw, readers, dmas = {}, {}, {}
+    seen, total = {}, {}
 
-    def wait(q, tok):
-        sem, val, clock, _ = tok
-        if know[q].get(sem, 0) < val:
-            eng[q].wait_ge(T.sem[sem], val)
-            know[q][sem] = val
-        for k, n in clock.items():
-            if know[q].get(k, 0) < n:
-                know[q][k] = n
+    def meet(x, y):
+        return x[1] < y[2] and y[1] < x[2] and not (x[3] == y[3] and x[3] > 1 and (x[1] - y[1]) % x[3])
 
     def before(q, R_, W_):
-        toks = [lastw[k] for k in R_ if k in lastw]
-        for k in W_:
-            toks += [x for x in list(readers.get(k, {}).values()) + ([lastw[k]] if k in lastw else [])
-                     if not (x[3] == q and q == "t")]
-        for tok in sorted(toks, key=lambda x: -x[1]):
-            wait(q, tok)
+        need = []
+        for pcs, w in ((R_, False), (W_, True)):
+            for x in pcs:
+                bank = x[0][0] == "p"
+                for y, w2, tok in seen.get(x[0], []):
+                    if tok[3] == q == "t":
+                        continue
+                    if (bank and tok[3] != q) or ((w or w2) and meet(x, y)):
+                        need.append(tok)
+        for sem, val, clock, _ in sorted(need, key=lambda z: -z[1]):
+            if know[q].get(sem, 0) < val:
+                eng[q].wait_ge(T.sem[sem], val)
+                know[q][sem] = val
+            for k, n in clock.items():
+                if know[q].get(k, 0) < n:
+                    know[q][k] = n
 
     def after(tok, R_, W_):
-        for k in W_:
-            lastw[k] = tok
-            readers[k] = {}
-        for k in R_:
-            readers.setdefault(k, {})[tok[0]] = tok
+        for pcs, w in ((R_, False), (W_, True)):
+            for x in pcs:
+                old = seen.get(x[0], [])
+                if w and x[3] == 1:
+                    old = [e for e in old if not (x[1] <= e[0][1] and e[0][2] <= x[2])]
+                old = [e for e in old if not (e[0] == x and e[1] == w and e[2][0] == tok[0])]
+                seen[x[0]] = old + [(x, w, tok)]
 
-    def op(q, fns, R_=(), W_=()):
+    def op(q, fns, R_, W_):
         before(q, R_, W_)
-        for f in (fns if isinstance(fns, list) else [fns]):
+        for f in fns:
             ins = f()
         cnt[q] += 1
         ins.then_inc(T.sem[q], 1)
         after((q, cnt[q], dict(know[q]), q), R_, W_)
 
-    def dma(q, sem, fns, R_=(), W_=()):
+    def dma(q, sem, fns, R_, W_):
         before(q, R_, W_)
         for f in fns:
-            dmas[sem] = dmas.get(sem, 0) + 16
+            total[sem] = total.get(sem, 0) + 16
             f().then_inc(T.sem[sem], 16)
-        after((sem, dmas[sem], dict(know[q]), "dma"), R_, W_)
+        after((sem, total[sem], dict(know[q]), "dma"), R_, W_)
 
     def arrive(sem, n, W_):
-        dmas[sem] = n
+        total[sem] = n
         after((sem, n, {}, "far"), (), W_)
 
     def finish(extra):
-        for sem, n in list(cnt.items()) + list(dmas.items()) + extra:
+        for sem, n in list(cnt.items()) + list(total.items()) + extra:
             if n and know["y"].get(sem, 0) < n:
                 g.sync.wait_ge(T.sem[sem], n)
 
@@ -95,159 +105,187 @@ def rank_program(g, core, T, topo):
     op, dma, arrive, finish, before = queues(g, T)
     others = [d for d in T.cores if d != core]
 
-    def cp(out, in_, R_, W_):
-        op("v", lambda: vec.tensor_copy(out=out, in_=in_), R_, W_)
+    def b(name, c0=0, c1=None, st=1):
+        c1 = SCRATCH[name][1][1] if c1 is None else c1
+        return (T[name][:, c0:c1:st], [(name, c0, c1 - (c1 - c0 - 1) % st, st)])
 
-    def tt(out, a, b, o, R_, W_):
-        op("v", lambda: vec.tensor_tensor(out=out, in0=a, in1=b, op=o), R_, W_)
+    def by(win, off):
+        return (win[0].indirect(off[0]), win[1], off[1])
 
-    def ts(out, a, s1, o1, s2, o2, R_, W_):
+    def call(q, f, out, ins, more=()):
+        aps = [x[0] if isinstance(x, tuple) else x for x in ins]
+        R_ = [pc for x in ins if isinstance(x, tuple) for part in x[1:] for pc in part] + (out[2] if len(out) > 2 else [])
+        op(q, [lambda: f(out[0], *aps)], R_, out[1] + [pc for x in more for pc in x[1]])
+
+    def cp(out, x):
+        call("v", lambda o, i: vec.tensor_copy(out=o, in_=i), out, [x])
+
+    def tt(out, x, y, o1):
+        call("v", lambda o, i, j: vec.tensor_tensor(out=o, in0=i, in1=j, op=o1), out, [x, y])
+
+    def ts(out, x, s1, o1, s2=None, o2=None):
         if o2 is None:
-            op("v", lambda: vec.tensor_scalar(out=out, in0=a, scalar1=s1, scalar2=None, op0=o1), R_, W_)
+            call("v", lambda o, i, u: vec.tensor_scalar(out=o, in0=i, scalar1=u, scalar2=None, op0=o1), out, [x, s1])
         else:
-            op("v", lambda: vec.tensor_scalar(out=out, in0=a, scalar1=s1, scalar2=s2, op0=o1, op1=o2), R_, W_)
+            call("v", lambda o, i, u, w: vec.tensor_scalar(out=o, in0=i, scalar1=u, scalar2=w, op0=o1, op1=o2), out, [x, s1, s2])
 
-    def scan(out, d0, d1, o0, o1, R_, W_):
-        op("v", lambda: vec.tensor_tensor_scan(out=out, data0=d0, data1=d1, initial=0.0, op0=o0, op1=o1), R_, W_)
+    def scan(out, d0, d1, o0, o1, first=0.0):
+        call("v", lambda o, i, j: vec.tensor_tensor_scan(out=o, data0=i, data1=j, initial=first, op0=o0, op1=o1), out, [d0, d1])
 
-    def fill(ap, x, W_):
-        op("v", lambda: vec.memset(ap, x), (), W_)
+    def fill(out, x):
+        call("v", lambda o: vec.memset(o, x), out, [])
 
-    def act(out, in_, R_, W_, func=F.Copy, **kw):
-        op("s", lambda: sca.activation(out, in_, func, **kw), R_, W_)
+    def act(out, x, func=F.Copy, bias=0.0, scale=1.0, total=None):
+        if total is None:
+            call("s", lambda o, i, u, w: sca.activation(o, i, func, bias=u, scale=w), out, [x, bias, scale])
+        else:
+            call("s", lambda o, i, u, w: sca.activation(o, i, func, bias=u, scale=w, accum_out=total[0]), out, [x, bias, scale], [total])
 
-    def iota(out, pattern, base, cm, W_):
-        op("p", lambda: g.iota(out, pattern, base, cm, allow_small_or_imprecise_dtypes=True), (), W_)
+    def move(q, out, x):
+        (act if q == "s" else cp)(out, x)
 
-    def mm(out, l, rr, st, sp):
-        return lambda: ten.matmul(out, l, rr, st, sp)
+    def iota(out, pattern, base, cm):
+        call("p", lambda o: g.iota(o, pattern, base, cm, allow_small_or_imprecise_dtypes=True), out, [])
 
-    def tab(name, a, b, *more):
-        return [(name, x) for x in range(a, b)] + [(name, x) for x in more]
+    def select(out, x, pattern, cmp_, other, base, cm):
+        call("p", lambda o, i: g.affine_select(o, i, pattern, cmp_, other, base, cm), out, [x])
 
-    def whole(name):
-        return tab(name, 0, 16, "n")
-    M16 = range(16)
-    NB, XS = ["NB0", "NB1"], ["XS", "XS0"]
-    BMk, DMk = [("BM", m) for m in M16], [("DM", m) for m in M16]
+    def pe(out, terms, start=True, stop=True):
+        fns = [lambda j=j, l=l, x=x: ten.matmul(out[0], l[0], x[0], start and j == 0, stop and j == len(terms) - 1) for j, (l, x) in enumerate(terms)]
+        op("t", fns, [pc for l, x in terms for pc in l[1] + x[1]], out[1])
 
-    dma("y", "d_nb0", [lambda: g.sync.dma_start(T.NBN[:, 0:1280], T.nb[:, 0:1280])], (), ["NB0"])
-    dma("s", "d_nb1", [lambda: g.scalar.dma_start(T.NBN[:, 1280:2560], T.nb[:, 1280:2560])], (), ["NB1"])
-    dma("y", "d_xs", [lambda: g.sync.dma_start(T.XSN[:, 16:2576], T.xs[:])], (), ["XS"])
-    dma("s", "d_lim", [lambda: g.scalar.dma_start(T.LIMI[:], T.lim[:])], (), ["LIMI"])
+    def lists(out, name, c0, c1):
+        pe(out, [(b("JM", 128 * m, 128 * m + 128), b(name, c0 + m, c1, 16)) for m in range(16)])
 
-    iota(T.TCI[:, 0:1], [[1, 1]], 0, 1, ["TCI"])
-    iota(T.LANE[:], [[1, 160]], 0, 0, ["LANE"])
-    fill(T.ONES[:], 1.0, ["ONES"])
-    ones = T.ONES[:]
-    op("p", lambda: g.affine_select(T.ID[:], ones, [[-1, 128]], A.is_equal, 0.0, 0, 1), ["ONES"], ["ID"])
-    op("p", lambda: g.affine_select(T.G1[:], ones, [[-16, 8], [0, 16]], A.is_ge, 0.0, 0, 1), ["ONES"], ["G1"])
-    op("p", lambda: g.affine_select(T.GG[:], T.G1[:], [[16, 8], [0, 16]], A.is_ge, 0.0, 15, -1), ["G1"], ["GG"])
-    iota(T.I16[:], [[16, 10]], 0, 0, ["I16"])
-    op("p", lambda: g.affine_select(T.TRI[:], T.GG[:], [[1, 128]], A.is_ge, 0.0, 0, -1), ["GG"], ["TRI"])
-    iota(T.EXPI[:], [[1, 160]], 0, 0, ["EXPI"])
-    iota(T.CBI[:], [[1, 64]], 2560 * 256 + 161, 0, ["CBI"])
-    iota(T.TC[:, 40:44], [[16, 4]], 2576, 0, ["T40"])
-    iota(T.LVM[:], [[0, 4], [1, 16]], 0, 0, ["LVM"])
-    iota(T.MASKI[:], [[-16, 4], [1, 64]], 0, 0, ["MASKI"])
-    iota(T.BIAS[:], [[0, 32], [-4, 16]], 61, 0, ["BIAS"])
-    iota(T.FNA[:], [[0, W]], V, 0, whole("FNA"))
-    iota(T.NU[:, 0:V], [[1, V]], 0, 0, ["NU"])
-    fill(T.XSN[:, 0:16], 0.0, ["XS0"])
-    fill(T.XSN[:, 2576:2592], 0.0, ["XS0"])
-    fill(T.BM[:], 0.0, BMk)
-    fill(T.DM[:], 0.0, DMk)
-    for m in M16:
-        act(T.BM[:, 128 * m + m:128 * m + 128:16], T.GG[:, m:128:16], ["GG"], [("BM", m)])
-    for m in M16:
-        act(T.DM[:, 128 * m + m:128 * m + 128:16], T.ID[:, m:128:16], ["ID"], [("DM", m)])
-    ts(T.TCI[:, 1:2], T.TCI[:, 0:1], 15, A.bitwise_and, None, None, ["TCI"], ["TCI1"])
-    for b in range(4):
-        ts(T.TCI[:, 4 + b:5 + b], T.TCI[:, 1:2], b, A.logical_shift_right, 1, A.bitwise_and, ["TCI1"], ["TCB%d" % b])
-    cp(T.TC[:, 0:1], T.TCI[:, 1:2], ["TCI1"], ["PM"])
-    for b in range(4):
-        up = float(2 ** (2 ** b))
-        ts(T.TC[:, 12 + b:13 + b], T.TCI[:, 4 + b:5 + b], up - 1.0, A.mult, 1.0, A.add, ["TCB%d" % b], ["UP%d" % b])
-        ts(T.TC[:, 16 + b:17 + b], T.TCI[:, 4 + b:5 + b], 1.0 / up - 1.0, A.mult, 1.0, A.add, ["TCB%d" % b], ["DN%d" % b])
-    for nm, c0, d in (("UP", 12, 1), ("DN", 16, 2)):
-        tt(T.TC[:, 20 + d:21 + d], T.TC[:, c0:c0 + 1], T.TC[:, c0 + 1:c0 + 2], A.mult, [nm + "0", nm + "1"], [nm + "a"])
-        tt(T.TC[:, 24 + d:25 + d], T.TC[:, c0 + 2:c0 + 3], T.TC[:, c0 + 3:c0 + 4], A.mult, [nm + "2", nm + "3"], [nm + "b"])
-        tt(T.TC[:, d:d + 1], T.TC[:, 20 + d:21 + d], T.TC[:, 24 + d:25 + d], A.mult, [nm + "a", nm + "b"], [nm])
-    pm, up, dn = T.TC[:, 0:1], T.TC[:, 1:2], T.TC[:, 2:3]
-    cp(T.EXPL[:], T.EXPI[:], ["EXPI"], ["EXPL"])
-    ts(T.PREB[:], T.LANE[:], float(2560 * 256), A.add, None, None, ["LANE"], ["PREB"])
+    def blk(name, t, q, n=1):
+        return b(name, B0 + 64 * (4 * t + q), B0 + 64 * (4 * t + q + n))
 
-    def signs(k):
-        c = 4 * k + r
-        s = slice(160 * k, 160 * k + 160)
-        ts(T.QD[:], T.LANE[:], float(256 * (15 - c)), A.add, None, None, ["LANE"], ["QD"])
-        ts(T.VN[:, s], T.LANE[:], 16.0, A.mult, float(c), A.add, ["LANE"], ["VN%d" % k])
-        ts(T.QPF[:], T.QD[:], dn, A.mult, -0.495, A.add, ["QD", "DN"], ["QPF"])
-        cp(T.QI[:], T.QPF[:], ["QPF"], ["QI"])
-        ts(T.QI2[:], T.QI[:], 1, A.bitwise_and, None, None, ["QI"], ["QI2"])
-        ts(T.SG[:, s], T.QI2[:], 2.0, A.mult, -1.0, A.add, ["QI2"], ["SG%d" % k])
-    for k in range(4):
-        signs(k)
-    ts(T.TC[:, 8:9], pm, 7.5, A.is_lt, 0.5, A.mult, ["PM"], ["W0"])
-    ts(T.TC[:, 9:10], pm, 11.5, A.is_lt, 0.5, A.mult, ["PM"], ["W1"])
-    ts(T.TC[:, 10:11], pm, 12.0, A.is_equal, None, None, ["PM"], ["W2"])
-    ts(T.TC[:, 11:12], pm, 13.0, A.is_equal, -2040.0, A.mult, ["PM"], ["W3"])
-    tt(T.TC[:, 28:29], T.TC[:, 8:9], up, A.mult, ["W0", "UP"], ["W4"])
-    tt(T.TC[:, 29:30], T.TC[:, 9:10], up, A.mult, ["W1", "UP"], ["W5"])
-    ts(T.TC[:, 45:46], T.TC[:, 10:11], 2.0 * EPS, A.mult, -EPS, A.add, ["W2"], ["NX"])
-    ts(T.TC[:, 32:33], T.TC[:, 10:11], 1280.0, A.mult, None, None, ["W2"], ["W8"])
-    tt(T.TC[:, 30:31], T.TC[:, 29:30], T.TC[:, 28:29], A.subtract, ["W4", "W5"], ["W6"])
-    ts(T.TC[:, 37:38], T.TC[:, 10:11], -7.5, A.mult, None, None, ["W2"], ["WC"])
-    ts(T.TC[:, 35:36], T.TC[:, 28:29], 16.0, A.mult, None, None, ["W4"], ["WA"])
-    ts(T.TC[:, 31:32], T.TC[:, 30:31], 160.0 / 256.0, A.mult, None, None, ["W6"], ["W7"])
-    ts(T.TC[:, 36:37], T.TC[:, 30:31], -1.0 / 256.0, A.mult, None, None, ["W6"], ["WB"])
-    tt(T.TC[:, 39:40], T.TC[:, 37:38], T.TC[:, 11:12], A.add, ["WC", "W3"], ["WE"])
-    tt(T.TC[:, 33:34], T.TC[:, 31:32], T.TC[:, 28:29], A.add, ["W7", "W4"], ["W9"])
-    tt(T.TC[:, 38:39], T.TC[:, 35:36], T.TC[:, 36:37], A.add, ["WA", "WB"], ["WD"])
-    tt(T.TC[:, 34:35], T.TC[:, 33:34], T.TC[:, 32:33], A.add, ["W8", "W9"], ["WJ"])
-    tt(T.TC[:, 44:45], T.TC[:, 38:39], T.TC[:, 39:40], A.add, ["WD", "WE"], ["WN"])
-    nx = T.TC[:, 45:46]
-    ts(T.CW1[:], T.I16[:], pm, A.add, 160.0, A.add, ["I16", "PM"], ["CW1"])
-    ts(T.CW[:], T.CW1[:], 1.0, A.add, None, None, ["CW1"], ["CW"])
-    fill(T.HX[:], 0.0, ["HX"])
-    fill(T.RM[:], 1.0, ["RM"])
-    fill(T.RM[:, 0:2560:16], 0.0, ["RM"])
-    fill(T.CA[:, 0:64], V * 1024 + 512, ["CA"])
-    cp(T.CB[:, 0:64], T.CBI[:], ["CBI"], ["CB"])
-    cp(T.LIMF[:], T.LIMI[:], ["LIMI"], ["LIMF"])
-    cp(T.THR[:], T.LIMF[:], ["LIMF"], ["THR"])
+    def mb(t, q, c0, c1):
+        return b("MB", SM * (4 * t + q) + c0, SM * (4 * t + q) + c1)
 
-    made = []
+    def cu(t, q, c0, c1):
+        return b("CU", SC * (4 * t + q) + c0, SC * (4 * t + q) + c1)
 
-    def own_s1(k):
-        s = slice(160 * k, 160 * k + 160)
-        if k not in made:
-            act(T.QF[:, s], T.NBN[:, 4 * k + r:V:16], NB, ["QF%d" % k])
-            act(T.QA[:], T.QF[:, s], ["QF%d" % k], ["QA"], scale=256.0, bias=-655360.0)
-        made.append(k)
+    def col(j):
+        return b("TC", j, j + 1)
 
-    def own_v1(k):
-        s = slice(160 * k, 160 * k + 160)
-        tt(T.NE[:], T.QF[:, s], T.VN[:, s], A.not_equal, ["QF%d" % k, "VN%d" % k], ["NE"])
-        tt(T.QM[:, s], T.QA[:], T.NE[:], A.mult, ["QA", "NE"], ["QM%d" % k])
+    dma("y", "d_xs", [lambda: g.sync.dma_start(T.XB[:, NAT:NAT + V], T.xs[:])], (), b("XB", NAT, NAT + V)[1])
+    dma("s", "d_nb0", [lambda: g.scalar.dma_start(T.NB[:, NAT:NAT + 1280], T.nb[:, 0:1280])], (), b("NB", NAT, NAT + 1280)[1])
+    dma("y", "d_nb1", [lambda: g.sync.dma_start(T.NB[:, NAT + 1280:NAT + V], T.nb[:, 1280:V])], (), b("NB", NAT + 1280, NAT + V)[1])
+    dma("s", "d_lim", [lambda: g.scalar.dma_start(T.LIMI[:], T.lim[:])], (), b("LIMI")[1])
 
-    def own_v2(k):
-        s = slice(160 * k, 160 * k + 160)
-        cp(T.QI[:], T.QF[:, s], ["QF%d" % k], ["QI"])
-        ts(T.QI2[:], T.QI[:], 15, A.bitwise_and, None, None, ["QI"], ["QI2"])
-        ts(T.QI3[:], T.QI[:], 4, A.logical_shift_right, None, None, ["QI"], ["QI3"])
-        ts(T.QD[:], T.QI2[:], -160.0, A.mult, 2400.0, A.add, ["QI2"], ["QD"])
-        tt(T.QPF[:], T.QD[:], T.QI3[:], A.add, ["QD", "QI3"], ["QPF"])
-        cp(T.QPU[:, s], T.QPF[:], ["QPF"], ["QPU%d" % k])
+    iota(b("TCI", 0, 1), [[1, 1]], 0, 1)
+    fill(b("ONES"), 1.0)
+    select(b("ID"), b("ONES"), [[-1, 128]], A.is_equal, 0.0, 0, 1)
+    select(b("G1"), b("ONES"), [[-16, 8], [0, 16]], A.is_ge, 0.0, 0, 1)
+    select(b("GG"), b("G1"), [[16, 8], [0, 16]], A.is_ge, 0.0, 15, -1)
+    iota(b("LANE"), [[1, 176]], 0, 0)
+    iota(b("TR"), [[16, 4]], 0, 0)
+    iota(b("EXPI"), [[1, 64]], 0, 0)
+    iota(b("CC"), [[1, 4], [256, 20]], NAT, 0)
+    iota(b("CST"), [[0, 4], [1, 64]], -64, 0)
+    iota(b("SCR", 0, 160), [[16, 160]], NAT, 0)
+    fill(b("XB", 0, NAT), 0.0)
+    fill(b("XB", NAT + V, B0), 0.0)
+    fill(b("NB", 0, NAT), float(V))
+    fill(b("NB", NAT + V, B0), float(V))
+    fill(b("JM"), 0.0)
+    fill(b("ZERO"), 0.0)
+    fill(b("D1", 160, 176), MAGIC)
+    fill(b("OC", 160, 176), float(V))
+    fill(b("QM", 160, 176), float(V))
+    fill(b("QL4", 160, 176), 0.0)
+    for t in range(R):
+        fill(mb(t, r, 160, 176), 0.0)
+        fill(mb(t, r, 304, 320), 0.0)
+    ts(b("TCI", 1, 2), b("TCI", 0, 1), 15, A.bitwise_and)
+    pm = col(0)
+    cp(pm, b("TCI", 1, 2))
+    e0, e1, e4, e5, e6 = col(1), col(2), col(3), col(4), col(5)
+    for c_, j in ((e0, 0), (e1, 1), (e4, 4), (e5, 5), (e6, 6)):
+        ts(c_, pm, float(j), A.is_equal)
+    ts(b("TR"), b("TR"), pm, A.add)
+    ts(b("TC", 8, 12), b("TR"), -64.5, A.add)
+    ts(col(6), e0, -63.0, A.mult, -1.0, A.add)
+    for t in range(R):
+        ts(col(12 + t), e1, -float(B0 // 64 + 1 + 4 * t + r), A.mult, e0, A.add)
+    ts(col(7), e1, 64.0, A.mult, e0, A.add)
+    ts(b("GW"), b("GG"), col(7), A.mult)
+    for m in range(16):
+        act(b("JM", 128 * m + m, 128 * m + 128, 16), b("GW", m, 128, 16))
+    cp(b("LIMF"), b("LIMI"))
+    ts(b("THR"), b("LIMF"), 0.3, A.add)
+    ts(b("LIMF"), b("LIMF"), 0.3, A.add)
 
-    def own_s2(k):
-        s = slice(160 * k, 160 * k + 160)
-        act(T.QN16[:, s], T.QF[:, s], ["QF%d" % k], ["QN%d" % k], bias=16.0)
-        act(T.PREA[:, s], T.QPF[:], ["QPF"], ["PREA%d" % k], scale=1024.0, bias=512.0)
+    def later_constants():
+        cp(b("EXPL"), b("EXPI"))
+        ts(col(17), e5, 64.0, A.mult, e4, A.add)
+        ts(b("GJ"), b("GG"), col(17), A.mult)
+        fill(b("W1"), 0.0)
+        for j in (4, 5):
+            ts(b("W1", j, 128, 16), b("GG", j, 128, 16), 2048.0, A.mult)
+        ts(b("W2"), b("ID"), e6, A.mult, 16.0, A.mult)
+        ts(b("IDN"), b("ID"), -8192.0, A.mult)
+        ts(b("IDX"), b("ID"), -1.0 / TINY, A.mult)
+        ts(b("IDB"), b("ID"), 4096.0, A.mult)
+        ts(b("O16"), b("ONES"), 1.0 / 16.0, A.mult)
+        cp(b("IDF"), b("ID"))
+        tt(col(18), e0, e4, A.add)
+        ts(col(19), e4, 32.0, A.mult)
+        tt(col(20), e1, e5, A.add)
+        tt(col(21), col(20), e6, A.add)
+        for q in range(N):
+            ts(col(22 + q), col(21), float(q), A.mult, col(19), A.add)
+            ts(b("CST", 64 * q, 64 * q + 64), b("CST", 64 * q, 64 * q + 64), col(18), A.mult, col(22 + q), A.add)
+        for t in range(R):
+            ts(col(26 + t), e6, float(4 * t % 16), A.mult)
+            ts(col(31 + t), col(20), float(B0 // 64 + 1 + 4 * t), A.mult, col(26 + t), A.add)
+        ts(col(36), pm, 16.0, A.mult)
+        ts(b("CC"), b("CC"), col(36), A.add)
+        ts(b("UU"), b("SCR"), pm, A.add)
+        tt(col(37), e4, e5, A.add)
+        ts(b("KT", 0, NAT), b("ZERO", 0, NAT), col(37), A.add, -4096.0, A.mult)
 
-    def expand(k, name, h):
-        act(T[name][:, 1280 * h:1280 * h + 1280], T.QF[:, 160 * k:160 * k + 160].indirect(T.EXPL[:, 80 * h:80 * h + 80]),
-            ["QF%d" % k, "EXPL"], [name + str(h)])
+    def masks():
+        iota(b("MK1", 0, 64), [[0, 4], [1, 16]], 0, 0)
+        for s in range(4):
+            iota(b("MK1", 64 + 8 * s * (s + 1), 64 + 8 * (s + 1) * (s + 2)), [[1, 16 * s + 16]], -16 * s, 0)
+        ts(b("MSK", 0, 64), b("MK1", 0, 64), pm, A.not_equal, -8192.0, A.mult)
+        ts(b("MSK", 64, 224), b("MK1", 64, 224), pm, A.is_ge, 8192.0, A.mult)
+        ts(b("MSK"), b("MSK"), -float(DUMP + 32), A.add)
+        for name, n, x, y in (("RM", V, 1.0, 0.0), ("RK", 1024, 128.0, -2.0 ** 24), ("RN", 1024, 0.0, 8192.0)):
+            fill(b(name), x)
+            fill(b(name, 0, n, 16), y)
+        fill(b("RD"), 0.0)
+        for s in range(4):
+            fill(b("RD", 8 * s * (s + 1), 8 * s * (s + 1) + 1), 8192.0)
+
+    def qf(k, name="QF", a=0, e=160):
+        w = 176 if name == "QM" else 160
+        return b(name, w * k + a, w * k + e)
+
+    def names(k):
+        act(qf(k), b("NB", NAT + 4 * k + r, NAT + V, 16))
+        act(qf(k, "QN"), qf(k), bias=float(NAT))
+
+    def own(k):
+        ts(b("QA"), b("LANE", 0, 160), 16.0, A.mult, float(4 * k + r), A.add)
+        tt(b("NE"), qf(k), b("QA"), A.is_equal)
+        ts(b("QB"), b("NE"), float(V), A.mult)
+        tt(qf(k, "QM"), qf(k), b("QB"), A.max)
+
+    def places(t):
+        k = t % 4
+        cp(b("QI"), qf(k))
+        ts(b("QI2"), b("QI"), 15, A.bitwise_and)
+        ts(b("QA"), qf(k), 1.0 / 16.0, A.mult)
+        ts(b("QB"), b("QI2"), SM - 1.0 / 16.0, A.mult)
+        tt(b("NE"), b("QA"), b("QB"), A.add)
+        ts(b("QP"), b("NE"), float(SM * (4 * t - 1) + 160), A.min)
+
+    def expand(t, js):
+        for j in js:
+            select(b("QEB" if t % 2 else "QEA", j, V, 16), qf(t % 4), [[0, 160]], A.is_ge, 0.0, 0, 0)
 
     mask = topo.mask(core, others[0])
     for d in others:
@@ -256,271 +294,219 @@ def rank_program(g, core, T, topo):
     ids = [DstId(rid=topo.addr(d)[0], pnc=topo.addr(d)[1]) for d in others]
     nsend = [0]
 
-    def send(kind, t, buf, w, n):
-        ap = T[buf][:, (4 * t + r) * w:(4 * t + r) * w + n]
-        before("p", [(buf, t, r)], ())
+    def send(kind, t, x):
+        before("p", x[1], ())
         g.remote_dma_fused([RemoteDMATransfer(dst_ids=ids, dma_engine_mask=mask, remote_sem=T.sem["a%d_%d_%d" % (kind, t, r)],
-                                              srcs=[ap], dsts=[ap for d in others])], local_sem=T.sem["lo"])
+                                              srcs=[x[0]], dsts=[x[0] for d in others])], local_sem=T.sem["lo"])
         nsend[0] += neng
     for t in range(R):
         for q in range(N):
             if q != r:
-                for kind, buf in ((1, "L1"), (2, "L2"), (3, "L3")):
-                    arrive("a%d_%d_%d" % (kind, t, q), neng, [(buf, t, q)])
+                arrive("a1_%d_%d" % (t, q), neng, mb(t, q, 0, SM)[1])
+                arrive("a2_%d_%d" % (t, q), neng, cu(t, q, 0, 68)[1])
 
-    def l1(t, q, a=0, b=64):
-        return T.L1[:, (4 * t + q) * SL + a:(4 * t + q) * SL + b]
+    def claims(name, t, q, src):
+        cp(by(b(name, DUMP, B0 + 256 * t), cu(t, q, 64, 68)), src)
 
-    def l2(t, q, a=0, b=64):
-        return T.L2[:, (4 * t + q) * SL + a:(4 * t + q) * SL + b]
-
-    def l3(t, q, a, b):
-        return T.L3[:, (4 * t + q) * LL + a:(4 * t + q) * LL + b]
-
-    def keep_sizes(t):
-        act(T.XSA[:], T.L1[:, 4 * t * SL:4 * (t + 1) * SL], [("L1", t, q) for q in range(N)], ["XSA"], func=F.Abs)
-        act(T.XSS[:], T.XSA[:], ["XSA"], ["XSS"], bias=-1.0)
-
-    def store_sizes(t):
+    def keys(t):
+        pe(b("pK", 0, 256), [(b("ID"), b("CST"))], True, False)
         for q in range(N):
-            cp(T.XSN[:, 16:XT].indirect(l3(t, q, 14, 18)), T.XSS[:, SL * q:SL * q + 64], ["XSS", ("L3", t, q)], XS)
+            pe(b("pK", 64 * q, 64 * q + 64), [(b("W1"), mb(t, q, 176, 240)), (b("W2"), mb(t, q, 240, 304))], False, q == N - 1)
+        act(blk("KT", t, 0, 4), b("pK", 0, 256), F.Identity, bias=col(31 + t))
 
-    def store_names(t):
+    def outputs(out, table, t):
         for q in range(N):
-            cp(T.NBN[:, 0:NT].indirect(l3(t, q, 14, 18)), l2(t, q), [("L2", t, q), ("L3", t, q)], NB)
+            c = (4 * t + q) % 16
+            act(b(out, c, V, 16), by(b(table, 0, B0 + 256 * (t + 1)), b("LO", 20 * q, 20 * q + 10)))
+        if t == 0:
+            for q in range(N):
+                act(b(table, NAT + q, NAT + V, 16), b(out, q, V, 16))
 
-    def store_gone(t):
-        for q in range(N):
-            cp(T.NU[:, 0:NT].indirect(l3(t, q, 14, 18)), T.ZERO[:], ["ZERO", ("L3", t, q)], ["NU"])
+    ORDER = [r] + [q for q in (3, 2, 1, 0) if q != r]
+    names(0)
+    ts(b("XL", 0, 80), b("NB", NAT + r, NAT + 1280, 16), float(NAT), A.add)
+    names(1)
+    expand(1, range(8))
+    ts(b("XL", 80, 160), b("NB", NAT + 1280 + r, NAT + V, 16), float(NAT), A.add)
 
-    PARTS = ((0, 48, "s"), (48, 96, "s"), (96, 160, "v"))
-    ts(T.QLU[:], T.NBN[:, r:V:16], 16.0, A.add, None, None, NB, ["QLU"])
-
-    cur, nxt = "A", "B"
     for t in range(R):
         k = t % 4
-        k1 = (t + 1) % 4
-        ks = slice(160 * k, 160 * k + 160)
-        lo = 640 * (4 - t)
-        n = V - lo
-        fn, xe = T["FN" + cur], T["XE" + cur]
-        qe, qe1 = ("QE", "QE2") if t % 2 else ("QE2", "QE")
-        FNk, XEk = whole("FN" + cur), whole("XE" + cur)
-        if t:
-            for h in range(2):
-                s, l = slice(1280 * h, 1280 * h + 1280), T.QPU[:, 160 * k + 80 * h:160 * k + 80 * h + 80]
-                act(T.XEG[:, s], xe[:, 0:2576].indirect(l), XEk + ["QPU%d" % k], ["XEG%d" % h], func=F.Abs)
-                tt(T.EQ[:, s], fn[:, 0:2576].indirect(l), T[qe][:, s], A.not_equal, FNk + ["QPU%d" % k, qe + str(h)], ["EQ%d" % h])
-                op("t", [mm(T.pE[:, 80 * h:80 * h + 80], T.DM[:, 128 * j:128 * j + 128], T.XEG[:, 1280 * h + j:1280 * h + 1280:16],
-                            j == 0, j == 15) for j in M16], DMk + ["XEG%d" % h], ["pE"])
-            scan(T.UNC[:], T.RN[:], T.EQ[:], A.max, A.min, ["RN", "EQ0", "EQ1"], ["UNC"])
-            ts(T.NONEL[:], T.pE[:, 0:160], 0.5, A.is_lt, None, None, ["pE"], ["NONEL"])
-            tt(T.WW[:], T.UNC[:, 15:V:16], T.NONEL[:], A.mult, ["UNC", "NONEL"], ["WW"])
-            tt(T.QL[:], T.QN16[:, ks], T.WW[:], A.mult, ["QN%d" % k, "WW"], ["QL"])
-            cp(T.QLU[:], T.QL[:], ["QL"], ["QLU"])
-        for a, b, q in PARTS:
-            o, i = T.XVG[:, 16 * a:16 * b], T.XSN[:, 0:2592].indirect(T.QLU[:, a:b])
-            if q == "s":
-                act(o, i, XS + ["QLU"], ["XVG%d" % a])
-            else:
-                cp(o, i, XS + ["QLU"], ["XVG%d" % a])
-        for a, b, q in (PARTS[0], PARTS[2], PARTS[1]):
-            op("t", [mm(T.pD[:, a:b], T.ID[:], T.XVG[:, 16 * a + j:16 * b:16], j == 0, j == 15) for j in M16],
-               ["ID", "XVG%d" % a], ["pD"])
-        if t:
-            scan(T.MXS[:], T.RM[:], T.XEG[:], A.mult, A.max, ["RM", "XEG0", "XEG1"], ["MXS"])
-            tt(T.OC[:], T.QM[:, ks], T.WW[:], A.mult, ["QM%d" % k, "WW"], ["OC"])
-            ts(T.MP[:], T.MXS[:, 15:V:16], 1.0, A.max, 1.0, A.subtract, ["MXS"], ["MP"])
-            tt(T.CODB[:], T.OC[:], T.PREB[:], A.add, ["OC", "PREB"], ["CODB"])
-            if t >= 2:
-                act(T.SGN[:, lo:V], xe[:, lo:V], tab("XE" + cur, lo // 160, 16), ["SGN"], func=F.Sign)
-            if t < 4:
-                own_s1(k1)
-                expand(k1, qe1, 0)
-            tt(T.DEG[:], T.pD[:, 0:160], T.MP[:], A.add, ["pD", "MP"], ["DEG"])
-        else:
-            own_s1(0)
-            own_v1(0)
-            tt(T.CODB[:], T.QM[:, ks], T.PREB[:], A.add, ["QM0", "PREB"], ["CODB"])
-            act(T.XEA[:], T.FNA[:], whole("FNA") + ["NX"], whole("XEA"), func=F.Identity, scale=0.0, bias=nx)
-            own_s1(1)
-            expand(1, qe1, 0)
-            expand(1, qe1, 1)
-            ts(T.DM64[:], T.LVM[:], pm, A.is_equal, None, None, ["LVM", "PM"], ["DM64"])
-            ts(T.TR4[:], T.TC[:, 40:44], pm, A.add, None, None, ["T40", "PM"], ["TR4"])
-            fill(T.ZERO[:], 0.0, ["ZERO"])
-            cp(T.DEG[:], T.pD[:, 0:160], ["pD"], ["DEG"])
-        ts(T.OK[:], T.DEG[:], T.THR[:], A.is_le, None, None, ["DEG", "THR"], ["OK"])
-        op("t", [mm(T.pC[:, 0:10], T.BM[:, 128 * m:128 * m + 128], T.OK[:, m:160:16], m == 0, m == 15) for m in M16], BMk + ["OK"], ["pC"])
-        ts(T.D1[:], T.DEG[:], 255.0, A.min, 1.0, A.add, ["DEG"], ["D1"])
-        tt(T.SD[:], T.D1[:], T.SG[:, ks], A.mult, ["D1", "SG%d" % k], ["SD"])
-        if t:
-            tt(T.CODA[:], T.SD[:], T.PREA[:, ks], A.add, ["SD", "PREA%d" % k], ["CODA"])
-        else:
-            ts(T.CODA[:], T.SD[:], 512.0, A.add, None, None, ["SD"], ["CODA"])
-        if t < 4:
-            ts(T.HX[:, 1:11], T.pC[:, 0:10], 8.5, A.is_ge, None, None, ["pC"], ["HX"])
-        else:
-            tt(T.HX[:, 1:11], T.pC[:, 0:10], T.THW[:], A.is_ge, ["pC", "THW"], ["HX"])
-        scan(T.XSC[:, 0:11], T.ONES[:, 0:11], T.HX[:, 0:11], A.mult, A.add, ["ONES", "HX"], ["XSC"])
-        op("t", [mm(T.pC[:, 16:26], T.TRI[:], T.HX[:, 1:11], True, False), mm(T.pC[:, 16:26], T.GG[:], T.XSC[:, 0:10], False, True),
-                 mm(T.pC[:, 32:33], T.GG[:], T.XSC[:, 10:11], True, True)], ["TRI", "GG", "HX", "XSC"], ["pC"])
-        tt(T.U1[:], T.pC[:, 16:26], T.CW[:], A.subtract, ["pC", "CW"], ["U1"])
-        tt(T.U2[:], T.U1[:], T.HX[:, 1:11], A.mult, ["U1", "HX"], ["U2"])
-        tt(T.U3[:], T.U2[:], T.CW1[:], A.add, ["U2", "CW1"], ["U3"])
-        cp(T.SLU[:], T.U3[:], ["U3"], ["SLU"])
-        L1k, L2k, L3k = ("L1", t, r), ("L2", t, r), ("L3", t, r)
-        cp(T.CA[:, 0:320].indirect(T.SLU[:]), T.CODA[:], ["SLU", "CODA"], ["CA"])
-        if t:
-            if t >= 2:
-                op("t", [mm(T.pW[:, 16:16 + n // 16], T.JM[:, 128 * m:128 * m + 128], T.SGN[:, lo + m:V:16], m == 0, m == 15) for m in M16],
-                   ["JM", "SGN"], ["pW"])
-            ts(T.C1[:], T.CA[:, 0:64], 10, A.logical_shift_right, None, None, ["CA"], ["C1"])
-            cp(T.QCU[:], T.C1[:], ["C1"], ["QCU"])
-            hs = [(b, slice(512 * b, 512 * b + 512), T.QCU[:, 32 * b:32 * b + 32]) for b in range(2)]
-            for b, s, l in hs:
-                act(T.QG[:, s], fn[:, 0:2576].indirect(l), FNk + ["QCU"], ["QG%d" % b])
-                op("t", mm(T["pN%d" % b][:], T.IDF[:], T.QG[:, s], True, False), ["IDF", "QG%d" % b], ["pN%d" % b])
-            for b, s, l in hs:
-                bank = ("pD", "pE")[b]
-                act(T.AXC[:, s], xe[:, 0:2576].indirect(l), XEk + ["QCU"], ["AXC%d" % b], func=F.Abs)
-                act(T.SGC[:, s], xe[:, 0:2576].indirect(l), XEk + ["QCU"], ["SGC%d" % b], func=F.Sign)
-                op("t", [mm(T[bank][:], T.ID[:], T.BIAS[:], True, False), mm(T[bank][:], T.GS[:], T.AXC[:, s], False, False),
-                         mm(T[bank][:], T.ID[:], T.SGC[:, s], False, True)], ["ID", "BIAS", "SGC%d" % b, "GS", "AXC%d" % b], [bank])
-        ts(T.C2[:], T.CA[:, 0:64], 1023, A.bitwise_and, None, None, ["CA"], ["C2"])
-        ts(l1(t, r), T.C2[:], 512.0, A.subtract, None, None, ["C2"], [L1k])
-        ts(l1(t, r, 64, SL), T.BIAS[:, 0:8], 0.0, A.mult, nx, A.add, ["BIAS", "NX"], [L1k])
-        send(1, t, "L1", SL, SL)
-        cp(T.CB[:, 0:320].indirect(T.SLU[:]), T.CODB[:], ["SLU", "CODB"], ["CB"])
-        fill(l2(t, r, 64, SL), float(V), [L2k])
-        ts(T.C3[:], T.CB[:, 0:64], 8, A.logical_shift_right, None, None, ["CB"], ["C3"])
-        ts(T.C4[:], T.CB[:, 0:64], 255, A.bitwise_and, None, None, ["CB"], ["C4"])
+        top = B0 + 256 * t
+        qe = "QEB" if t % 2 else "QEA"
         if t == 0:
-            cp(l2(t, r), T.C3[:], ["C3"], [L2k])
-            send(2, t, "L2", SL, SL)
-        ts(T.LV[:], T.C4[:], 16.0, A.mult, float(4 * k + r), A.add, ["C4"], ["LV"])
-        ts(l3(t, r, 4, 14), T.U3[:], 64.0, A.min, None, None, ["U3"], [L3k])
-        if t:
-            for b, s, l in hs:
-                tt(T.MM[:, s], T.LV[:, 0:64].indirect(T.EXPL[:, 32 * b:32 * b + 32]), T.QG[:, s], A.is_equal, ["LV", "EXPL", "QG%d" % b], ["MM%d" % b])
-                op("t", mm(T["pN%d" % b][:], T.IDB[:], T.MM[:, s], False, True), ["IDB", "MM%d" % b], ["pN%d" % b])
-        tt(T.LVM[:], T.LV[:], T.DM64[:], A.mult, ["LV", "DM64"], ["LVM"])
-        scan(T.LVS[:], T.RM[:, 0:64], T.LVM[:], A.mult, A.add, ["RM", "LVM"], ["LVS"])
-        cp(l3(t, r, 14, 18), T.LVS[:, 15:64:16], ["LVS"], [L3k])
-        if t == 0:
-            ts(l3(t, r, 0, 4), T.TR4[:], 0.0, A.mult, None, None, ["TR4"], [L3k])
-            send(3, t, "L3", LL, 18)
+            for a, e, q in SIZES0:
+                move(q, b("XG", 16 * a, 16 * e), by(b("XB", 0, B0), b("XL", a, e)))
+                pe(b("pD", a, e), [(b("ID"), b("XG", 16 * a + j, 16 * e, 16)) for j in range(16)])
+            own(0)
         else:
+            for q in ORDER:
+                cp(blk("NB", t - 1, q), cu(t - 1, q, 0, 64))
+            if t > 1:
+                for q in (3, 2, 1, 0):
+                    claims("NB", t - 1, q, cu(t - 1, q, 0, 64))
             if t < 4:
-                if k1:
-                    own_v1(k1)
-                own_v2(k1)
-            store_gone(t - 1)
-            for b in range(2):
-                bank = ("pD", "pE")[b]
-                scan(T.TS[:, 512 * b:512 * b + 512], T.RM[:, 0:512], T[bank][:], A.mult, A.max, ["RM", bank], ["TS%d" % b])
-            cp(T.TI[:], T.TS[:, 15:1024:16], ["TS0", "TS1"], ["TI"])
-            ts(T.TB[:], T.TI[:], 2, A.bitwise_and, None, None, ["TI"], ["TB"])
-            cp(T.TF[:], T.TB[:], ["TB"], ["TF"])
-            op("t", [mm(T.pC[:, 48:52], T.JM[:, 128 * m:128 * m + 128], T.TF[:, m:64:16], m == 0, m == 15) for m in M16], ["JM", "TF"], ["pC"])
-            op("t", [mm(T.pM[:, 0:256], T.ID[:], T.MASKJ[:], True, False)] +
-               [mm(T.pM[:, 64 * s:64 * s + 64], T.GJ[:], T.TF[:], False, s == 3) for s in range(4)], ["ID", "MASKJ", "GJ", "TF"], ["pM"])
-            for b in range(2):
-                scan(T.NS[:, 512 * b:512 * b + 512], T.RN[:, 0:512], T["pN%d" % b][:], A.max, A.min, ["RN", "pN%d" % b], ["NS%d" % b])
-            tt(l2(t, r), T.NS[:, 15:1024:16], T.C3[:], A.min, ["NS0", "NS1", "C3"], [L2k])
-            send(2, t, "L2", SL, SL)
-            tt(T.CV[:], T.NONEL[:], T.WW[:], A.subtract, ["NONEL", "WW"], ["CV"])
-            cp(T.EW[:], T.pC[:, 48:52], ["pC"], ["EW"])
-            for s in range(4):
-                ts(T.DC[:, 64 * s:64 * s + 64], T.pM[:, 64 * s:64 * s + 64], T.EW[:, s:s + 1], A.is_equal, 4096.0, A.mult, ["pM", "EW"], ["DC%d" % s])
-            scan(T.DS[:], T.R64[:], T.DC[:], A.mult, A.max, ["R64"] + ["DC%d" % s for s in range(4)], ["DS"])
-            tt(T.EO[:, 0:4], T.DS[:, 63:256:64], T.EW[:], A.add, ["DS", "EW"], ["EO0"])
-            ts(T.EO[:, 4:8], T.EO[:, 0:4], 2559.5, A.is_lt, None, None, ["EO0"], ["EO1"])
-            tt(T.EO[:, 8:12], T.EO[:, 0:4], T.TR4[:], A.subtract, ["EO0", "TR4"], ["EO2"])
-            tt(T.EO[:, 12:16], T.EO[:, 8:12], T.EO[:, 4:8], A.mult, ["EO1", "EO2"], ["EO3"])
-            tt(T.EO[:, 16:20], T.EO[:, 12:16], T.TR4[:], A.add, ["EO3", "TR4"], ["EO4"])
-            ts(l3(t, r, 0, 4), T.EO[:, 16:20], float(lo), A.subtract, None, None, ["EO4"], [L3k])
-            send(3, t, "L3", LL, 18)
-        if t < 4:
-            ts(T.TM[:], T.pC[:, 32:33], 64.0, A.min, None, None, ["pC"], ["TM"])
-            op("t", mm(T.pC[:, 40:41], T.ONES[:], T.TM[:], True, True), ["ONES", "TM"], ["pC"])
-            if t == 0:
-                own_v1(1)
-                own_v2(1)
-            own_s2(k1)
-            ts(T.AI[:], T.pC[:, 40:41], 1.0 / 16.0, A.mult, None, None, ["pC"], ["AI"])
-            ts(T.AJ[:], T.AI[:], 7, A.bitwise_and, None, None, ["AI"], ["AJ"])
-            tt(T.THR[:], T.LIMF[:], T.AJ[:], A.add, ["LIMF", "AJ"], ["THR"])
-            fill(T.CA[:, 0:64], V * 1024 + 512, ["CA"])
-            cp(T.CB[:, 0:64], T.CBI[:], ["CBI"], ["CB"])
-        if t == 0:
-            ts(T.THA[:], T.U3[:], 63.5, A.is_lt, 100.0, A.mult, ["U3"], ["THA"])
-            ts(T.THW[:], T.THA[:], 8.5, A.max, None, None, ["THA"], ["THW"])
-            iota(T.FNB[:], [[0, W]], V, 0, whole("FNB"))
-            fill(T.RN[:], 0.0, ["RN"])
-            fill(T.RN[:, 0:2560:16], 8192.0, ["RN"])
-            ts(T.JM[:], T.BM[:], T.TC[:, 34:35], A.mult, None, None, BMk + ["WJ"], ["JM"])
-            ts(T.GJ[:], T.GG[:], T.TC[:, 34:35], A.mult, None, None, ["GG", "WJ"], ["GJ"])
-            ts(T.GN[:], T.GG[:], T.TC[:, 44:45], A.mult, None, None, ["GG", "WN"], ["GN"])
-            ts(T.GS[:], T.GG[:], 64.0, A.mult, None, None, ["GG"], ["GS"])
-            ts(T.IDB[:], T.ID[:], 4096.0, A.mult, None, None, ["ID"], ["IDB"])
-            cp(T.IDF[:], T.ID[:], ["ID"], ["IDF"])
-            ts(T.MASKJ[:], T.MASKI[:], pm, A.is_ge, 8192.0, A.mult, ["MASKI", "PM"], ["MASKJ"])
-            fill(T.R64[:], 1.0, ["R64"])
-            fill(T.R64[:, 0:256:64], 0.0, ["R64"])
-        else:
-            if t < 4:
-                expand(k1, qe1, 1)
+                expand(t + 1, range(16))
+            keys(t - 1)
+            outputs("YN", "NB", t - 1)
             if t == 1:
-                act(T.XEB[:], T.FNB[:], whole("FNB") + ["NX"], whole("XEB"), func=F.Identity, scale=0.0, bias=nx)
-            if t >= 2:
-                ts(T.JL[:, lo // 16:160], T.pW[:, 16:16 + n // 16], 2607.5, A.add, None, None, ["pW"], ["JL"])
-            if t == 4:
-                cl = 160 * (15 - r)
-                act(T.AXR[:], xe[:, cl:cl + 160], [("XE" + cur, 15 - r)], ["AXR"], func=F.Abs)
-                ts(T.LIVE[:], T.AXR[:], 0.5, A.is_lt, None, None, ["AXR"], ["LIVE"])
-                tt(T.CV[:], T.CV[:], T.LIVE[:], A.mult, ["CV", "LIVE"], ["CV"])
-            ts(T.CV2[:], T.CV[:], float(V), A.mult, None, None, ["CV"], ["CV2"])
-            col = T.NBN[:, 4 * k + r:V:16]
-            tt(col, col, T.CV2[:], A.max, NB + ["CV2"], NB)
-            keep_sizes(t - 1)
-            store_sizes(t - 1)
-            store_names(t - 1)
-        b0 = lo // 160
-        wx, wf = tab("XE" + cur, b0, 16, "n"), tab("FN" + cur, b0, 16, "n")
-        if t < 4:
-            to = nxt if t >= 2 else cur
-            if t:
+                names(3)
+            if t > 1:
+                lists(b("pL", 0, 80 * (t - 1)), "MB", 0, SM * 4 * (t - 1))
+            banks = ("pZ", "pN0", "pN1")
+
+            def cover(j):
+                a, e = COVER[j]
+                tt(b("EQ", 16 * a, 16 * e), by(b("NB", 0, top), b("QL", a, e)), b(qe, 16 * a, 16 * e), A.is_equal)
+                pe(b(banks[j], a, e), [(b("ID"), b("ELB", a, e))] + [(b("IDN"), b("EQ", 16 * a + i, 16 * e, 16)) for i in range(16)])
+
+            def pick(j):
+                a, e = COVER[j]
+                tt(b("XL4", a, e), b(banks[j], a, e), b("QX", a, e), A.min)
+                cp(b("XL", a, e), b("XL4", a, e))
+                for a, e, q in SIZES[j]:
+                    move(q, b("XG", 16 * a, 16 * e), by(b("XB", 0, top), b("XL", a, e)))
+
+            def sums(j):
+                a, e = COVER[j]
+                pe(b("pD", a, e), [(b("ID"), b("XG", 16 * a + i, 16 * e, 16)) for i in range(16)], True, False)
+                scan(b("MXS", 16 * a, 16 * e), b("RM", 16 * a, 16 * e), b("XG", 16 * a, 16 * e), A.mult, A.min)
+                pe(b("pD", a, e), [(b("IDX"), b("MXS", 16 * a + 15, 16 * e, 16))], False, True)
+            cover(0)
+            if t > 1:
                 for q in (3, 2, 1, 0):
-                    cp(xe[:, lo:W].indirect(l3(t, q, 0, 4)), l1(t, q), [("L1", t, q), ("L3", t, q)], wx)
-            for buf, nm, ld in (("L1", "XE", l1), ("L2", "FN", l2)):
-                for q in range(N):
-                    bk = 15 - 4 * t - q
-                    act(T[nm + to][:, 160 * bk:160 * bk + 160], ld(t, q, 0, SL).indirect(l3(t, q, 4, 14)), [(buf, t, q), ("L3", t, q)], [(nm + to, bk)])
-            if t:
-                for q in (3, 2, 1, 0):
-                    cp(fn[:, lo:W].indirect(l3(t, q, 0, 4)), l2(t, q), [("L2", t, q), ("L3", t, q)], wf)
-            if t >= 2:
-                act(T["XE" + to][:, lo:V], xe[:, 0:2576].indirect(T.JL[:, lo // 16:160]), XEk + ["JL"], tab("XE" + to, b0, 16))
-                cp(T["FN" + to][:, lo:V], fn[:, 0:2576].indirect(T.JL[:, lo // 16:160]), FNk + ["JL"], tab("FN" + to, b0, 16))
-                cur, nxt = nxt, cur
-        else:
+                    claims("XB", t - 1, q, blk("XB", t - 1, q))
+            pick(0)
+            cover(1)
+            if t > 1:
+                cp(b("JL", 0, 80 * (t - 1)), b("pL", 0, 80 * (t - 1)))
+            pick(1)
+            cover(2)
+            sums(0)
+            pick(2)
+            sums(1)
+            sums(2)
+        ts(b("OK"), b("pD", 0, 160), b("THR"), A.is_le)
+        pe(b("pC", 0, 160), ([(b("ID"), b("DEAD"))] if t == 4 else []) + [(b("GG"), b("OK"))])
+        ts(b("D1", 0, 160), b("pD", 0, 160), 255.0, A.min, MAGIC, A.add)
+        ts(b("HH"), b("pC", 0, 160), 8.5, A.is_ge)
+        scan(b("RR"), b("HH"), b("ZERO"), A.add, A.min, -65.0)
+        for s in range(4):
+            act(b("EQ", 160 * s, 160 * s + 160), b("RR"), F.Sign, bias=col(8 + s), scale=-1.0, total=b("ACC", s, s + 1))
+        tt(b("YY"), b("HH"), b("RR"), A.mult)
+        ts(mb(t, r, 0, 160), b("YY"), col(6), A.max, col(12 + t), A.mult)
+        if t > 1:
             for q in (3, 2, 1, 0):
-                cp(xe[:, lo:W].indirect(l3(t, q, 0, 4)), l1(t, q), [("L1", t, q), ("L3", t, q)], wx)
-            keep_sizes(t)
-            store_names(t)
-            dma("y", "d_yn", [lambda: g.sync.dma_start(T.yn[:], T.NBN[:, 0:V])], NB, ())
-            store_sizes(t)
-            dma("y", "d_yx", [lambda: g.sync.dma_start(T.yx[:], T.XSN[:, 16:2576])], XS, ())
-            xo, xk = T["XE" + nxt], "XE" + nxt
-            act(xo[:, 0:1280], xe[:, 0:2576].indirect(T.JL[:, 0:80]), XEk + ["JL"], tab(xk, 0, 8))
-            cp(xo[:, 1280:V], xe[:, 0:2576].indirect(T.JL[:, 80:160]), XEk + ["JL"], tab(xk, 8, 16))
-            for j, (a, b) in enumerate(((0, 480), (480, 960), (960, 1280), (1280, 1760), (1760, 2240), (2240, 2560))):
-                bank = ("pN0", "pN1", "pM", "pW", "pD", "pE")[j]
-                act(T.SGN[:, a:b], xo[:, a:b], tab(xk, a // 160, b // 160), [("SGN", j)] + (["SGN"] if j == 0 else []), func=F.Sign)
-                op("t", mm(T[bank][:, 0:b - a], T.GN[:], T.SGN[:, a:b], True, True), ["GN", ("SGN", j)], [bank])
-                for p in range(a, b, 160):
-                    c = 15 - p // 160
-                    tt(T.YJ[:, c:V:16], T[bank][:, p - a:p - a + 160], T.NU[:, c:V:16], A.max, [bank, "NU"], [("YJ", c)])
-            dma("y", "d_yj", [lambda i=i: g.sync.dma_start(T.yj[i:i + 1, :], T.YJ[16 * i:16 * i + 1, :]) for i in range(8)], [("YJ", c) for c in M16], ())
+                claims("KT", t - 1, q, blk("KT", t - 1, q))
+        ts(b("LN"), b("ACC"), 0.5, A.mult, 80.0, A.add)
+        ln = b("LN")
+        if t:
+            cp(b("QC"), by(b("QL4"), ln))
+        act(mb(t, r, 176, 240), by(b("D1"), ln), bias=-MAGIC)
+        act(mb(t, r, 240, 304), by(b("LANE"), ln))
+        send(1, t, mb(t, r, 0, SM))
+        if t == 0:
+            cp(b("ST", 0, 64), by(b("QM", 0, 176), ln))
+            cp(b("ST", 64, 68), b("TR"))
+        else:
+            h = [(512 * i, 512 * i + 512, b("QC", 32 * i, 32 * i + 32)) for i in range(2)]
+            pe(b("pM", 0, 224), [(b("ID"), b("MSK"))], True, False)
+            cp(b("KG", 0, 512), by(b("KT", 0, top), h[0][2]))
+            act(b("KG", 512, 1024), by(b("KT", 0, top), h[1][2]))
+            for i, (a, e, l) in enumerate(h):
+                act(b("QG", a, e), by(b("NB", 0, top), l))
+            for a, e, l in h:
+                scan(b("TS", a, e), b("RK", a, e), b("KG", a, e), A.add, A.max)
+            ts(b("RK1"), b("TS", 15, 1024, 16), MAGIC128, A.add, MAGIC128, A.subtract)
+            tt(b("TF"), b("TS", 15, 1024, 16), b("RK1"), A.subtract)
+            pe(b("pM", 0, 64), [(b("GJ"), b("TF"))], False, False)
+            for s in range(4):
+                pe(b("pM", 64 + 8 * s * (s + 1), 64 + 8 * (s + 1) * (s + 2)), [(b("GJ"), b("TF", 0, 16 * s + 16))], False, s == 3)
+            ts(b("LV"), by(b("LANE"), ln), 16.0, A.mult, float(4 * k + r), A.add)
+
+            def mine(i):
+                a, e, l = h[i]
+                pe(b("pN%d" % i), [(b("IDF"), b("QG", a, e))], True, False)
+                tt(b("MM", a, e), by(b("LV"), b("EXPL", 32 * i, 32 * i + 32)), b("QG", a, e), A.is_equal)
+                pe(b("pN%d" % i), [(b("IDB"), b("MM", a, e))], False, True)
+            mine(0)
+            scan(b("EWS"), b("RM", 0, 64), b("pM", 0, 64), A.mult, A.max)
+            for s in range(4):
+                ew = b("EWS", 16 * s + 15, 16 * s + 16)
+                ts(b("DC", 8 * s * (s + 1), 8 * (s + 1) * (s + 2)), b("pM", 64 + 8 * s * (s + 1), 64 + 8 * (s + 1) * (s + 2)), ew, A.not_equal, ew, A.mult)
+            mine(1)
+            ts(b("CV"), b("XL4"), 0.5, A.is_le, float(V), A.mult)
+            tt(b("OC", 0, 160), b("QM2"), b("CV"), A.max)
+            scan(b("NS", 0, 512), b("RN", 0, 512), b("pN0"), A.max, A.min)
+            scan(b("DS"), b("RD"), b("DC"), A.max, A.min)
+            ts(b("OCC"), by(b("OC"), ln), float(V), A.min)
+            scan(b("NS", 512, 1024), b("RN", 512, 1024), b("pN1"), A.max, A.min)
+            for s in range(4):
+                j = 8 * (s + 1) * (s + 2)
+                ts(b("ST", 64 + s, 65 + s), b("DS", j - 1, j), b("TR", s, s + 1), A.max)
+            tt(b("ST", 0, 64), b("NS", 15, 1024, 16), b("OCC"), A.min)
+            if t > 1:
+                for j in range(4 * (t - 1)):
+                    act(b("MB", SM * j, SM * j + 160), by(b("KT", 0, top), b("JL", 20 * j, 20 * j + 10)))
+        cp(cu(t, r, 0, 68), b("ST", 0, 68))
+        send(2, t, cu(t, r, 0, 68))
+        if t == 0:
+            expand(1, range(8, 16))
+            names(2)
+            iota(b("KT", NAT, B0), [[1, B0 - NAT]], 0, 0)
+            ts(b("DEAD"), b("YY"), -0.5, A.is_lt, -16.0, A.mult)
+            ts(b("LIVE"), b("YY"), -0.5, A.is_ge)
+            places(1)
+            later_constants()
+            masks()
+        if t < 4:
+            ts(b("TM"), b("RR", 159, 160), 65.0, A.add, 64.0, A.min)
+            pe(b("pC", 200, 201), [(b("O16"), b("TM"))])
+            if t:
+                places(t + 1)
+            for a, e, q in LISTS:
+                move(q, b("GM", 16 * a, 16 * e), by(b("MB", 0, SM * 4 * (t + 1)), b("QP", a, e)))
+            for a, e, q in LISTS:
+                lists(b("pL", a, e), "GM", 16 * a, 16 * e)
+        if t == 4:
+            tt(b("CV"), b("CV"), b("LIVE"), A.mult)
+            pe(b("pL", 0, 160), [(b("JM", 128 * c, 128 * c + 128), b("MB", SM * c, SM * c + 160)) for c in range(16)])
+        if t:
+            x = b("NB", NAT + 4 * k + r, NAT + V, 16)
+            tt(x, x, b("CV"), A.max)
+        lists(b("pK", 256, 336), "MB", SM * 4 * t, SM * 4 * (t + 1))
+        if t < 4:
+            cp(b("AI"), b("pC", 200, 201))
+            ts(b("AJ"), b("AI"), 7, A.bitwise_and)
+            tt(b("THR"), b("LIMF"), b("AJ"), A.add)
+            if t < 3:
+                own(t + 1)
+            k1 = (t + 1) % 4
+            cp(b("QL"), b("pL", 0, 160))
+            ts(b("ELB"), b("pL", 0, 160), 128.0, A.mult, 8192.0, A.max)
+            tt(b("QX"), b("pL", 0, 160), qf(k1, "QN"), A.max)
+            tt(b("QM2"), b("pL", 0, 160), qf(k1, "QM"), A.max)
+            cp(b("QL4", 0, 160), b("pL", 0, 160))
+        else:
+            tt(b("OL4"), b("pL", 0, 160), b("UU"), A.max)
+            cp(b("OL"), b("OL4"))
+        tt(b("LO4"), b("pK", 256, 336), b("CC"), A.max)
+        cp(b("LO"), b("LO4"))
+        if t < 4:
+            ts(b("CC"), b("CC"), 4.0 if t < 3 else -12.0, A.add)
+        for q in range(N):
+            act(blk("XB", t, q), mb(t, q, 176, 240))
+        outputs("YX", "XB", t)
+        if t < 4:
+            act(blk("XB", t, 0, 4), blk("XB", t, 0, 4), scale=-TINY)
+    dma("y", "d_yx", [lambda: g.sync.dma_start(T.yx[:], T.YX[:])], b("YX")[1], ())
+    keys(4)
+    for q in ORDER:
+        cp(blk("NB", 4, q), cu(4, q, 0, 64))
+    outputs("YN", "NB", 4)
+    dma("y", "d_yn", [lambda: g.sync.dma_start(T.yn[:], T.YN[:])], b("YN")[1], ())
+    for q in (3, 2, 1, 0):
+        claims("KT", 4, q, blk("KT", 4, q))
+    cp(b("YJ", 0, 1536), by(b("KT", 0, B0 + 1024), b("OL", 0, 96)))
+    act(b("YJ", 1536, V), by(b("KT", 0, B0 + 1024), b("OL", 96, 160)))
+    dma("s", "d_yj", [lambda i=i: g.scalar.dma_start(T.yj[i:i + 1, :], T.YJ[16 * i + 6:16 * i + 7, :]) for i in range(8)], b("YJ")[1], ())
     finish([("lo", nsend[0])])

@@ -4,7 +4,7 @@ from concourse.mybir import AluOpType, ActivationFunctionType
 A = AluOpType
 F = ActivationFunctionType
 V, N, R = 2560, 4, 5
-NAT, DUMP, B0 = 16, 2592, 2688
+NAT, PAD, DUMP, B0 = 16, 2576, 2592, 2688
 TW = B0 + 64 * N * R
 SM, SC = 320, 72
 MAGIC = 1.5 * 2.0 ** 23
@@ -12,26 +12,26 @@ MAGIC128 = 1.5 * 2.0 ** 30
 TINY = 2.0 ** -14
 COVER = ((0, 64), (64, 128), (128, 160))
 SIZES = (((0, 64, "s"),), ((64, 128, "s"),), ((128, 160, "v"),))
-LISTS = ((0, 96, "s"), (96, 160, "v"))
-SIZES0 = ((0, 40, "s"), (40, 80, "v"), (80, 120, "s"), (120, 160, "v"))
+LISTS = ((0, 80, "s"), (80, 160, "v"))
+SIZES0 = ((0, 20, "s"), (20, 40, "v"), (40, 60, "s"), (60, 80, "v"), (80, 100, "s"), (100, 120, "v"), (120, 140, "s"), (140, 160, "v"))
 
 SCRATCH = {}
 for _d, _spec in (
     ("float32", "NB:%d KT:%d YN:2560 YJ:2560 QEA:2560 QEB:2560 QF:640 QN:640 QM:704 QL4:176 QX:160 XL4:160 CV:160 QM2:160 OC:176 D1:176 "
-     "LANE:176 ACC:4 LV:64 OCC:64 KG:1024 QG:1024 TS:1024 NS:1024 RK1:64 EWS:64 DC:160 DS:160 ST:72 TR:4 CC:80 LO4:80 UU:160 OL4:160 "
-     "LIMF:1 THR:1 TC:48 IDF:128 NE:160 QA:160 QB:160 SCR:160" % (TW, TW)),
-    ("bfloat16", "XB:%d MB:%d YX:2560 EQ:2560 XG:2560 MXS:2560 GM:2560 RM:2560 RK:1024 RN:1024 RD:160 MM:1024 JM:2048 ELB:160 OK:160 "
+     "LANE:176 ACC:4 LV:64 OCC:64 KG:1024 QG:1024 TS:1024 NS:1024 RK1:64 EWS:64 DC:256 DS:256 ST:72 TR:4 CC:80 LO4:80 UU:160 OL4:160 "
+     "LIMF:1 THR:1 TC:48 IDF:128 NE:640 QA:640 QB:640 SCR:160" % (TW, TW)),
+    ("bfloat16", "XB:%d MB:%d YX:2560 EQ:2560 XG:2560 MXS:2560 GM:2560 RM:2560 RK:1024 RN:1024 RD:256 MM:1024 JM:2048 ELB:160 OK:160 "
      "HH:160 RR:160 YY:160 ZERO:160 DEAD:160 LIVE:160 TF:64 TM:1 ONES:128 O16:128 ID:128 G1:128 GG:128 GW:128 IDN:128 IDX:128 IDB:128 GJ:128 "
-     "W1:128 W2:128 CST:256 MSK:224 MK1:224" % (TW, SM * N * R)),
-    ("int32", "LIMI:1 AI:1 AJ:1 QI:160 QI2:160 TCI:2 EXPI:64"),
-    ("uint16", "CU:%d QL:160 XL:160 QP:160 LN:4 QC:64 EXPL:64 JL:240 LO:80 OL:160" % (SC * N * R)),
+     "W1:128 W2:128 CST:256 MSK:320 MK1:320 SG:640" % (TW, SM * N * R)),
+    ("int32", "LIMI:1 AI:1 AJ:1 QI:640 QI2:640 TCI:2 EXPI:64"),
+    ("uint16", "CU:%d QL:160 XL:160 QP:640 LN:4 QC:64 EXPL:64 JL:240 LO:80 OL:160" % (SC * N * R)),
 ):
     for _e in _spec.split():
         SCRATCH[_e.split(":")[0]] = ("sbuf", [128, int(_e.split(":")[1])], _d)
 for _e in "pZ pD pC pL pN0 pN1 pM pK".split():
     SCRATCH[_e] = ("psum", [128, 512], "float32")
-SEMAPHORES = ["v", "s", "t", "p", "lo", "d_nb0", "d_nb1", "d_xs", "d_lim", "d_yn", "d_yx", "d_yj"] + [
-    "a%d_%d_%d" % (k, t, q) for k in (1, 2) for t in range(R) for q in range(N)]
+SEMAPHORES = ["v", "s", "t", "p", "lo", "d_xs", "d_lim", "d_yn", "d_yx", "d_yj"] + ["d_nb%d" % j for j in range(4)] + [
+    "a%d_%d_%d" % (k, t, q) for k in (1, 2) for t in range(R) for q in range(N)] + ["a3_4_%d" % q for q in range(N)]
 
 
 def queues(g, T):
@@ -169,10 +169,11 @@ def rank_program(g, core, T, topo):
     def col(j):
         return b("TC", j, j + 1)
 
-    dma("y", "d_xs", [lambda: g.sync.dma_start(T.XB[:, NAT:NAT + V], T.xs[:])], (), b("XB", NAT, NAT + V)[1])
-    dma("s", "d_nb0", [lambda: g.scalar.dma_start(T.NB[:, NAT:NAT + 1280], T.nb[:, 0:1280])], (), b("NB", NAT, NAT + 1280)[1])
-    dma("y", "d_nb1", [lambda: g.sync.dma_start(T.NB[:, NAT + 1280:NAT + V], T.nb[:, 1280:V])], (), b("NB", NAT + 1280, NAT + V)[1])
     dma("s", "d_lim", [lambda: g.scalar.dma_start(T.LIMI[:], T.lim[:])], (), b("LIMI")[1])
+    dma("y", "d_xs", [lambda: g.sync.dma_start(T.XB[:, NAT:PAD], T.xs[:])], (), b("XB", NAT, PAD)[1])
+    for j in range(4):
+        dma("y", "d_nb%d" % j, [lambda: g.sync.dma_start(T.NB[:, NAT + 640 * j:NAT + 640 * j + 640], T.nb[:, 640 * j:640 * j + 640])],
+            (), b("NB", NAT + 640 * j, NAT + 640 * j + 640)[1])
 
     iota(b("TCI", 0, 1), [[1, 1]], 0, 1)
     fill(b("ONES"), 1.0)
@@ -185,16 +186,21 @@ def rank_program(g, core, T, topo):
     iota(b("CC"), [[1, 4], [256, 20]], NAT, 0)
     iota(b("CST"), [[0, 4], [1, 64]], -64, 0)
     iota(b("SCR", 0, 160), [[16, 160]], NAT, 0)
-    fill(b("XB", 0, NAT), 0.0)
-    fill(b("XB", NAT + V, B0), 0.0)
-    fill(b("NB", 0, NAT), float(V))
-    fill(b("NB", NAT + V, B0), float(V))
+    iota(b("MK1", 0, 64), [[0, 4], [1, 16]], 0, 0)
+    iota(b("MK1", 64, 320), [[-16, 4], [1, 64]], 0, 0)
+    iota(b("KT", NAT, PAD), [[1, V]], 0, 0)
     fill(b("JM"), 0.0)
+    for name, n, x, y in (("RM", V, 1.0, 0.0), ("RK", 1024, 128.0, -2.0 ** 24), ("RN", 1024, 0.0, 8192.0), ("RD", 256, 0.0, 8192.0)):
+        fill(b(name), x)
+        fill(b(name, 0, n, 64 if name == "RD" else 16), y)
+    for name, x in (("XB", 0.0), ("NB", float(V))):
+        fill(b(name, 0, NAT), x)
+        fill(b(name, PAD, B0), x)
+    fill(b("KT", 0, NAT), 0.0)
     fill(b("ZERO"), 0.0)
-    fill(b("D1", 160, 176), MAGIC)
-    fill(b("OC", 160, 176), float(V))
-    fill(b("QM", 160, 176), float(V))
-    fill(b("QL4", 160, 176), 0.0)
+    fill(b("W1"), 0.0)
+    for name, x in (("D1", MAGIC), ("OC", float(V)), ("QM", float(V)), ("QL4", 0.0)):
+        fill(b(name, 160, 176), x)
     for t in range(R):
         fill(mb(t, r, 160, 176), 0.0)
         fill(mb(t, r, 304, 320), 0.0)
@@ -204,84 +210,70 @@ def rank_program(g, core, T, topo):
     e0, e1, e4, e5, e6 = col(1), col(2), col(3), col(4), col(5)
     for c_, j in ((e0, 0), (e1, 1), (e4, 4), (e5, 5), (e6, 6)):
         ts(c_, pm, float(j), A.is_equal)
-    ts(b("TR"), b("TR"), pm, A.add)
-    ts(b("TC", 8, 12), b("TR"), -64.5, A.add)
-    ts(col(6), e0, -63.0, A.mult, -1.0, A.add)
-    for t in range(R):
-        ts(col(12 + t), e1, -float(B0 // 64 + 1 + 4 * t + r), A.mult, e0, A.add)
     ts(col(7), e1, 64.0, A.mult, e0, A.add)
+    ts(col(17), e5, 64.0, A.mult, e4, A.add)
     ts(b("GW"), b("GG"), col(7), A.mult)
     for m in range(16):
         act(b("JM", 128 * m + m, 128 * m + 128, 16), b("GW", m, 128, 16))
+    ts(b("TR"), b("TR"), pm, A.add)
+    ts(col(6), e0, -63.0, A.mult, -1.0, A.add)
+    for t in range(R):
+        ts(col(12 + t), e1, -float(B0 // 64 + 1 + 4 * t + r), A.mult, e0, A.add)
+    ts(b("TC", 8, 12), b("TR"), -64.5, A.add)
+    cp(b("EXPL"), b("EXPI"))
+    ts(b("GJ"), b("GG"), col(17), A.mult)
+    for j in (4, 5):
+        ts(b("W1", j, 128, 16), b("GG", j, 128, 16), 2048.0, A.mult)
+    ts(b("W2"), b("ID"), e6, A.mult, 16.0, A.mult)
+    for name, x in (("IDN", -8192.0), ("IDX", -1.0 / TINY), ("IDB", 4096.0), ("IDF", 1.0)):
+        ts(b(name), b("ID"), x, A.mult)
+    ts(b("O16"), b("ONES"), 1.0 / 16.0, A.mult)
+    tt(col(18), e0, e4, A.add)
+    ts(col(19), e4, 32.0, A.mult)
+    tt(col(20), e1, e5, A.add)
+    tt(col(37), e4, e5, A.add)
+    ts(col(36), pm, 16.0, A.mult)
+    tt(col(21), col(20), e6, A.add)
+    for t in range(R):
+        ts(col(26 + t), e6, float(4 * t % 16), A.mult)
+    for q in range(N):
+        ts(col(22 + q), col(21), float(q), A.mult, col(19), A.add)
+    for t in range(R):
+        ts(col(31 + t), col(20), float(B0 // 64 + 1 + 4 * t), A.mult, col(26 + t), A.add)
+    for q in range(N):
+        ts(b("CST", 64 * q, 64 * q + 64), b("CST", 64 * q, 64 * q + 64), col(18), A.mult, col(22 + q), A.add)
+    ts(b("CC"), b("CC"), col(36), A.add)
+    ts(b("UU"), b("SCR"), pm, A.add)
+    ts(b("KT", PAD, B0), b("ZERO", 0, B0 - PAD), col(37), A.add, -4096.0, A.mult)
+    ts(b("MSK", 0, 64), b("MK1", 0, 64), pm, A.not_equal, -8192.0, A.mult)
+    ts(b("MSK", 64, 320), b("MK1", 64, 320), pm, A.is_ge, 8192.0, A.mult)
+    ts(b("MSK"), b("MSK"), -float(DUMP + 32), A.add)
     cp(b("LIMF"), b("LIMI"))
     ts(b("THR"), b("LIMF"), 0.3, A.add)
     ts(b("LIMF"), b("LIMF"), 0.3, A.add)
-
-    def later_constants():
-        cp(b("EXPL"), b("EXPI"))
-        ts(col(17), e5, 64.0, A.mult, e4, A.add)
-        ts(b("GJ"), b("GG"), col(17), A.mult)
-        fill(b("W1"), 0.0)
-        for j in (4, 5):
-            ts(b("W1", j, 128, 16), b("GG", j, 128, 16), 2048.0, A.mult)
-        ts(b("W2"), b("ID"), e6, A.mult, 16.0, A.mult)
-        ts(b("IDN"), b("ID"), -8192.0, A.mult)
-        ts(b("IDX"), b("ID"), -1.0 / TINY, A.mult)
-        ts(b("IDB"), b("ID"), 4096.0, A.mult)
-        ts(b("O16"), b("ONES"), 1.0 / 16.0, A.mult)
-        cp(b("IDF"), b("ID"))
-        tt(col(18), e0, e4, A.add)
-        ts(col(19), e4, 32.0, A.mult)
-        tt(col(20), e1, e5, A.add)
-        tt(col(21), col(20), e6, A.add)
-        for q in range(N):
-            ts(col(22 + q), col(21), float(q), A.mult, col(19), A.add)
-            ts(b("CST", 64 * q, 64 * q + 64), b("CST", 64 * q, 64 * q + 64), col(18), A.mult, col(22 + q), A.add)
-        for t in range(R):
-            ts(col(26 + t), e6, float(4 * t % 16), A.mult)
-            ts(col(31 + t), col(20), float(B0 // 64 + 1 + 4 * t), A.mult, col(26 + t), A.add)
-        ts(col(36), pm, 16.0, A.mult)
-        ts(b("CC"), b("CC"), col(36), A.add)
-        ts(b("UU"), b("SCR"), pm, A.add)
-        tt(col(37), e4, e5, A.add)
-        ts(b("KT", 0, NAT), b("ZERO", 0, NAT), col(37), A.add, -4096.0, A.mult)
-
-    def masks():
-        iota(b("MK1", 0, 64), [[0, 4], [1, 16]], 0, 0)
-        for s in range(4):
-            iota(b("MK1", 64 + 8 * s * (s + 1), 64 + 8 * (s + 1) * (s + 2)), [[1, 16 * s + 16]], -16 * s, 0)
-        ts(b("MSK", 0, 64), b("MK1", 0, 64), pm, A.not_equal, -8192.0, A.mult)
-        ts(b("MSK", 64, 224), b("MK1", 64, 224), pm, A.is_ge, 8192.0, A.mult)
-        ts(b("MSK"), b("MSK"), -float(DUMP + 32), A.add)
-        for name, n, x, y in (("RM", V, 1.0, 0.0), ("RK", 1024, 128.0, -2.0 ** 24), ("RN", 1024, 0.0, 8192.0)):
-            fill(b(name), x)
-            fill(b(name, 0, n, 16), y)
-        fill(b("RD"), 0.0)
-        for s in range(4):
-            fill(b("RD", 8 * s * (s + 1), 8 * s * (s + 1) + 1), 8192.0)
 
     def qf(k, name="QF", a=0, e=160):
         w = 176 if name == "QM" else 160
         return b(name, w * k + a, w * k + e)
 
     def names(k):
-        act(qf(k), b("NB", NAT + 4 * k + r, NAT + V, 16))
-        act(qf(k, "QN"), qf(k), bias=float(NAT))
+        act(qf(k), b("NB", NAT + 4 * k + r, PAD, 16))
 
     def own(k):
-        ts(b("QA"), b("LANE", 0, 160), 16.0, A.mult, float(4 * k + r), A.add)
-        tt(b("NE"), qf(k), b("QA"), A.is_equal)
-        ts(b("QB"), b("NE"), float(V), A.mult)
-        tt(qf(k, "QM"), qf(k), b("QB"), A.max)
+        act(qf(k, "QA"), b("LANE", 0, 160), scale=16.0, bias=float(4 * k + r))
+        tt(qf(k, "NE"), qf(k), qf(k, "QA"), A.is_equal)
+        act(qf(k, "QB"), qf(k, "NE"), scale=float(V))
+        tt(qf(k, "QM"), qf(k), qf(k, "QB"), A.max)
 
     def places(t):
         k = t % 4
-        cp(b("QI"), qf(k))
-        ts(b("QI2"), b("QI"), 15, A.bitwise_and)
-        ts(b("QA"), qf(k), 1.0 / 16.0, A.mult)
-        ts(b("QB"), b("QI2"), SM - 1.0 / 16.0, A.mult)
-        tt(b("NE"), b("QA"), b("QB"), A.add)
-        ts(b("QP"), b("NE"), float(SM * (4 * t - 1) + 160), A.min)
+        cp(qf(k, "QI"), qf(k))
+        act(qf(k, "QA"), qf(k), scale=1.0 / 16.0)
+        ts(qf(k, "QI2"), qf(k, "QI"), 15, A.bitwise_and)
+        ts(qf(k, "QB"), qf(k, "QI2"), SM - 1.0 / 16.0, A.mult)
+        tt(qf(k, "NE"), qf(k, "QA"), qf(k, "QB"), A.add)
+        ts(qf(k, "QP"), qf(k, "NE"), float(SM * (4 * t - 1) + 160), A.min)
+        act(qf(k, "QN"), qf(k), bias=float(NAT))
 
     def expand(t, js):
         for j in js:
@@ -303,7 +295,9 @@ def rank_program(g, core, T, topo):
         for q in range(N):
             if q != r:
                 arrive("a1_%d_%d" % (t, q), neng, mb(t, q, 0, SM)[1])
-                arrive("a2_%d_%d" % (t, q), neng, cu(t, q, 0, 68)[1])
+                arrive("a2_%d_%d" % (t, q), neng, cu(t, q, 0, 68 if t < 4 else 64)[1])
+                if t == 4:
+                    arrive("a3_%d_%d" % (t, q), neng, cu(t, q, 64, 68)[1])
 
     def claims(name, t, q, src):
         cp(by(b(name, DUMP, B0 + 256 * t), cu(t, q, 64, 68)), src)
@@ -314,29 +308,30 @@ def rank_program(g, core, T, topo):
             pe(b("pK", 64 * q, 64 * q + 64), [(b("W1"), mb(t, q, 176, 240)), (b("W2"), mb(t, q, 240, 304))], False, q == N - 1)
         act(blk("KT", t, 0, 4), b("pK", 0, 256), F.Identity, bias=col(31 + t))
 
-    def outputs(out, table, t):
+    def outputs(out, table, t, on="ssss"):
         for q in range(N):
-            c = (4 * t + q) % 16
-            act(b(out, c, V, 16), by(b(table, 0, B0 + 256 * (t + 1)), b("LO", 20 * q, 20 * q + 10)))
-        if t == 0:
-            for q in range(N):
-                act(b(table, NAT + q, NAT + V, 16), b(out, q, V, 16))
+            move(on[q], b(out, (4 * t + q) % 16, V, 16), by(b(table, 0, B0 + 256 * (t + 1)), b("LO", 20 * q, 20 * q + 10)))
+
+    def again(out, table):
+        for q in range(N):
+            act(b(table, NAT + q, PAD, 16), b(out, q, V, 16))
 
     ORDER = [r] + [q for q in (3, 2, 1, 0) if q != r]
-    names(0)
-    ts(b("XL", 0, 80), b("NB", NAT + r, NAT + 1280, 16), float(NAT), A.add)
-    names(1)
-    expand(1, range(8))
-    ts(b("XL", 80, 160), b("NB", NAT + 1280 + r, NAT + V, 16), float(NAT), A.add)
-
     for t in range(R):
         k = t % 4
         top = B0 + 256 * t
         qe = "QEB" if t % 2 else "QEA"
         if t == 0:
             for a, e, q in SIZES0:
+                if a % 40 == 0:
+                    ts(b("XL", a, a + 40), b("NB", NAT + 16 * a + r, NAT + 16 * a + 640, 16), float(NAT), A.add)
+                if a == 140:
+                    names(1)
+                    expand(1, range(6))
                 move(q, b("XG", 16 * a, 16 * e), by(b("XB", 0, B0), b("XL", a, e)))
-                pe(b("pD", a, e), [(b("ID"), b("XG", 16 * a + j, 16 * e, 16)) for j in range(16)])
+                if e % 80 == 0:
+                    pe(b("pD", e - 80, e), [(b("ID"), b("XG", 16 * e - 1280 + j, 16 * e, 16)) for j in range(16)])
+            names(0)
             own(0)
         else:
             for q in ORDER:
@@ -346,17 +341,18 @@ def rank_program(g, core, T, topo):
                     claims("NB", t - 1, q, cu(t - 1, q, 0, 64))
             if t < 4:
                 expand(t + 1, range(16))
+            ts(b("QL"), b("pL", 0, 160), float(PAD), A.max, float(PAD), A.subtract)
+            act(b("ELB"), b("pL", 0, 160), scale=128.0, bias=8192.0)
+            act(b("QL4", 0, 160), b("pL", 0, 160), F.Relu, bias=-float(PAD))
             keys(t - 1)
             outputs("YN", "NB", t - 1)
-            if t == 1:
-                names(3)
             if t > 1:
-                lists(b("pL", 0, 80 * (t - 1)), "MB", 0, SM * 4 * (t - 1))
+                lists(b("pM", 0, 80 * (t - 1)), "MB", 0, SM * 4 * (t - 1))
             banks = ("pZ", "pN0", "pN1")
 
             def cover(j):
                 a, e = COVER[j]
-                tt(b("EQ", 16 * a, 16 * e), by(b("NB", 0, top), b("QL", a, e)), b(qe, 16 * a, 16 * e), A.is_equal)
+                tt(b("EQ", 16 * a, 16 * e), by(b("NB", PAD, top), b("QL", a, e)), b(qe, 16 * a, 16 * e), A.is_equal)
                 pe(b(banks[j], a, e), [(b("ID"), b("ELB", a, e))] + [(b("IDN"), b("EQ", 16 * a + i, 16 * e, 16)) for i in range(16)])
 
             def pick(j):
@@ -371,32 +367,45 @@ def rank_program(g, core, T, topo):
                 pe(b("pD", a, e), [(b("ID"), b("XG", 16 * a + i, 16 * e, 16)) for i in range(16)], True, False)
                 scan(b("MXS", 16 * a, 16 * e), b("RM", 16 * a, 16 * e), b("XG", 16 * a, 16 * e), A.mult, A.min)
                 pe(b("pD", a, e), [(b("IDX"), b("MXS", 16 * a + 15, 16 * e, 16))], False, True)
+
+            def key_claims(qs):
+                if t > 1:
+                    for q in qs:
+                        claims("KT", t - 1, q, blk("KT", t - 1, q))
             cover(0)
+            tt(b("QX"), b("pL", 0, 160), qf(k, "QN"), A.max)
             if t > 1:
                 for q in (3, 2, 1, 0):
                     claims("XB", t - 1, q, blk("XB", t - 1, q))
             pick(0)
             cover(1)
-            if t > 1:
-                cp(b("JL", 0, 80 * (t - 1)), b("pL", 0, 80 * (t - 1)))
+            key_claims((3, 2))
+            tt(b("QM2"), b("pL", 0, 160), qf(k, "QM"), A.max)
             pick(1)
             cover(2)
+            if t > 1:
+                ts(b("JL", 0, 80 * (t - 1)), b("pM", 0, 80 * (t - 1)), float(PAD), A.max, float(PAD), A.subtract)
             sums(0)
             pick(2)
+            if t == 2:
+                again("YN", "NB")
+            if t == 3:
+                again("YX", "XB")
             sums(1)
             sums(2)
+            ts(b("CV"), b("XL4"), 0.5, A.is_le, float(V), A.mult)
+            tt(b("OC", 0, 160), b("QM2"), b("CV"), A.max)
         ts(b("OK"), b("pD", 0, 160), b("THR"), A.is_le)
         pe(b("pC", 0, 160), ([(b("ID"), b("DEAD"))] if t == 4 else []) + [(b("GG"), b("OK"))])
         ts(b("D1", 0, 160), b("pD", 0, 160), 255.0, A.min, MAGIC, A.add)
         ts(b("HH"), b("pC", 0, 160), 8.5, A.is_ge)
         scan(b("RR"), b("HH"), b("ZERO"), A.add, A.min, -65.0)
         for s in range(4):
-            act(b("EQ", 160 * s, 160 * s + 160), b("RR"), F.Sign, bias=col(8 + s), scale=-1.0, total=b("ACC", s, s + 1))
+            act(b("SG", 160 * s, 160 * s + 160), b("RR"), F.Sign, bias=col(8 + s), scale=-1.0, total=b("ACC", s, s + 1))
         tt(b("YY"), b("HH"), b("RR"), A.mult)
         ts(mb(t, r, 0, 160), b("YY"), col(6), A.max, col(12 + t), A.mult)
-        if t > 1:
-            for q in (3, 2, 1, 0):
-                claims("KT", t - 1, q, blk("KT", t - 1, q))
+        if t:
+            key_claims((1, 0))
         ts(b("LN"), b("ACC"), 0.5, A.mult, 80.0, A.add)
         ln = b("LN")
         if t:
@@ -407,106 +416,129 @@ def rank_program(g, core, T, topo):
         if t == 0:
             cp(b("ST", 0, 64), by(b("QM", 0, 176), ln))
             cp(b("ST", 64, 68), b("TR"))
+            cp(cu(t, r, 0, 68), b("ST", 0, 68))
+            send(2, t, cu(t, r, 0, 68))
         else:
             h = [(512 * i, 512 * i + 512, b("QC", 32 * i, 32 * i + 32)) for i in range(2)]
-            pe(b("pM", 0, 224), [(b("ID"), b("MSK"))], True, False)
-            cp(b("KG", 0, 512), by(b("KT", 0, top), h[0][2]))
-            act(b("KG", 512, 1024), by(b("KT", 0, top), h[1][2]))
-            for i, (a, e, l) in enumerate(h):
-                act(b("QG", a, e), by(b("NB", 0, top), l))
-            for a, e, l in h:
-                scan(b("TS", a, e), b("RK", a, e), b("KG", a, e), A.add, A.max)
-            ts(b("RK1"), b("TS", 15, 1024, 16), MAGIC128, A.add, MAGIC128, A.subtract)
-            tt(b("TF"), b("TS", 15, 1024, 16), b("RK1"), A.subtract)
-            pe(b("pM", 0, 64), [(b("GJ"), b("TF"))], False, False)
-            for s in range(4):
-                pe(b("pM", 64 + 8 * s * (s + 1), 64 + 8 * (s + 1) * (s + 2)), [(b("GJ"), b("TF", 0, 16 * s + 16))], False, s == 3)
-            ts(b("LV"), by(b("LANE"), ln), 16.0, A.mult, float(4 * k + r), A.add)
+            pe(b("pM", 0, 320), [(b("ID"), b("MSK"))], True, False)
+
+            def gather(name, table, on):
+                for (a, e, l), q in zip(h, on):
+                    move(q, b(name, a, e), by(b(table, PAD, top), l))
+
+            def best():
+                for a, e, l in h:
+                    scan(b("TS", a, e), b("RK", a, e), b("KG", a, e), A.add, A.max)
+                ts(b("RK1"), b("TS", 15, 1024, 16), MAGIC128, A.add, MAGIC128, A.subtract)
+                tt(b("TF"), b("TS", 15, 1024, 16), b("RK1"), A.subtract)
+                for s in range(5):
+                    pe(b("pM", 64 * s, 64 * s + 64), [(b("GJ"), b("TF"))], False, s == 4)
+
+            def first():
+                scan(b("EWS"), b("RM", 0, 64), b("pM", 0, 64), A.mult, A.max)
+                for s in range(4):
+                    ew = b("EWS", 16 * s + 15, 16 * s + 16)
+                    ts(b("DC", 64 * s, 64 * s + 64), b("pM", 64 * s + 64, 64 * s + 128), ew, A.not_equal, ew, A.mult)
+
+            def kept():
+                scan(b("DS"), b("RD"), b("DC"), A.max, A.min)
+                tt(b("ST", 64, 68), b("DS", 63, 256, 64), b("TR"), A.max)
 
             def mine(i):
                 a, e, l = h[i]
                 pe(b("pN%d" % i), [(b("IDF"), b("QG", a, e))], True, False)
                 tt(b("MM", a, e), by(b("LV"), b("EXPL", 32 * i, 32 * i + 32)), b("QG", a, e), A.is_equal)
                 pe(b("pN%d" % i), [(b("IDB"), b("MM", a, e))], False, True)
-            mine(0)
-            scan(b("EWS"), b("RM", 0, 64), b("pM", 0, 64), A.mult, A.max)
-            for s in range(4):
-                ew = b("EWS", 16 * s + 15, 16 * s + 16)
-                ts(b("DC", 8 * s * (s + 1), 8 * (s + 1) * (s + 2)), b("pM", 64 + 8 * s * (s + 1), 64 + 8 * (s + 1) * (s + 2)), ew, A.not_equal, ew, A.mult)
-            mine(1)
-            ts(b("CV"), b("XL4"), 0.5, A.is_le, float(V), A.mult)
-            tt(b("OC", 0, 160), b("QM2"), b("CV"), A.max)
-            scan(b("NS", 0, 512), b("RN", 0, 512), b("pN0"), A.max, A.min)
-            scan(b("DS"), b("RD"), b("DC"), A.max, A.min)
-            ts(b("OCC"), by(b("OC"), ln), float(V), A.min)
-            scan(b("NS", 512, 1024), b("RN", 512, 1024), b("pN1"), A.max, A.min)
-            for s in range(4):
-                j = 8 * (s + 1) * (s + 2)
-                ts(b("ST", 64 + s, 65 + s), b("DS", j - 1, j), b("TR", s, s + 1), A.max)
-            tt(b("ST", 0, 64), b("NS", 15, 1024, 16), b("OCC"), A.min)
+
+            def least(i):
+                scan(b("NS", 512 * i, 512 * i + 512), b("RN", 0, 512), b("pN%d" % i), A.max, A.min)
+
+            def pivots():
+                act(b("LV"), by(b("LANE"), ln), scale=16.0, bias=float(4 * k + r))
+                act(b("OCC"), by(b("OC"), ln))
+            if t < 4:
+                gather("KG", "KT", "vs")
+                pivots()
+                gather("QG", "NB", "ss")
+                best()
+                mine(0)
+                first()
+                mine(1)
+                kept()
+                least(0)
+                least(1)
+                tt(b("ST", 0, 64), b("NS", 15, 1024, 16), b("OCC"), A.min)
+                ts(cu(t, r, 0, 68), b("ST", 0, 68), float(V), A.min)
+                send(2, t, cu(t, r, 0, 68))
+            else:
+                pivots()
+                gather("QG", "NB", "vs")
+                gather("KG", "KT", "ss")
+                mine(0)
+                mine(1)
+                least(0)
+                least(1)
+                tt(b("ST", 0, 64), b("NS", 15, 1024, 16), b("OCC"), A.min)
+                ts(cu(t, r, 0, 64), b("ST", 0, 64), float(V), A.min)
+                send(2, t, cu(t, r, 0, 64))
+                best()
+                first()
+                kept()
+                cp(cu(t, r, 64, 68), b("ST", 64, 68))
+                send(3, t, cu(t, r, 64, 68))
             if t > 1:
                 for j in range(4 * (t - 1)):
-                    act(b("MB", SM * j, SM * j + 160), by(b("KT", 0, top), b("JL", 20 * j, 20 * j + 10)))
-        cp(cu(t, r, 0, 68), b("ST", 0, 68))
-        send(2, t, cu(t, r, 0, 68))
+                    act(b("MB", SM * j, SM * j + 160), by(b("KT", PAD, top), b("JL", 20 * j, 20 * j + 10)))
         if t == 0:
-            expand(1, range(8, 16))
+            expand(1, range(6, 16))
+            places(1)
             names(2)
-            iota(b("KT", NAT, B0), [[1, B0 - NAT]], 0, 0)
+            names(3)
             ts(b("DEAD"), b("YY"), -0.5, A.is_lt, -16.0, A.mult)
             ts(b("LIVE"), b("YY"), -0.5, A.is_ge)
-            places(1)
-            later_constants()
-            masks()
+            for j in (1, 2, 3):
+                own(j)
+            for j in (2, 3, 4):
+                places(j)
         if t < 4:
+            k1 = (t + 1) % 4
             ts(b("TM"), b("RR", 159, 160), 65.0, A.add, 64.0, A.min)
             pe(b("pC", 200, 201), [(b("O16"), b("TM"))])
-            if t:
-                places(t + 1)
-            for a, e, q in LISTS:
-                move(q, b("GM", 16 * a, 16 * e), by(b("MB", 0, SM * 4 * (t + 1)), b("QP", a, e)))
-            for a, e, q in LISTS:
-                lists(b("pL", a, e), "GM", 16 * a, 16 * e)
         if t == 4:
             tt(b("CV"), b("CV"), b("LIVE"), A.mult)
-            pe(b("pL", 0, 160), [(b("JM", 128 * c, 128 * c + 128), b("MB", SM * c, SM * c + 160)) for c in range(16)])
         if t:
-            x = b("NB", NAT + 4 * k + r, NAT + V, 16)
+            x = b("NB", NAT + 4 * k + r, PAD, 16)
             tt(x, x, b("CV"), A.max)
-        lists(b("pK", 256, 336), "MB", SM * 4 * t, SM * 4 * (t + 1))
         if t < 4:
             cp(b("AI"), b("pC", 200, 201))
             ts(b("AJ"), b("AI"), 7, A.bitwise_and)
             tt(b("THR"), b("LIMF"), b("AJ"), A.add)
-            if t < 3:
-                own(t + 1)
-            k1 = (t + 1) % 4
-            cp(b("QL"), b("pL", 0, 160))
-            ts(b("ELB"), b("pL", 0, 160), 128.0, A.mult, 8192.0, A.max)
-            tt(b("QX"), b("pL", 0, 160), qf(k1, "QN"), A.max)
-            tt(b("QM2"), b("pL", 0, 160), qf(k1, "QM"), A.max)
-            cp(b("QL4", 0, 160), b("pL", 0, 160))
-        else:
-            tt(b("OL4"), b("pL", 0, 160), b("UU"), A.max)
-            cp(b("OL"), b("OL4"))
+        lists(b("pK", 256, 336), "MB", SM * 4 * t, SM * 4 * (t + 1))
+        if t < 4:
+            for a, e, q in LISTS:
+                move(q, b("GM", 16 * a, 16 * e), by(b("MB", 0, SM * 4 * (t + 1)), qf(k1, "QP", a, e)))
+                lists(b("pL", a, e), "GM", 16 * a, 16 * e)
         tt(b("LO4"), b("pK", 256, 336), b("CC"), A.max)
         cp(b("LO"), b("LO4"))
-        if t < 4:
-            ts(b("CC"), b("CC"), 4.0 if t < 3 else -12.0, A.add)
         for q in range(N):
             act(blk("XB", t, q), mb(t, q, 176, 240))
         outputs("YX", "XB", t)
         if t < 4:
             act(blk("XB", t, 0, 4), blk("XB", t, 0, 4), scale=-TINY)
+            act(b("CC"), b("CC"), bias=4.0 if t < 3 else -12.0)
+        else:
+            pe(b("pL", 0, 160), [(b("JM", 128 * c, 128 * c + 128), b("MB", SM * c, SM * c + 160)) for c in range(16)])
+            tt(b("OL4"), b("pL", 0, 160), b("UU"), A.max)
+            cp(b("OL"), b("OL4"))
     dma("y", "d_yx", [lambda: g.sync.dma_start(T.yx[:], T.YX[:])], b("YX")[1], ())
-    keys(4)
     for q in ORDER:
         cp(blk("NB", 4, q), cu(4, q, 0, 64))
-    outputs("YN", "NB", 4)
+    outputs("YN", "NB", 4, "svsv")
     dma("y", "d_yn", [lambda: g.sync.dma_start(T.yn[:], T.YN[:])], b("YN")[1], ())
+    keys(4)
     for q in (3, 2, 1, 0):
         claims("KT", 4, q, blk("KT", 4, q))
-    cp(b("YJ", 0, 1536), by(b("KT", 0, B0 + 1024), b("OL", 0, 96)))
-    act(b("YJ", 1536, V), by(b("KT", 0, B0 + 1024), b("OL", 96, 160)))
+    cp(b("YJ", 0, 1280), by(b("KT", 0, B0 + 1024), b("OL", 0, 80)))
+    act(b("YJ", 1280, V), by(b("KT", 0, B0 + 1024), b("OL", 80, 160)))
     dma("s", "d_yj", [lambda i=i: g.scalar.dma_start(T.yj[i:i + 1, :], T.YJ[16 * i + 6:16 * i + 7, :]) for i in range(8)], b("YJ")[1], ())
     finish([("lo", nsend[0])])

@@ -6,32 +6,37 @@ F = ActivationFunctionType
 V, N, R = 2560, 4, 5
 NAT, PAD, DUMP, B0 = 16, 2576, 2592, 2688
 TW = B0 + 64 * N * R
-SM, SC = 320, 72
+SM, SC = 256, 136
+LS = SM // 16
 MAGIC = 1.5 * 2.0 ** 23
 MAGIC128 = 1.5 * 2.0 ** 30
 TINY = 2.0 ** -14
 COVER = ((0, 64), (64, 128), (128, 160))
-SIZES = (((0, 64, "s"),), ((64, 128, "s"),), ((128, 160, "v"),))
-LISTS = ((0, 80, "s"), (80, 160, "v"))
+SIZES = (((0, 64, "s"),), ((64, 128, "s"),), ((128, 160, "s"),))
+LISTS = ((0, 64, "s"), (128, 160, "s"), (64, 128, "v"))
+LORD = (0, 2, 1)
+PLAN = "f3 l0 f2 q0 s0 f1 l2 f0 q2 s2 o c0 x3 l1 x2 q1 s1 x1 p0 x0 g0 y c1 k3 jl k2 m0 p1 g1 c2 u2 w2 p2 g2 cv k1 m1 m2"
+KD = (0,)
+ZV = (2,)
 SIZES0 = ((0, 20, "s"), (20, 40, "v"), (40, 60, "s"), (60, 80, "v"), (80, 100, "s"), (100, 120, "v"), (120, 140, "s"), (140, 160, "v"))
 
 SCRATCH = {}
 for _d, _spec in (
-    ("float32", "NB:%d KT:%d YN:2560 YJ:2560 QEA:2560 QEB:2560 QF:640 QN:640 QM:704 QL4:176 QX:160 XL4:160 CV:160 QM2:160 OC:176 D1:176 "
-     "LANE:176 ACC:4 LV:64 OCC:64 KG:1024 QG:1024 TS:1024 NS:1024 RK1:64 EWS:64 DC:256 DS:256 ST:72 TR:4 CC:80 LO4:80 UU:160 OL4:160 "
-     "LIMF:1 THR:1 TC:48 IDF:128 NE:640 QA:640 QB:640 SCR:160" % (TW, TW)),
-    ("bfloat16", "XB:%d MB:%d YX:2560 EQ:2560 XG:2560 MXS:2560 GM:2560 RM:2560 RK:1024 RN:1024 RD:256 MM:1024 JM:2048 ELB:160 OK:160 "
+    ("float32", "NB:%d KT:%d VR:%d YN:2560 YJ:2560 QEA:2560 QEB:2560 QF:640 QN:640 QM:640 QW:640 QL4:176 QX:160 XL4:160 CV:160 QM2:160 OC:176 D1:176 "
+     "LANE:176 ACC:4 LV:64 OCC:64 KG:1024 QG:1024 TS:1024 NS:1024 RK1:64 EWS:64 DC:256 DS:256 ST:72 TR:4 TR8:4 CC:64 LO4:64 UU:160 OL4:160 "
+     "LIMF:1 THR:1 TC:48 NE:160 QA:640 QB:160 VN:640 SCR:160 QLA:160 XT:160" % (TW, TW, TW)),
+    ("bfloat16", "XB:%d XO:%d MB:%d YX:2560 EQ:2560 XG:2560 MXS:2560 GM:2560 RM:1024 RK:512 RN:512 RD:256 MM:1024 JM:2048 ELB:160 OK:160 "
      "HH:160 RR:160 YY:160 ZERO:160 DEAD:160 LIVE:160 TF:64 TM:1 ONES:128 O16:128 ID:128 G1:128 GG:128 GW:128 IDN:128 IDX:128 IDB:128 GJ:128 "
-     "W1:128 W2:128 CST:256 MSK:320 MK1:320 SG:640" % (TW, SM * N * R)),
+     "W1:128 LB:1024 CST:256 MSK:320 MK1:320 SG:640 IDC:128 RST:512 UN:512" % (TW, TW, SM * N * R)),
     ("int32", "LIMI:1 AI:1 AJ:1 QI:640 QI2:640 TCI:2 EXPI:64"),
-    ("uint16", "CU:%d QL:160 XL:160 QP:640 LN:4 QC:64 EXPL:64 JL:240 LO:80 OL:160" % (SC * N * R)),
+    ("uint16", "CU:%d QL:160 XL:160 QP:640 LN:4 QC:64 EXPL:64 JL:192 LO:64 OL:160" % (SC * N * R)),
 ):
     for _e in _spec.split():
         SCRATCH[_e.split(":")[0]] = ("sbuf", [128, int(_e.split(":")[1])], _d)
 for _e in "pZ pD pC pL pN0 pN1 pM pK".split():
     SCRATCH[_e] = ("psum", [128, 512], "float32")
 SEMAPHORES = ["v", "s", "t", "p", "lo", "d_xs", "d_lim", "d_yn", "d_yx", "d_yj"] + ["d_nb%d" % j for j in range(4)] + [
-    "a%d_%d_%d" % (k, t, q) for k in (1, 2) for t in range(R) for q in range(N)] + ["a3_4_%d" % q for q in range(N)]
+    "a%d_%d_%d" % (k, t, q) for k in (1, 2) for t in range(R) for q in range(N)] + ["a%d_4_%d" % (k, q) for k in (3, 4) for q in range(N)]
 
 
 def queues(g, T):
@@ -183,32 +188,34 @@ def rank_program(g, core, T, topo):
     iota(b("LANE"), [[1, 176]], 0, 0)
     iota(b("TR"), [[16, 4]], 0, 0)
     iota(b("EXPI"), [[1, 64]], 0, 0)
-    iota(b("CC"), [[1, 4], [256, 20]], NAT, 0)
+    iota(b("CC"), [[1, 4], [256, LS]], NAT - 1024, 0)
     iota(b("CST"), [[0, 4], [1, 64]], -64, 0)
     iota(b("SCR", 0, 160), [[16, 160]], NAT, 0)
     iota(b("MK1", 0, 64), [[0, 4], [1, 16]], 0, 0)
     iota(b("MK1", 64, 320), [[-16, 4], [1, 64]], 0, 0)
-    iota(b("KT", NAT, PAD), [[1, V]], 0, 0)
+    iota(b("VN"), [[4, 640]], r, 0)
+    iota(b("VR", 0, B0), [[1, B0]], -NAT, 0)
+    fill(b("ZERO"), 0.0)
     fill(b("JM"), 0.0)
-    for name, n, x, y in (("RM", V, 1.0, 0.0), ("RK", 1024, 128.0, -2.0 ** 24), ("RN", 1024, 0.0, 8192.0), ("RD", 256, 0.0, 8192.0)):
+    for name, n, x, y in (("RM", 1024, 1.0, 0.0), ("RK", 512, 128.0, -2.0 ** 24), ("RN", 512, 0.0, 8192.0), ("RD", 256, 0.0, 16384.0)):
         fill(b(name), x)
         fill(b(name, 0, n, 64 if name == "RD" else 16), y)
-    for name, x in (("XB", 0.0), ("NB", float(V))):
+    for name, x in (("XB", 0.0), ("XO", 0.0), ("NB", float(V))):
         fill(b(name, 0, NAT), x)
         fill(b(name, PAD, B0), x)
-    fill(b("KT", 0, NAT), 0.0)
-    fill(b("ZERO"), 0.0)
     fill(b("W1"), 0.0)
-    for name, x in (("D1", MAGIC), ("OC", float(V)), ("QM", float(V)), ("QL4", 0.0)):
+    fill(b("RST"), 0.0)
+    fill(b("RST", 15, 512, 16), 8192.0)
+    fill(b("ST", 68, 72), 0.0)
+    for name, x in (("D1", MAGIC), ("OC", float(V)), ("QL4", 0.0)):
         fill(b(name, 160, 176), x)
-    for t in range(R):
-        fill(mb(t, r, 160, 176), 0.0)
-        fill(mb(t, r, 304, 320), 0.0)
+    for j in range(N * R):
+        act(b("MB", SM * j + 224, SM * j + SM), b("ZERO", 0, 32))
     ts(b("TCI", 1, 2), b("TCI", 0, 1), 15, A.bitwise_and)
     pm = col(0)
     cp(pm, b("TCI", 1, 2))
-    e0, e1, e4, e5, e6 = col(1), col(2), col(3), col(4), col(5)
-    for c_, j in ((e0, 0), (e1, 1), (e4, 4), (e5, 5), (e6, 6)):
+    e0, e1, e4, e5 = col(1), col(2), col(3), col(4)
+    for c_, j in ((e0, 0), (e1, 1), (e4, 4), (e5, 5)):
         ts(c_, pm, float(j), A.is_equal)
     ts(col(7), e1, 64.0, A.mult, e0, A.add)
     ts(col(17), e5, 64.0, A.mult, e4, A.add)
@@ -220,12 +227,12 @@ def rank_program(g, core, T, topo):
     for t in range(R):
         ts(col(12 + t), e1, -float(B0 // 64 + 1 + 4 * t + r), A.mult, e0, A.add)
     ts(b("TC", 8, 12), b("TR"), -64.5, A.add)
+    ts(b("TR8"), b("TR"), 8192.0, A.add)
     cp(b("EXPL"), b("EXPI"))
     ts(b("GJ"), b("GG"), col(17), A.mult)
     for j in (4, 5):
-        ts(b("W1", j, 128, 16), b("GG", j, 128, 16), 2048.0, A.mult)
-    ts(b("W2"), b("ID"), e6, A.mult, 16.0, A.mult)
-    for name, x in (("IDN", -8192.0), ("IDX", -1.0 / TINY), ("IDB", 4096.0), ("IDF", 1.0)):
+        ts(b("W1", j, 128, 16), b("GG", j, 128, 16), -2048.0, A.mult)
+    for name, x in (("IDN", -8192.0), ("IDX", -1.0 / TINY), ("IDB", 4096.0), ("IDC", -4096.0)):
         ts(b(name), b("ID"), x, A.mult)
     ts(b("O16"), b("ONES"), 1.0 / 16.0, A.mult)
     tt(col(18), e0, e4, A.add)
@@ -233,47 +240,47 @@ def rank_program(g, core, T, topo):
     tt(col(20), e1, e5, A.add)
     tt(col(37), e4, e5, A.add)
     ts(col(36), pm, 16.0, A.mult)
-    tt(col(21), col(20), e6, A.add)
-    for t in range(R):
-        ts(col(26 + t), e6, float(4 * t % 16), A.mult)
+    ts(col(38), col(37), 4080.0 * 2048.0, A.mult)
     for q in range(N):
-        ts(col(22 + q), col(21), float(q), A.mult, col(19), A.add)
-    for t in range(R):
-        ts(col(31 + t), col(20), float(B0 // 64 + 1 + 4 * t), A.mult, col(26 + t), A.add)
+        ts(col(22 + q), col(20), float(q), A.mult, col(19), A.add)
+    for t in range(R - 1):
+        ts(col(31 + t), col(20), float(B0 // 64 + 1 + 4 * t), A.mult, col(38), A.add)
     for q in range(N):
         ts(b("CST", 64 * q, 64 * q + 64), b("CST", 64 * q, 64 * q + 64), col(18), A.mult, col(22 + q), A.add)
     ts(b("CC"), b("CC"), col(36), A.add)
     ts(b("UU"), b("SCR"), pm, A.add)
     ts(b("KT", PAD, B0), b("ZERO", 0, B0 - PAD), col(37), A.add, -4096.0, A.mult)
-    ts(b("MSK", 0, 64), b("MK1", 0, 64), pm, A.not_equal, -8192.0, A.mult)
-    ts(b("MSK", 64, 320), b("MK1", 64, 320), pm, A.is_ge, 8192.0, A.mult)
-    ts(b("MSK"), b("MSK"), -float(DUMP + 32), A.add)
+    ts(b("MSK", 0, 64), b("MK1", 0, 64), pm, A.not_equal, -16384.0, A.mult)
+    ts(b("MSK", 64, 320), b("MK1", 64, 320), pm, A.is_ge, 4096.0, A.mult)
+    ts(b("MSK"), b("MSK"), 8192.0 - DUMP - 32, A.add)
     cp(b("LIMF"), b("LIMI"))
     ts(b("THR"), b("LIMF"), 0.3, A.add)
     ts(b("LIMF"), b("LIMF"), 0.3, A.add)
 
     def qf(k, name="QF", a=0, e=160):
-        w = 176 if name == "QM" else 160
-        return b(name, w * k + a, w * k + e)
+        return b(name, 160 * k + a, 160 * k + e) if name == "QP" else b(name, 4 * a + k, 4 * e, 4)
 
-    def names(k):
-        act(qf(k), b("NB", NAT + 4 * k + r, PAD, 16))
+    def quarter(name, j):
+        return b(name, 160 * j, 160 * j + 160)
 
-    def own(k):
-        act(qf(k, "QA"), b("LANE", 0, 160), scale=16.0, bias=float(4 * k + r))
-        tt(qf(k, "NE"), qf(k), qf(k, "QA"), A.is_equal)
-        act(qf(k, "QB"), qf(k, "NE"), scale=float(V))
-        tt(qf(k, "QM"), qf(k), qf(k, "QB"), A.max)
+    def names(j):
+        act(quarter("QF", j), b("NB", NAT + 640 * j + r, NAT + 640 * j + 640, 4))
+
+    def own(j):
+        tt(b("NE"), quarter("QF", j), quarter("VN", j), A.is_equal)
+        ts(b("QB"), b("NE"), float(V), A.mult)
+        tt(quarter("QM", j), quarter("QF", j), b("QB"), A.max)
+
+    def columns():
+        act(b("QN"), b("QF"), scale=1.0 / 16.0, bias=64.0)
+        cp(b("QI"), b("QF"))
+        ts(b("QI2"), b("QI"), 15, A.bitwise_and)
+        ts(b("QA"), b("QI2"), SM - 1.0 / 16.0, A.mult)
+        tt(b("QW"), b("QN"), b("QA"), A.add)
+        act(b("QN"), b("QF"), bias=float(NAT))
 
     def places(t):
-        k = t % 4
-        cp(qf(k, "QI"), qf(k))
-        act(qf(k, "QA"), qf(k), scale=1.0 / 16.0)
-        ts(qf(k, "QI2"), qf(k, "QI"), 15, A.bitwise_and)
-        ts(qf(k, "QB"), qf(k, "QI2"), SM - 1.0 / 16.0, A.mult)
-        tt(qf(k, "NE"), qf(k, "QA"), qf(k, "QB"), A.add)
-        ts(qf(k, "QP"), qf(k, "NE"), float(SM * (4 * t - 1) + 160), A.min)
-        act(qf(k, "QN"), qf(k), bias=float(NAT))
+        ts(qf(t % 4, "QP"), qf(t % 4, "QW"), float(SM * 4 * t - 32), A.min)
 
     def expand(t, js):
         for j in js:
@@ -294,10 +301,11 @@ def rank_program(g, core, T, topo):
     for t in range(R):
         for q in range(N):
             if q != r:
-                arrive("a1_%d_%d" % (t, q), neng, mb(t, q, 0, SM)[1])
+                arrive("a1_%d_%d" % (t, q), neng, mb(t, q, 0, 224)[1])
                 arrive("a2_%d_%d" % (t, q), neng, cu(t, q, 0, 68 if t < 4 else 64)[1])
                 if t == 4:
-                    arrive("a3_%d_%d" % (t, q), neng, cu(t, q, 64, 68)[1])
+                    arrive("a3_%d_%d" % (t, q), neng, cu(t, q, 64, SC)[1])
+                    arrive("a4_%d_%d" % (t, q), neng, b("LB", 256 * q, 256 * q + 256)[1])
 
     def claims(name, t, q, src):
         cp(by(b(name, DUMP, B0 + 256 * t), cu(t, q, 64, 68)), src)
@@ -305,12 +313,45 @@ def rank_program(g, core, T, topo):
     def keys(t):
         pe(b("pK", 0, 256), [(b("ID"), b("CST"))], True, False)
         for q in range(N):
-            pe(b("pK", 64 * q, 64 * q + 64), [(b("W1"), mb(t, q, 176, 240)), (b("W2"), mb(t, q, 240, 304))], False, q == N - 1)
+            pe(b("pK", 64 * q, 64 * q + 64), [(b("W1"), mb(t, q, 0, 64))], False, q == N - 1)
         act(blk("KT", t, 0, 4), b("pK", 0, 256), F.Identity, bias=col(31 + t))
 
     def outputs(out, table, t, on="ssss"):
         for q in range(N):
-            move(on[q], b(out, (4 * t + q) % 16, V, 16), by(b(table, 0, B0 + 256 * (t + 1)), b("LO", 20 * q, 20 * q + 10)))
+            move(on[q], b(out, (4 * t + q) % 16, V, 16), by(b(table, 0, B0 + 256 * (t + 1)), b("LO", LS * q + 4, LS * q + 14)))
+
+    def spots(t):
+        lists(b("pZ", 256, 256 + 4 * LS), "MB", SM * 4 * t, SM * 4 * (t + 1))
+        tt(b("LO4"), b("pZ", 256, 256 + 4 * LS), b("CC"), A.max)
+        cp(b("LO"), b("LO4"))
+
+    def slots(t, step):
+        j, k = int(step[1]), t % 4
+        a, e = COVER[j]
+        x = b(("pL", "pD", "pM")[j], a, e)
+        if step[0] == "l":
+            ts(b("QL", a, e), x, float(PAD), A.max, float(PAD), A.subtract)
+        elif step[0] == "s":
+            if j in ZV:
+                act(b("QLA", a, e), x)
+            else:
+                act(b("ELB", a, e), x, scale=128.0, bias=8192.0)
+            act(b("QL4", a, e), x, F.Relu, bias=-float(PAD))
+        else:
+            tt(b("QX", a, e), x, qf(k, "QN", a, e), A.max)
+            tt(b("QM2", a, e), x, qf(k, "QM", a, e), A.max)
+
+    def follow_list(t):
+        if t > 1:
+            ts(b("JL", 0, 4 * LS * (t - 1)), b("pK", 0, 4 * LS * (t - 1)), float(PAD), A.max, float(PAD), A.subtract)
+
+    def follow(t, js):
+        for j in js:
+            act(b("MB", SM * j + 64, SM * j + 224), by(b("KT", PAD, B0 + 256 * t), b("JL", LS * j + 4, LS * j + 14)))
+
+    def variables(js):
+        for j in js:
+            act(blk("VR", 0, j), b("LB", 256 * (j % 4) + 64 * (j // 4), 256 * (j % 4) + 64 * (j // 4) + 64), scale=16.0, bias=float(j))
 
     def again(out, table):
         for q in range(N):
@@ -325,39 +366,52 @@ def rank_program(g, core, T, topo):
             for a, e, q in SIZES0:
                 if a % 40 == 0:
                     ts(b("XL", a, a + 40), b("NB", NAT + 16 * a + r, NAT + 16 * a + 640, 16), float(NAT), A.add)
-                if a == 140:
-                    names(1)
-                    expand(1, range(6))
+                    if a < 120:
+                        names(a // 40)
                 move(q, b("XG", 16 * a, 16 * e), by(b("XB", 0, B0), b("XL", a, e)))
+                if e in (20, 60, 100):
+                    c0 = NAT + (e - 20) // 40 * 860
+                    act(b("XO", c0, min(c0 + 860, PAD)), b("XB", c0, min(c0 + 860, PAD)))
+                if e % 40 == 0 and e < 160:
+                    own(e // 40 - 1)
                 if e % 80 == 0:
                     pe(b("pD", e - 80, e), [(b("ID"), b("XG", 16 * e - 1280 + j, 16 * e, 16)) for j in range(16)])
-            names(0)
-            own(0)
+            names(3)
+            own(3)
+            act(b("OC", 0, 160), qf(0, "QM"))
+            expand(1, range(3))
         else:
             for q in ORDER:
                 cp(blk("NB", t - 1, q), cu(t - 1, q, 0, 64))
-            if t > 1:
-                for q in (3, 2, 1, 0):
-                    claims("NB", t - 1, q, cu(t - 1, q, 0, 64))
             if t < 4:
                 expand(t + 1, range(16))
-            ts(b("QL"), b("pL", 0, 160), float(PAD), A.max, float(PAD), A.subtract)
-            act(b("ELB"), b("pL", 0, 160), scale=128.0, bias=8192.0)
-            act(b("QL4", 0, 160), b("pL", 0, 160), F.Relu, bias=-float(PAD))
-            keys(t - 1)
-            outputs("YN", "NB", t - 1)
-            if t > 1:
-                lists(b("pM", 0, 80 * (t - 1)), "MB", 0, SM * 4 * (t - 1))
+            else:
+                send(4, t, b("LB", 256 * r, 256 * r + 256))
             banks = ("pZ", "pN0", "pN1")
 
             def cover(j):
                 a, e = COVER[j]
-                tt(b("EQ", 16 * a, 16 * e), by(b("NB", PAD, top), b("QL", a, e)), b(qe, 16 * a, 16 * e), A.is_equal)
-                pe(b(banks[j], a, e), [(b("ID"), b("ELB", a, e))] + [(b("IDN"), b("EQ", 16 * a + i, 16 * e, 16)) for i in range(16)])
+                tt(b("EQ", 16 * a, 16 * e), by(b("NB", PAD, top), b("QL", a, e)), b(qe, 16 * a, 16 * e), A.not_equal if j in ZV else A.is_equal)
+                if j not in ZV:
+                    pe(b(banks[j], a, e), [(b("ID"), b("ELB", a, e))] + [(b("IDN"), b("EQ", 16 * a + i, 16 * e, 16)) for i in range(16)])
+
+            def uncovered(j):
+                a, e = COVER[j]
+                scan(b("UN", 0, 16 * (e - a)), b("RN", 0, 16 * (e - a)), b("EQ", 16 * a, 16 * e), A.max, A.min)
 
             def pick(j):
                 a, e = COVER[j]
-                tt(b("XL4", a, e), b(banks[j], a, e), b("QX", a, e), A.min)
+                if j in ZV:
+                    tt(b("XL4", a, e), b("XT", a, e), b("QLA", a, e), A.max)
+                else:
+                    tt(b("XL4", a, e), b(banks[j], a, e), b("QX", a, e), A.min)
+
+            def kept_names(j):
+                a, e = COVER[j]
+                tt(b("XT", a, e), b("UN", 15, 16 * (e - a), 16), b("QX", a, e), A.mult)
+
+            def sizes(j):
+                a, e = COVER[j]
                 cp(b("XL", a, e), b("XL4", a, e))
                 for a, e, q in SIZES[j]:
                     move(q, b("XG", 16 * a, 16 * e), by(b("XB", 0, top), b("XL", a, e)))
@@ -365,62 +419,72 @@ def rank_program(g, core, T, topo):
             def sums(j):
                 a, e = COVER[j]
                 pe(b("pD", a, e), [(b("ID"), b("XG", 16 * a + i, 16 * e, 16)) for i in range(16)], True, False)
-                scan(b("MXS", 16 * a, 16 * e), b("RM", 16 * a, 16 * e), b("XG", 16 * a, 16 * e), A.mult, A.min)
+                scan(b("MXS", 16 * a, 16 * e), b("RM", 0, 16 * (e - a)), b("XG", 16 * a, 16 * e), A.mult, A.min)
                 pe(b("pD", a, e), [(b("IDX"), b("MXS", 16 * a + 15, 16 * e, 16))], False, True)
 
             def key_claims(qs):
                 if t > 1:
                     for q in qs:
                         claims("KT", t - 1, q, blk("KT", t - 1, q))
-            cover(0)
-            tt(b("QX"), b("pL", 0, 160), qf(k, "QN"), A.max)
-            if t > 1:
-                for q in (3, 2, 1, 0):
-                    claims("XB", t - 1, q, blk("XB", t - 1, q))
-            pick(0)
-            cover(1)
-            key_claims((3, 2))
-            tt(b("QM2"), b("pL", 0, 160), qf(k, "QM"), A.max)
-            pick(1)
-            cover(2)
-            if t > 1:
-                ts(b("JL", 0, 80 * (t - 1)), b("pM", 0, 80 * (t - 1)), float(PAD), A.max, float(PAD), A.subtract)
-            sums(0)
-            pick(2)
+            for step in PLAN.split():
+                j = int(step[1:]) if step[1:].isdigit() else None
+                if step[0] in "lqs":
+                    slots(t, step)
+                elif step == "o":
+                    outputs("YN", "NB", t - 1)
+                elif step == "y":
+                    outputs("YX", "XO", t - 1)
+                    act(b("CC"), b("CC"), bias=4.0 if t < 4 else -12.0)
+                elif step == "cv":
+                    act(b("XT"), b("XL4"), F.Sign, bias=0.5, scale=-1.0)
+                    act(b("CV"), b("XT"), F.Relu, scale=float(V))
+                elif step == "jl":
+                    follow_list(t)
+                elif step[0] in "xf":
+                    if t > 1:
+                        claims("XB" if step[0] == "x" else "NB", t - 1, j, blk("XB", t - 1, j) if step[0] == "x" else cu(t - 1, j, 0, 64))
+                elif step[0] == "k":
+                    key_claims((j,))
+                else:
+                    {"c": cover, "u": uncovered, "p": pick, "g": sizes, "w": kept_names, "m": sums}[step[0]](j)
             if t == 2:
                 again("YN", "NB")
             if t == 3:
-                again("YX", "XB")
-            sums(1)
-            sums(2)
-            ts(b("CV"), b("XL4"), 0.5, A.is_le, float(V), A.mult)
-            tt(b("OC", 0, 160), b("QM2"), b("CV"), A.max)
+                again("YX", "XO")
+            if t == 4:
+                variables(range(8))
         ts(b("OK"), b("pD", 0, 160), b("THR"), A.is_le)
         pe(b("pC", 0, 160), ([(b("ID"), b("DEAD"))] if t == 4 else []) + [(b("GG"), b("OK"))])
-        ts(b("D1", 0, 160), b("pD", 0, 160), 255.0, A.min, MAGIC, A.add)
+        if t:
+            pe(b("pM", 0, 320), [(b("ID"), b("MSK"))], True, False)
+            for i in range(2):
+                pe(b("pN%d" % i), [(b("ID"), b("RST"))], True, False)
+        act(b("D1", 0, 160), b("pD", 0, 160), bias=MAGIC)
+        if t:
+            tt(b("OC", 0, 160), b("QM2"), b("CV"), A.max)
         ts(b("HH"), b("pC", 0, 160), 8.5, A.is_ge)
         scan(b("RR"), b("HH"), b("ZERO"), A.add, A.min, -65.0)
         for s in range(4):
             act(b("SG", 160 * s, 160 * s + 160), b("RR"), F.Sign, bias=col(8 + s), scale=-1.0, total=b("ACC", s, s + 1))
+        if t < 4:
+            ts(b("TM"), b("RR", 159, 160), 65.0, A.add, 64.0, A.min)
+            pe(b("pC", 200, 201), [(b("O16"), b("TM"))])
         tt(b("YY"), b("HH"), b("RR"), A.mult)
-        ts(mb(t, r, 0, 160), b("YY"), col(6), A.max, col(12 + t), A.mult)
+        ts(mb(t, r, 64, 224), b("YY"), col(6), A.max, col(12 + t), A.mult)
         if t:
-            key_claims((1, 0))
+            key_claims(KD)
         ts(b("LN"), b("ACC"), 0.5, A.mult, 80.0, A.add)
         ln = b("LN")
         if t:
             cp(b("QC"), by(b("QL4"), ln))
-        act(mb(t, r, 176, 240), by(b("D1"), ln), bias=-MAGIC)
-        act(mb(t, r, 240, 304), by(b("LANE"), ln))
-        send(1, t, mb(t, r, 0, SM))
+        act(mb(t, r, 0, 64), by(b("D1"), ln), F.Relu, bias=MAGIC + 255.0, scale=-1.0)
+        send(1, t, mb(t, r, 0, 224))
         if t == 0:
-            cp(b("ST", 0, 64), by(b("QM", 0, 176), ln))
-            cp(b("ST", 64, 68), b("TR"))
-            cp(cu(t, r, 0, 68), b("ST", 0, 68))
+            cp(cu(t, r, 64, 68), b("TR"))
+            cp(cu(t, r, 0, 64), by(b("OC"), ln))
             send(2, t, cu(t, r, 0, 68))
         else:
             h = [(512 * i, 512 * i + 512, b("QC", 32 * i, 32 * i + 32)) for i in range(2)]
-            pe(b("pM", 0, 320), [(b("ID"), b("MSK"))], True, False)
 
             def gather(name, table, on):
                 for (a, e, l), q in zip(h, on):
@@ -428,7 +492,7 @@ def rank_program(g, core, T, topo):
 
             def best():
                 for a, e, l in h:
-                    scan(b("TS", a, e), b("RK", a, e), b("KG", a, e), A.add, A.max)
+                    scan(b("TS", a, e), b("RK"), b("KG", a, e), A.add, A.max)
                 ts(b("RK1"), b("TS", 15, 1024, 16), MAGIC128, A.add, MAGIC128, A.subtract)
                 tt(b("TF"), b("TS", 15, 1024, 16), b("RK1"), A.subtract)
                 for s in range(5):
@@ -442,20 +506,21 @@ def rank_program(g, core, T, topo):
 
             def kept():
                 scan(b("DS"), b("RD"), b("DC"), A.max, A.min)
-                tt(b("ST", 64, 68), b("DS", 63, 256, 64), b("TR"), A.max)
+                tt(b("ST", 64, 68), b("DS", 63, 256, 64), b("TR8"), A.max)
 
             def mine(i):
                 a, e, l = h[i]
-                pe(b("pN%d" % i), [(b("IDF"), b("QG", a, e))], True, False)
                 tt(b("MM", a, e), by(b("LV"), b("EXPL", 32 * i, 32 * i + 32)), b("QG", a, e), A.is_equal)
-                pe(b("pN%d" % i), [(b("IDB"), b("MM", a, e))], False, True)
+                pe(b("pN%d" % i), [(b("IDB"), b("MM", a, e))], False, False)
+                pe(b("pN%d" % i, 0, 511), [(b("IDC"), b("MM", a + 1, e))], False, False)
+                pe(b("pN%d" % i, 15, 511, 16), [(b("IDB"), b("MM", a + 16, e, 16))], False, True)
 
             def least(i):
-                scan(b("NS", 512 * i, 512 * i + 512), b("RN", 0, 512), b("pN%d" % i), A.max, A.min)
+                scan(b("NS", 512 * i, 512 * i + 512), b("QG", 512 * i, 512 * i + 512), b("pN%d" % i), A.min, A.add, 8192.0)
 
             def pivots():
                 act(b("LV"), by(b("LANE"), ln), scale=16.0, bias=float(4 * k + r))
-                act(b("OCC"), by(b("OC"), ln))
+                act(b("OCC"), by(b("OC"), ln), bias=8192.0)
             if t < 4:
                 gather("KG", "KT", "vs")
                 pivots()
@@ -468,7 +533,7 @@ def rank_program(g, core, T, topo):
                 least(0)
                 least(1)
                 tt(b("ST", 0, 64), b("NS", 15, 1024, 16), b("OCC"), A.min)
-                ts(cu(t, r, 0, 68), b("ST", 0, 68), float(V), A.min)
+                ts(cu(t, r, 0, 68), b("ST", 0, 68), 8192.0, A.subtract, float(V), A.min)
                 send(2, t, cu(t, r, 0, 68))
             else:
                 pivots()
@@ -476,34 +541,34 @@ def rank_program(g, core, T, topo):
                 gather("KG", "KT", "ss")
                 mine(0)
                 mine(1)
+                follow(t, range(12))
                 least(0)
                 least(1)
                 tt(b("ST", 0, 64), b("NS", 15, 1024, 16), b("OCC"), A.min)
-                ts(cu(t, r, 0, 64), b("ST", 0, 64), float(V), A.min)
+                ts(cu(t, r, 0, 64), b("ST", 0, 64), 8192.0, A.subtract, float(V), A.min)
                 send(2, t, cu(t, r, 0, 64))
                 best()
                 first()
+                spots(t)
                 kept()
-                cp(cu(t, r, 64, 68), b("ST", 64, 68))
-                send(3, t, cu(t, r, 64, 68))
-            if t > 1:
-                for j in range(4 * (t - 1)):
-                    act(b("MB", SM * j, SM * j + 160), by(b("KT", PAD, top), b("JL", 20 * j, 20 * j + 10)))
+                ts(cu(t, r, 64, 72), b("ST", 64, 72), 8192.0, A.subtract)
+                cp(cu(t, r, 72, SC), by(b("LANE"), ln))
+                send(3, t, cu(t, r, 64, SC))
+            if t < 4:
+                follow(t, range(4 * (t - 1)))
+            else:
+                pe(b("pL", 0, 160), [(b("JM", 128 * c, 128 * c + 128), b("MB", SM * c + 64, SM * c + 224)) for c in range(16)])
+        if t < 4:
+            act(b("LB", 256 * r + 64 * t, 256 * r + 64 * t + 64), by(b("LANE"), ln))
         if t == 0:
-            expand(1, range(6, 16))
+            expand(1, range(3, 16))
+            columns()
             places(1)
-            names(2)
-            names(3)
             ts(b("DEAD"), b("YY"), -0.5, A.is_lt, -16.0, A.mult)
             ts(b("LIVE"), b("YY"), -0.5, A.is_ge)
-            for j in (1, 2, 3):
-                own(j)
             for j in (2, 3, 4):
                 places(j)
-        if t < 4:
-            k1 = (t + 1) % 4
-            ts(b("TM"), b("RR", 159, 160), 65.0, A.add, 64.0, A.min)
-            pe(b("pC", 200, 201), [(b("O16"), b("TM"))])
+        k1 = (t + 1) % 4
         if t == 4:
             tt(b("CV"), b("CV"), b("LIVE"), A.mult)
         if t:
@@ -513,32 +578,39 @@ def rank_program(g, core, T, topo):
             cp(b("AI"), b("pC", 200, 201))
             ts(b("AJ"), b("AI"), 7, A.bitwise_and)
             tt(b("THR"), b("LIMF"), b("AJ"), A.add)
-        lists(b("pK", 256, 336), "MB", SM * 4 * t, SM * 4 * (t + 1))
-        if t < 4:
-            for a, e, q in LISTS:
-                move(q, b("GM", 16 * a, 16 * e), by(b("MB", 0, SM * 4 * (t + 1)), qf(k1, "QP", a, e)))
-                lists(b("pL", a, e), "GM", 16 * a, 16 * e)
-        tt(b("LO4"), b("pK", 256, 336), b("CC"), A.max)
-        cp(b("LO"), b("LO4"))
+
+            def gather_map(on):
+                for a, e, q in LISTS:
+                    if q == on:
+                        move(q, b("GM", 16 * a, 16 * e), by(b("MB", 0, SM * 4 * (t + 1)), qf(k1, "QP", a, e)))
+            gather_map("s")
+            for q in range(N):
+                act(blk("XB", t, q), mb(t, q, 0, 64), scale=TINY, bias=-255.0 * TINY)
+            spots(t)
+            keys(t)
+            gather_map("v")
+            for j in LORD:
+                a, e = COVER[j]
+                lists(b(("pL", "pD", "pM")[j], a, e), "GM", 16 * a, 16 * e)
+            if t:
+                lists(b("pK", 0, 4 * LS * t), "MB", 0, SM * 4 * t)
         for q in range(N):
-            act(blk("XB", t, q), mb(t, q, 176, 240))
-        outputs("YX", "XB", t)
-        if t < 4:
-            act(blk("XB", t, 0, 4), blk("XB", t, 0, 4), scale=-TINY)
-            act(b("CC"), b("CC"), bias=4.0 if t < 3 else -12.0)
-        else:
-            pe(b("pL", 0, 160), [(b("JM", 128 * c, 128 * c + 128), b("MB", SM * c, SM * c + 160)) for c in range(16)])
-            tt(b("OL4"), b("pL", 0, 160), b("UU"), A.max)
-            cp(b("OL"), b("OL4"))
+            act(blk("XO", t, q), mb(t, q, 0, 64), scale=-1.0, bias=255.0)
+        if t == 4:
+            outputs("YX", "XO", t)
     dma("y", "d_yx", [lambda: g.sync.dma_start(T.yx[:], T.YX[:])], b("YX")[1], ())
     for q in ORDER:
         cp(blk("NB", 4, q), cu(4, q, 0, 64))
     outputs("YN", "NB", 4, "svsv")
     dma("y", "d_yn", [lambda: g.sync.dma_start(T.yn[:], T.YN[:])], b("YN")[1], ())
-    keys(4)
+    variables(range(8, 16))
+    tt(b("OL4"), b("pL", 0, 160), b("UU"), A.max)
+    cp(b("OL"), b("OL4"))
     for q in (3, 2, 1, 0):
-        claims("KT", 4, q, blk("KT", 4, q))
-    cp(b("YJ", 0, 1280), by(b("KT", 0, B0 + 1024), b("OL", 0, 80)))
-    act(b("YJ", 1280, V), by(b("KT", 0, B0 + 1024), b("OL", 80, 160)))
-    dma("s", "d_yj", [lambda i=i: g.scalar.dma_start(T.yj[i:i + 1, :], T.YJ[16 * i + 6:16 * i + 7, :]) for i in range(8)], b("YJ")[1], ())
+        ts(blk("VR", 4, q), cu(4, q, 72, SC), 16.0, A.mult, float(q), A.add)
+    for q in (3, 2, 1, 0):
+        claims("VR", 4, q, blk("VR", 4, q))
+    cp(b("YJ", 0, 1280), by(b("VR", 0, B0 + 1024), b("OL", 0, 80)))
+    act(b("YJ", 1280, V), by(b("VR", 0, B0 + 1024), b("OL", 80, 160)))
+    dma("s", "d_yj", [lambda: g.scalar.dma_start(T.yj[:], T.YJ[0:128:16, :])], b("YJ")[1], ())
     finish([("lo", nsend[0])])

@@ -15,16 +15,15 @@ COVER = ((0, 64), (64, 128), (128, 160))
 SIZES = (((0, 64, "s"),), ((64, 128, "s"),), ((128, 160, "s"),))
 LISTS = ((0, 64, "s"), (128, 160, "s"), (64, 128, "v"))
 LORD = (0, 2, 1)
-PLAN = "f3 l0 f2 q0 s0 f1 l2 f0 q2 s2 o c0 x3 l1 x2 q1 s1 x1 p0 x0 g0 y c1 k3 jl k2 m0 p1 g1 c2 u2 w2 p2 g2 cv k1 m1 m2"
+PLAN = "f3 l0 f2 q0 s0 f1 l2 f0 q2 s2 o c0 x3 l1 x2 q1 s1 x1 p0 x0 g0 y c1 c2 jl u2 p1 w2 g1 p2 k3 g2 cv m0 k2 k1 m1 m2"
 KD = (0,)
 ZV = (2,)
-SIZES0 = ((0, 20, "s"), (20, 40, "v"), (40, 60, "s"), (60, 80, "v"), (80, 100, "s"), (100, 120, "v"), (120, 140, "s"), (140, 160, "v"))
 
 SCRATCH = {}
 for _d, _spec in (
-    ("float32", "NB:%d KT:%d VR:%d YN:2560 YJ:2560 QEA:2560 QEB:2560 QF:640 QN:640 QM:640 QW:640 QL4:176 QX:160 XL4:160 CV:160 QM2:160 OC:176 D1:176 "
-     "LANE:176 ACC:4 LV:64 OCC:64 KG:1024 QG:1024 TS:1024 NS:1024 RK1:64 EWS:64 DC:256 DS:256 ST:72 TR:4 TR8:4 CC:64 LO4:64 UU:160 OL4:160 "
-     "LIMF:1 THR:1 TC:48 NE:160 QA:640 QB:160 VN:640 SCR:160 QLA:160 XT:160" % (TW, TW, TW)),
+    ("float32", "NB:%d KT:%d VR:%d YN:2560 YJ:2560 QEA:2560 QEB:2560 QF:640 QN:640 QM:640 QW:640 QL4:176 QX:160 XL4:160 CV:160 QM2:160 OC:176 "
+     "D1:176 LANE:176 ACC:4 LV:64 OCC:64 KG:1024 QG:1024 TS:1024 NS:1024 RK1:64 EWS:64 DC:256 DS:256 ST:72 TR:4 TR8:4 CC:64 LO4:64 UU:160 "
+     "OL4:160 LIMF:1 THR:1 TC:48 NE:160 QA:640 QB:160 VN:640 SCR:160 QLA:160 XT:160" % (TW, TW, TW)),
     ("bfloat16", "XB:%d XO:%d MB:%d YX:2560 EQ:2560 XG:2560 MXS:2560 GM:2560 RM:1024 RK:512 RN:512 RD:256 MM:1024 JM:2048 ELB:160 OK:160 "
      "HH:160 RR:160 YY:160 ZERO:160 DEAD:160 LIVE:160 TF:64 TM:1 ONES:128 O16:128 ID:128 G1:128 GG:128 GW:128 IDN:128 IDX:128 IDB:128 GJ:128 "
      "W1:128 LB:1024 CST:256 MSK:320 MK1:320 SG:640 IDC:128 RST:512 UN:512" % (TW, TW, SM * N * R)),
@@ -185,77 +184,79 @@ def rank_program(g, core, T, topo):
     select(b("ID"), b("ONES"), [[-1, 128]], A.is_equal, 0.0, 0, 1)
     select(b("G1"), b("ONES"), [[-16, 8], [0, 16]], A.is_ge, 0.0, 0, 1)
     select(b("GG"), b("G1"), [[16, 8], [0, 16]], A.is_ge, 0.0, 15, -1)
-    iota(b("LANE"), [[1, 176]], 0, 0)
     iota(b("TR"), [[16, 4]], 0, 0)
-    iota(b("EXPI"), [[1, 64]], 0, 0)
     iota(b("CC"), [[1, 4], [256, LS]], NAT - 1024, 0)
     iota(b("CST"), [[0, 4], [1, 64]], -64, 0)
+    iota(b("EXPI"), [[1, 64]], 0, 0)
     iota(b("SCR", 0, 160), [[16, 160]], NAT, 0)
+    iota(b("VN"), [[4, 640]], r, 0)
+    iota(b("LANE"), [[1, 176]], 0, 0)
     iota(b("MK1", 0, 64), [[0, 4], [1, 16]], 0, 0)
     iota(b("MK1", 64, 320), [[-16, 4], [1, 64]], 0, 0)
-    iota(b("VN"), [[4, 640]], r, 0)
-    iota(b("VR", 0, B0), [[1, B0]], -NAT, 0)
+    for name, n, x in (("RK", 512, 128), ("RN", 512, 0), ("RST", 512, 0), ("RD", 256, 0)):
+        iota(b(name), [[0, n]], x, 0)
     fill(b("ZERO"), 0.0)
+    ts(b("TCI", 1, 2), b("TCI", 0, 1), 15, A.bitwise_and)
     fill(b("JM"), 0.0)
-    for name, n, x, y in (("RM", 1024, 1.0, 0.0), ("RK", 512, 128.0, -2.0 ** 24), ("RN", 512, 0.0, 8192.0), ("RD", 256, 0.0, 16384.0)):
-        fill(b(name), x)
-        fill(b(name, 0, n, 64 if name == "RD" else 16), y)
+    pm = col(0)
+    cp(pm, b("TCI", 1, 2))
     for name, x in (("XB", 0.0), ("XO", 0.0), ("NB", float(V))):
         fill(b(name, 0, NAT), x)
         fill(b(name, PAD, B0), x)
-    fill(b("W1"), 0.0)
-    fill(b("RST"), 0.0)
-    fill(b("RST", 15, 512, 16), 8192.0)
-    fill(b("ST", 68, 72), 0.0)
-    for name, x in (("D1", MAGIC), ("OC", float(V)), ("QL4", 0.0)):
-        fill(b(name, 160, 176), x)
-    for j in range(N * R):
-        act(b("MB", SM * j + 224, SM * j + SM), b("ZERO", 0, 32))
-    ts(b("TCI", 1, 2), b("TCI", 0, 1), 15, A.bitwise_and)
-    pm = col(0)
-    cp(pm, b("TCI", 1, 2))
     e0, e1, e4, e5 = col(1), col(2), col(3), col(4)
     for c_, j in ((e0, 0), (e1, 1), (e4, 4), (e5, 5)):
         ts(c_, pm, float(j), A.is_equal)
+    cp(b("LIMF"), b("LIMI"))
+    for name, x in (("D1", MAGIC), ("OC", float(V)), ("QL4", 0.0)):
+        fill(b(name, 160, 176), x)
+    ts(b("THR"), b("LIMF"), 0.3, A.add)
+    for j in range(N * R):
+        act(b("MB", SM * j + 224, SM * j + SM), b("ZERO", 0, 32))
     ts(col(7), e1, 64.0, A.mult, e0, A.add)
     ts(col(17), e5, 64.0, A.mult, e4, A.add)
+    ts(b("LIMF"), b("LIMF"), 0.3, A.add)
+    ts(col(6), e0, -63.0, A.mult, -1.0, A.add)
     ts(b("GW"), b("GG"), col(7), A.mult)
     for m in range(16):
         act(b("JM", 128 * m + m, 128 * m + 128, 16), b("GW", m, 128, 16))
     ts(b("TR"), b("TR"), pm, A.add)
-    ts(col(6), e0, -63.0, A.mult, -1.0, A.add)
     for t in range(R):
         ts(col(12 + t), e1, -float(B0 // 64 + 1 + 4 * t + r), A.mult, e0, A.add)
     ts(b("TC", 8, 12), b("TR"), -64.5, A.add)
-    ts(b("TR8"), b("TR"), 8192.0, A.add)
-    cp(b("EXPL"), b("EXPI"))
-    ts(b("GJ"), b("GG"), col(17), A.mult)
-    for j in (4, 5):
-        ts(b("W1", j, 128, 16), b("GG", j, 128, 16), -2048.0, A.mult)
-    for name, x in (("IDN", -8192.0), ("IDX", -1.0 / TINY), ("IDB", 4096.0), ("IDC", -4096.0)):
-        ts(b(name), b("ID"), x, A.mult)
     ts(b("O16"), b("ONES"), 1.0 / 16.0, A.mult)
+    fill(b("W1"), 0.0)
+    fill(b("RM"), 1.0)
     tt(col(18), e0, e4, A.add)
     ts(col(19), e4, 32.0, A.mult)
     tt(col(20), e1, e5, A.add)
     tt(col(37), e4, e5, A.add)
     ts(col(36), pm, 16.0, A.mult)
+    for j in (4, 5):
+        ts(b("W1", j, 128, 16), b("GG", j, 128, 16), -2048.0, A.mult)
     ts(col(38), col(37), 4080.0 * 2048.0, A.mult)
     for q in range(N):
         ts(col(22 + q), col(20), float(q), A.mult, col(19), A.add)
+    ts(b("CC"), b("CC"), col(36), A.add)
     for t in range(R - 1):
         ts(col(31 + t), col(20), float(B0 // 64 + 1 + 4 * t), A.mult, col(38), A.add)
     for q in range(N):
         ts(b("CST", 64 * q, 64 * q + 64), b("CST", 64 * q, 64 * q + 64), col(18), A.mult, col(22 + q), A.add)
-    ts(b("CC"), b("CC"), col(36), A.add)
-    ts(b("UU"), b("SCR"), pm, A.add)
     ts(b("KT", PAD, B0), b("ZERO", 0, B0 - PAD), col(37), A.add, -4096.0, A.mult)
-    ts(b("MSK", 0, 64), b("MK1", 0, 64), pm, A.not_equal, -16384.0, A.mult)
-    ts(b("MSK", 64, 320), b("MK1", 64, 320), pm, A.is_ge, 4096.0, A.mult)
-    ts(b("MSK"), b("MSK"), 8192.0 - DUMP - 32, A.add)
-    cp(b("LIMF"), b("LIMI"))
-    ts(b("THR"), b("LIMF"), 0.3, A.add)
-    ts(b("LIMF"), b("LIMF"), 0.3, A.add)
+    for name, x in (("IDN", -8192.0), ("IDX", -1.0 / TINY), ("IDB", 4096.0), ("IDC", -4096.0)):
+        act(b(name), b("ID"), scale=x)
+    ts(b("TR8"), b("TR"), 8192.0, A.add)
+    cp(b("EXPL"), b("EXPI"))
+    ts(b("GJ"), b("GG"), col(17), A.mult)
+    ts(b("UU"), b("SCR"), pm, A.add)
+    fill(b("ST", 68, 72), 0.0)
+
+    def masks():
+        ts(b("MSK", 0, 64), b("MK1", 0, 64), pm, A.not_equal, -16384.0, A.mult)
+        ts(b("MSK", 64, 320), b("MK1", 64, 320), pm, A.is_ge, 4096.0, A.mult)
+        for name, c0, n, st, y in (("RM", 0, 1024, 16, 0.0), ("RK", 0, 512, 16, -2.0 ** 24), ("RN", 0, 512, 16, 8192.0),
+                                   ("RD", 0, 256, 64, 16384.0), ("RST", 15, 512, 16, 8192.0)):
+            fill(b(name, c0, n, st), y)
+        ts(b("MSK"), b("MSK"), 8192.0 - DUMP - 32, A.add)
 
     def qf(k, name="QF", a=0, e=160):
         return b(name, 160 * k + a, 160 * k + e) if name == "QP" else b(name, 4 * a + k, 4 * e, 4)
@@ -268,6 +269,8 @@ def rank_program(g, core, T, topo):
 
     def own(j):
         tt(b("NE"), quarter("QF", j), quarter("VN", j), A.is_equal)
+
+    def but_own(j):
         ts(b("QB"), b("NE"), float(V), A.mult)
         tt(quarter("QM", j), quarter("QF", j), b("QB"), A.max)
 
@@ -302,13 +305,13 @@ def rank_program(g, core, T, topo):
         for q in range(N):
             if q != r:
                 arrive("a1_%d_%d" % (t, q), neng, mb(t, q, 0, 224)[1])
-                arrive("a2_%d_%d" % (t, q), neng, cu(t, q, 0, 68 if t < 4 else 64)[1])
+                arrive("a2_%d_%d" % (t, q), neng, cu(t, q, 0, 68 if t < 4 else 128)[1])
                 if t == 4:
-                    arrive("a3_%d_%d" % (t, q), neng, cu(t, q, 64, SC)[1])
+                    arrive("a3_%d_%d" % (t, q), neng, cu(t, q, 128, SC)[1])
                     arrive("a4_%d_%d" % (t, q), neng, b("LB", 256 * q, 256 * q + 256)[1])
 
     def claims(name, t, q, src):
-        cp(by(b(name, DUMP, B0 + 256 * t), cu(t, q, 64, 68)), src)
+        cp(by(b(name, DUMP, B0 + 256 * t), cu(t, q, 64, 68) if t < 4 else cu(t, q, 128, 132)), src)
 
     def keys(t):
         pe(b("pK", 0, 256), [(b("ID"), b("CST"))], True, False)
@@ -322,8 +325,9 @@ def rank_program(g, core, T, topo):
 
     def spots(t):
         lists(b("pZ", 256, 256 + 4 * LS), "MB", SM * 4 * t, SM * 4 * (t + 1))
+
+    def spots_or_own():
         tt(b("LO4"), b("pZ", 256, 256 + 4 * LS), b("CC"), A.max)
-        cp(b("LO"), b("LO4"))
 
     def slots(t, step):
         j, k = int(step[1]), t % 4
@@ -341,10 +345,6 @@ def rank_program(g, core, T, topo):
             tt(b("QX", a, e), x, qf(k, "QN", a, e), A.max)
             tt(b("QM2", a, e), x, qf(k, "QM", a, e), A.max)
 
-    def follow_list(t):
-        if t > 1:
-            ts(b("JL", 0, 4 * LS * (t - 1)), b("pK", 0, 4 * LS * (t - 1)), float(PAD), A.max, float(PAD), A.subtract)
-
     def follow(t, js):
         for j in js:
             act(b("MB", SM * j + 64, SM * j + 224), by(b("KT", PAD, B0 + 256 * t), b("JL", LS * j + 4, LS * j + 14)))
@@ -357,27 +357,34 @@ def rank_program(g, core, T, topo):
         for q in range(N):
             act(b(table, NAT + q, PAD, 16), b(out, q, V, 16))
 
+    def pristine(t):
+        for q in range(N):
+            act(blk("XO", t, q), mb(t, q, 0, 64), scale=-1.0, bias=255.0)
+
     ORDER = [r] + [q for q in (3, 2, 1, 0) if q != r]
     for t in range(R):
         k = t % 4
         top = B0 + 256 * t
         qe = "QEB" if t % 2 else "QEA"
         if t == 0:
-            for a, e, q in SIZES0:
-                if a % 40 == 0:
-                    ts(b("XL", a, a + 40), b("NB", NAT + 16 * a + r, NAT + 16 * a + 640, 16), float(NAT), A.add)
-                    if a < 120:
-                        names(a // 40)
-                move(q, b("XG", 16 * a, 16 * e), by(b("XB", 0, B0), b("XL", a, e)))
-                if e in (20, 60, 100):
-                    c0 = NAT + (e - 20) // 40 * 860
-                    act(b("XO", c0, min(c0 + 860, PAD)), b("XB", c0, min(c0 + 860, PAD)))
-                if e % 40 == 0 and e < 160:
-                    own(e // 40 - 1)
-                if e % 80 == 0:
-                    pe(b("pD", e - 80, e), [(b("ID"), b("XG", 16 * e - 1280 + j, 16 * e, 16)) for j in range(16)])
+            for j in range(4):
+                a = 40 * j
+                ts(b("XL", a, a + 40), b("NB", NAT + 16 * a + r, NAT + 16 * a + 640, 16), float(NAT), A.add)
+                if j < 3:
+                    names(j)
+                if j:
+                    own(j - 1)
+                act(b("XG", 16 * a, 16 * a + 320), by(b("XB", 0, B0), b("XL", a, a + 20)))
+                cp(b("XG", 16 * a + 320, 16 * a + 640), by(b("XB", 0, B0), b("XL", a + 20, a + 40)))
+                if j % 2:
+                    pe(b("pD", a - 40, a + 40), [(b("ID"), b("XG", 16 * a - 640 + i, 16 * a + 640, 16)) for i in range(16)])
+                if j < 3:
+                    act(b("XO", NAT + 860 * j, min(NAT + 860 * j + 860, PAD)), b("XB", NAT + 860 * j, min(NAT + 860 * j + 860, PAD)))
+                if j:
+                    but_own(j - 1)
             names(3)
             own(3)
+            but_own(3)
             act(b("OC", 0, 160), qf(0, "QM"))
             expand(1, range(3))
         else:
@@ -387,6 +394,7 @@ def rank_program(g, core, T, topo):
                 expand(t + 1, range(16))
             else:
                 send(4, t, b("LB", 256 * r, 256 * r + 256))
+                iota(b("VR", 0, B0), [[1, B0]], -NAT, 0)
             banks = ("pZ", "pN0", "pN1")
 
             def cover(j):
@@ -399,16 +407,16 @@ def rank_program(g, core, T, topo):
                 a, e = COVER[j]
                 scan(b("UN", 0, 16 * (e - a)), b("RN", 0, 16 * (e - a)), b("EQ", 16 * a, 16 * e), A.max, A.min)
 
+            def kept_names(j):
+                a, e = COVER[j]
+                tt(b("XT", a, e), b("UN", 15, 16 * (e - a), 16), b("QX", a, e), A.mult)
+
             def pick(j):
                 a, e = COVER[j]
                 if j in ZV:
                     tt(b("XL4", a, e), b("XT", a, e), b("QLA", a, e), A.max)
                 else:
                     tt(b("XL4", a, e), b(banks[j], a, e), b("QX", a, e), A.min)
-
-            def kept_names(j):
-                a, e = COVER[j]
-                tt(b("XT", a, e), b("UN", 15, 16 * (e - a), 16), b("QX", a, e), A.mult)
 
             def sizes(j):
                 a, e = COVER[j]
@@ -422,31 +430,30 @@ def rank_program(g, core, T, topo):
                 scan(b("MXS", 16 * a, 16 * e), b("RM", 0, 16 * (e - a)), b("XG", 16 * a, 16 * e), A.mult, A.min)
                 pe(b("pD", a, e), [(b("IDX"), b("MXS", 16 * a + 15, 16 * e, 16))], False, True)
 
-            def key_claims(qs):
+            def claimed_by(name, q):
                 if t > 1:
-                    for q in qs:
-                        claims("KT", t - 1, q, blk("KT", t - 1, q))
+                    claims(name, t - 1, q, cu(t - 1, q, 0, 64) if name == "NB" else blk(name, t - 1, q))
+
+            def last_sizes():
+                outputs("YX", "XO", t - 1)
+                act(b("CC"), b("CC"), bias=4.0 if t < 4 else -12.0)
+
+            def covered_rows():
+                act(b("XT"), b("XL4"), F.Sign, bias=0.5, scale=-1.0)
+                act(b("CV"), b("XT"), F.Relu, scale=float(V))
+
+            def roots():
+                if t > 1:
+                    ts(b("JL", 0, 4 * LS * (t - 1)), b("pK", 0, 4 * LS * (t - 1)), float(PAD), A.max, float(PAD), A.subtract)
             for step in PLAN.split():
-                j = int(step[1:]) if step[1:].isdigit() else None
                 if step[0] in "lqs":
                     slots(t, step)
-                elif step == "o":
-                    outputs("YN", "NB", t - 1)
-                elif step == "y":
-                    outputs("YX", "XO", t - 1)
-                    act(b("CC"), b("CC"), bias=4.0 if t < 4 else -12.0)
-                elif step == "cv":
-                    act(b("XT"), b("XL4"), F.Sign, bias=0.5, scale=-1.0)
-                    act(b("CV"), b("XT"), F.Relu, scale=float(V))
-                elif step == "jl":
-                    follow_list(t)
-                elif step[0] in "xf":
-                    if t > 1:
-                        claims("XB" if step[0] == "x" else "NB", t - 1, j, blk("XB", t - 1, j) if step[0] == "x" else cu(t - 1, j, 0, 64))
-                elif step[0] == "k":
-                    key_claims((j,))
+                elif step[0] in "fxk":
+                    claimed_by({"f": "NB", "x": "XB", "k": "KT"}[step[0]], int(step[1]))
+                elif step[1:].isdigit():
+                    {"c": cover, "u": uncovered, "w": kept_names, "p": pick, "g": sizes, "m": sums}[step[0]](int(step[1]))
                 else:
-                    {"c": cover, "u": uncovered, "p": pick, "g": sizes, "w": kept_names, "m": sums}[step[0]](j)
+                    {"o": lambda: outputs("YN", "NB", t - 1), "y": last_sizes, "cv": covered_rows, "jl": roots}[step]()
             if t == 2:
                 again("YN", "NB")
             if t == 3:
@@ -466,13 +473,14 @@ def rank_program(g, core, T, topo):
         scan(b("RR"), b("HH"), b("ZERO"), A.add, A.min, -65.0)
         for s in range(4):
             act(b("SG", 160 * s, 160 * s + 160), b("RR"), F.Sign, bias=col(8 + s), scale=-1.0, total=b("ACC", s, s + 1))
+        tt(b("YY"), b("HH"), b("RR"), A.mult)
         if t < 4:
             ts(b("TM"), b("RR", 159, 160), 65.0, A.add, 64.0, A.min)
             pe(b("pC", 200, 201), [(b("O16"), b("TM"))])
-        tt(b("YY"), b("HH"), b("RR"), A.mult)
         ts(mb(t, r, 64, 224), b("YY"), col(6), A.max, col(12 + t), A.mult)
         if t:
-            key_claims(KD)
+            for q in KD:
+                claimed_by("KT", q)
         ts(b("LN"), b("ACC"), 0.5, A.mult, 80.0, A.add)
         ln = b("LN")
         if t:
@@ -484,39 +492,55 @@ def rank_program(g, core, T, topo):
             cp(cu(t, r, 0, 64), by(b("OC"), ln))
             send(2, t, cu(t, r, 0, 68))
         else:
-            h = [(512 * i, 512 * i + 512, b("QC", 32 * i, 32 * i + 32)) for i in range(2)]
-
             def gather(name, table, on):
-                for (a, e, l), q in zip(h, on):
-                    move(q, b(name, a, e), by(b(table, PAD, top), l))
+                for i in range(2):
+                    move(on[i], b(name, 512 * i, 512 * i + 512), by(b(table, PAD, top), b("QC", 32 * i, 32 * i + 32)))
 
-            def best():
-                for a, e, l in h:
-                    scan(b("TS", a, e), b("RK"), b("KG", a, e), A.add, A.max)
+            def best(i):
+                scan(b("TS", 512 * i, 512 * i + 512), b("RK"), b("KG", 512 * i, 512 * i + 512), A.add, A.max)
+
+            def rounded():
                 ts(b("RK1"), b("TS", 15, 1024, 16), MAGIC128, A.add, MAGIC128, A.subtract)
+
+            def claimed():
                 tt(b("TF"), b("TS", 15, 1024, 16), b("RK1"), A.subtract)
                 for s in range(5):
                     pe(b("pM", 64 * s, 64 * s + 64), [(b("GJ"), b("TF"))], False, s == 4)
 
-            def first():
+            def diagonal():
                 scan(b("EWS"), b("RM", 0, 64), b("pM", 0, 64), A.mult, A.max)
+
+            def first():
                 for s in range(4):
                     ew = b("EWS", 16 * s + 15, 16 * s + 16)
                     ts(b("DC", 64 * s, 64 * s + 64), b("pM", 64 * s + 64, 64 * s + 128), ew, A.not_equal, ew, A.mult)
 
-            def kept():
+            def alone():
                 scan(b("DS"), b("RD"), b("DC"), A.max, A.min)
+
+            def kept():
                 tt(b("ST", 64, 68), b("DS", 63, 256, 64), b("TR8"), A.max)
 
-            def mine(i):
-                a, e, l = h[i]
-                tt(b("MM", a, e), by(b("LV"), b("EXPL", 32 * i, 32 * i + 32)), b("QG", a, e), A.is_equal)
-                pe(b("pN%d" % i), [(b("IDB"), b("MM", a, e))], False, False)
-                pe(b("pN%d" % i, 0, 511), [(b("IDC"), b("MM", a + 1, e))], False, False)
-                pe(b("pN%d" % i, 15, 511, 16), [(b("IDB"), b("MM", a + 16, e, 16))], False, True)
+            def mine(j):
+                tt(b("MM", 256 * j, 256 * j + 256), by(b("LV"), b("EXPL", 16 * j, 16 * j + 16)), b("QG", 256 * j, 256 * j + 256), A.is_equal)
+
+            def steps(j):
+                a, e, bank, c0 = 256 * j, 256 * j + 256, "pN%d" % (j // 2), 256 * (j % 2)
+                pe(b(bank, c0, c0 + 256), [(b("IDB"), b("MM", a, e))], False, False)
+                pe(b(bank, c0, c0 + 255), [(b("IDC"), b("MM", a + 1, e))], False, False)
+                pe(b(bank, c0 + 15, c0 + 255, 16), [(b("IDB"), b("MM", a + 16, e, 16))], False, j % 2 == 1)
 
             def least(i):
                 scan(b("NS", 512 * i, 512 * i + 512), b("QG", 512 * i, 512 * i + 512), b("pN%d" % i), A.min, A.add, 8192.0)
+
+            def new_names():
+                tt(b("ST", 0, 64), b("NS", 15, 1024, 16), b("OCC"), A.min)
+
+            def covered():
+                if t == 4:
+                    tt(b("CV"), b("CV"), b("LIVE"), A.mult)
+                x = b("NB", NAT + 4 * k + r, PAD, 16)
+                tt(x, x, b("CV"), A.max)
 
             def pivots():
                 act(b("LV"), by(b("LANE"), ln), scale=16.0, bias=float(4 * k + r))
@@ -525,89 +549,100 @@ def rank_program(g, core, T, topo):
                 gather("KG", "KT", "vs")
                 pivots()
                 gather("QG", "NB", "ss")
-                best()
-                mine(0)
-                first()
-                mine(1)
-                kept()
+                best(0)
+                best(1)
+                rounded()
+                for j, f in enumerate((claimed, diagonal, first, alone)):
+                    mine(j)
+                    if j:
+                        steps(j)
+                    f()
+                    if not j:
+                        steps(j)
                 least(0)
+                kept()
                 least(1)
-                tt(b("ST", 0, 64), b("NS", 15, 1024, 16), b("OCC"), A.min)
+                new_names()
                 ts(cu(t, r, 0, 68), b("ST", 0, 68), 8192.0, A.subtract, float(V), A.min)
                 send(2, t, cu(t, r, 0, 68))
+                follow(t, range(4 * (t - 1)))
             else:
                 pivots()
                 gather("QG", "NB", "vs")
                 gather("KG", "KT", "ss")
-                mine(0)
-                mine(1)
+                for j in range(4):
+                    mine(j)
+                    steps(j)
                 follow(t, range(12))
-                least(0)
-                least(1)
-                tt(b("ST", 0, 64), b("NS", 15, 1024, 16), b("OCC"), A.min)
+                cp(cu(t, r, 64, 128), by(b("LANE"), ln))
+                for i in range(2):
+                    least(i)
+                    best(i)
+                new_names()
+                rounded()
                 ts(cu(t, r, 0, 64), b("ST", 0, 64), 8192.0, A.subtract, float(V), A.min)
-                send(2, t, cu(t, r, 0, 64))
-                best()
-                first()
+                send(2, t, cu(t, r, 0, 128))
+                claimed()
                 spots(t)
-                kept()
-                ts(cu(t, r, 64, 72), b("ST", 64, 72), 8192.0, A.subtract)
-                cp(cu(t, r, 72, SC), by(b("LANE"), ln))
-                send(3, t, cu(t, r, 64, SC))
-            if t < 4:
-                follow(t, range(4 * (t - 1)))
-            else:
+                covered()
+                diagonal()
+                spots_or_own()
+                first()
+                cp(b("LO"), b("LO4"))
+                pristine(t)
+                outputs("YX", "XO", t)
                 pe(b("pL", 0, 160), [(b("JM", 128 * c, 128 * c + 128), b("MB", SM * c + 64, SM * c + 224)) for c in range(16)])
-        if t < 4:
-            act(b("LB", 256 * r + 64 * t, 256 * r + 64 * t + 64), by(b("LANE"), ln))
+                alone()
+                kept()
+                ts(cu(t, r, 128, SC), b("ST", 64, 72), 8192.0, A.subtract)
+                send(3, t, cu(t, r, 128, SC))
+        if t == 4:
+            break
+        act(b("LB", 256 * r + 64 * t, 256 * r + 64 * t + 64), by(b("LANE"), ln))
         if t == 0:
             expand(1, range(3, 16))
             columns()
             places(1)
+            masks()
             ts(b("DEAD"), b("YY"), -0.5, A.is_lt, -16.0, A.mult)
             ts(b("LIVE"), b("YY"), -0.5, A.is_ge)
             for j in (2, 3, 4):
                 places(j)
-        k1 = (t + 1) % 4
-        if t == 4:
-            tt(b("CV"), b("CV"), b("LIVE"), A.mult)
-        if t:
-            x = b("NB", NAT + 4 * k + r, PAD, 16)
-            tt(x, x, b("CV"), A.max)
-        if t < 4:
-            cp(b("AI"), b("pC", 200, 201))
-            ts(b("AJ"), b("AI"), 7, A.bitwise_and)
-            tt(b("THR"), b("LIMF"), b("AJ"), A.add)
 
-            def gather_map(on):
-                for a, e, q in LISTS:
-                    if q == on:
-                        move(q, b("GM", 16 * a, 16 * e), by(b("MB", 0, SM * 4 * (t + 1)), qf(k1, "QP", a, e)))
-            gather_map("s")
-            for q in range(N):
-                act(blk("XB", t, q), mb(t, q, 0, 64), scale=TINY, bias=-255.0 * TINY)
-            spots(t)
-            keys(t)
-            gather_map("v")
-            for j in LORD:
-                a, e = COVER[j]
-                lists(b(("pL", "pD", "pM")[j], a, e), "GM", 16 * a, 16 * e)
-            if t:
-                lists(b("pK", 0, 4 * LS * t), "MB", 0, SM * 4 * t)
+        def gather_map(on):
+            for a, e, q in LISTS:
+                if q == on:
+                    move(q, b("GM", 16 * a, 16 * e), by(b("MB", 0, SM * 4 * (t + 1)), qf((t + 1) % 4, "QP", a, e)))
+        gather_map("s")
         for q in range(N):
-            act(blk("XO", t, q), mb(t, q, 0, 64), scale=-1.0, bias=255.0)
-        if t == 4:
-            outputs("YX", "XO", t)
+            act(blk("XB", t, q), mb(t, q, 0, 64), scale=TINY, bias=-255.0 * TINY)
+        spots(t)
+        keys(t)
+        gather_map("v")
+        for j in LORD:
+            a, e = COVER[j]
+            lists(b(("pL", "pD", "pM")[j], a, e), "GM", 16 * a, 16 * e)
+        if t:
+            lists(b("pK", 0, 4 * LS * t), "MB", 0, SM * 4 * t)
+        pristine(t)
+        cp(b("AI"), b("pC", 200, 201))
+        spots_or_own()
+        ts(b("AJ"), b("AI"), 7, A.bitwise_and)
+        cp(b("LO"), b("LO4"))
+        tt(b("THR"), b("LIMF"), b("AJ"), A.add)
+        if t:
+            covered()
     dma("y", "d_yx", [lambda: g.sync.dma_start(T.yx[:], T.YX[:])], b("YX")[1], ())
-    for q in ORDER:
+    variables(range(8, 16))
+    tt(b("OL4"), b("pL", 0, 160), b("UU"), A.max)
+    cp(blk("NB", 4, r), cu(4, r, 0, 64))
+    cp(b("OL"), b("OL4"))
+    for q in ORDER[1:]:
         cp(blk("NB", 4, q), cu(4, q, 0, 64))
     outputs("YN", "NB", 4, "svsv")
     dma("y", "d_yn", [lambda: g.sync.dma_start(T.yn[:], T.YN[:])], b("YN")[1], ())
-    variables(range(8, 16))
-    tt(b("OL4"), b("pL", 0, 160), b("UU"), A.max)
-    cp(b("OL"), b("OL4"))
     for q in (3, 2, 1, 0):
-        ts(blk("VR", 4, q), cu(4, q, 72, SC), 16.0, A.mult, float(q), A.add)
+        ts(blk("VR", 4, q), cu(4, q, 64, 128), 16.0, A.mult, float(q), A.add)
     for q in (3, 2, 1, 0):
         claims("VR", 4, q, blk("VR", 4, q))
     cp(b("YJ", 0, 1280), by(b("VR", 0, B0 + 1024), b("OL", 0, 80)))

@@ -12,30 +12,32 @@ MAGIC = 1.5 * 2.0 ** 23
 MAGIC128 = 1.5 * 2.0 ** 30
 TINY = 2.0 ** -14
 COVER = ((0, 64), (64, 128), (128, 160))
-SIZES = (((0, 64, "s"),), ((64, 128, "s"),), ((128, 160, "s"),))
-LISTS = ((0, 64, "s"), (128, 160, "s"), (64, 128, "v"))
+SHARE = (0, 24, 32, 48)
 LORD = (0, 2, 1)
-PLAN = "f3 l0 f2 q0 s0 f1 l2 f0 q2 s2 o c0 x3 l1 x2 q1 s1 x1 p0 x0 g0 y c1 c2 jl u2 p1 w2 g1 p2 k3 g2 cv m0 k2 k1 m1 m2"
-KD = (0,)
+PLAN = "n0 f3 n1 f2 n2 l2 f1 n3 q2 s2 f0 o c0 x3 l1 x2 q1 s1 x1 p0 x0 g0 y c1 c2 jl u2 p1 w2 g1 p2 k3 g2 cv m0 k2 a0 k1 a1 h0 m1 a2 h1 m2 k0 h2"
+PLAN1 = "n0 n1 n2 n3 c0 l1 q1 s1 l2 q2 s2 z c1 p0 g0 c2 p1 u2 g1 w2 p2 g2 cv m0 a0 m2 a1 h0 a2 m1 h1 h2"
+LISTS0 = ((0, 32, "s"), (64, 96, "s"), (128, 160, "s"), (32, 64, "v"), (96, 128, "v"))
 ZV = (2,)
+PIECES = ((0, 44), (44, 88), (88, 132), (132, 160))
+E0, E1 = 4, 10
 
 SCRATCH = {}
 for _d, _spec in (
-    ("float32", "NB:%d KT:%d VR:%d YN:2560 YJ:2560 QEA:2560 QEB:2560 QF:640 QN:640 QM:640 QW:640 QL4:176 QX:160 XL4:160 CV:160 QM2:160 OC:176 "
-     "D1:176 LANE:176 ACC:4 LV:64 OCC:64 KG:1024 QG:1024 TS:1024 NS:1024 RK1:64 EWS:64 DC:256 DS:256 ST:72 TR:4 TR8:4 CC:64 LO4:64 UU:160 "
-     "OL4:160 LIMF:1 THR:1 TC:48 NE:160 QA:640 QB:160 VN:640 SCR:160 QLA:160 XT:160" % (TW, TW, TW)),
-    ("bfloat16", "XB:%d XO:%d MB:%d YX:2560 EQ:2560 XG:2560 MXS:2560 GM:2560 RM:1024 RK:512 RN:512 RD:256 MM:1024 JM:2048 ELB:160 OK:160 "
+    ("float32", "NB:%d KT:%d VR:%d YN:2560 YJ:2560 QEA:2560 QEB:2560 QF:640 QN:640 QW:640 QL4:176 QX:160 XL4:160 CV:160 CW:160 OC:176 "
+     "D1:176 LANE:176 ACC:2 LV:64 OCC:64 KG:1024 QG:1024 TS:1024 NS:1024 RK1:64 EWS:64 EK:4 ST:68 TR:4 TR8:4 CC:64 LO4:64 UU:160 "
+     "OL4:160 LIMF:1 THR:1 TC:48 QA:640 QB:640 NE:64 NF:64 OC8:64 QM:320 VN:160 SCR:160 QLA:160 XT:160 XU:160 XS:160" % (TW, TW, TW)),
+    ("bfloat16", "XB:%d XO:%d MB:%d YX:2560 EQ:2560 XG:2560 MXS:2560 GM:2560 RM:1024 RK:512 RN:512 RD:256 DC:256 DS:256 MM:1024 JM:2048 ELB:160 OK:160 "
      "HH:160 RR:160 YY:160 ZERO:160 DEAD:160 LIVE:160 TF:64 TM:1 ONES:128 O16:128 ID:128 G1:128 GG:128 GW:128 IDN:128 IDX:128 IDB:128 GJ:128 "
-     "W1:128 LB:1024 CST:256 MSK:320 MK1:320 SG:640 IDC:128 RST:512 UN:512" % (TW, TW, SM * N * R)),
-    ("int32", "LIMI:1 AI:1 AJ:1 QI:640 QI2:640 TCI:2 EXPI:64"),
-    ("uint16", "CU:%d QL:160 XL:160 QP:640 LN:4 QC:64 EXPL:64 JL:192 LO:64 OL:160" % (SC * N * R)),
+     "W1:128 LB:1024 SB:256 CST:256 MSK:320 MK1:320 SG:640 SH:320 RL:320 IDC:128 IDK:128 ID16:128 ONE:512 LC:64 RST:512 UN:512" % (TW, TW, SM * N * R)),
+    ("int32", "LIMI:1 AI:1 AJ:1 TCI:2"),
+    ("uint16", "CU:%d QL:160 XL:160 QP:640 LN:4 QC:64 JL:192 LO:64 OL:160" % (SC * N * R)),
 ):
     for _e in _spec.split():
         SCRATCH[_e.split(":")[0]] = ("sbuf", [128, int(_e.split(":")[1])], _d)
 for _e in "pZ pD pC pL pN0 pN1 pM pK".split():
     SCRATCH[_e] = ("psum", [128, 512], "float32")
-SEMAPHORES = ["v", "s", "t", "p", "lo", "d_xs", "d_lim", "d_yn", "d_yx", "d_yj"] + ["d_nb%d" % j for j in range(4)] + [
-    "a%d_%d_%d" % (k, t, q) for k in (1, 2) for t in range(R) for q in range(N)] + ["a%d_4_%d" % (k, q) for k in (3, 4) for q in range(N)]
+SEMAPHORES = ["v", "s", "t", "p", "lo", "d_xs", "d_lim", "d_yn", "d_yo", "d_yx", "d_yj"] + ["d_nb%d" % j for j in range(4)] + [
+    "a%d_%d_%d" % (k, t, q) for k in (1, 2) for t in range(R) for q in range(N)] + ["a3_%d_%d" % (t, q) for t in (0, 4) for q in range(N)]
 
 
 def queues(g, T):
@@ -167,6 +169,9 @@ def rank_program(g, core, T, topo):
     def mb(t, q, c0, c1):
         return b("MB", SM * (4 * t + q) + c0, SM * (4 * t + q) + c1)
 
+    def sized(t, q):
+        return mb(t, q, 0, 64) if t else b("SB", 64 * q, 64 * q + 64)
+
     def cu(t, q, c0, c1):
         return b("CU", SC * (4 * t + q) + c0, SC * (4 * t + q) + c1)
 
@@ -175,9 +180,9 @@ def rank_program(g, core, T, topo):
 
     dma("s", "d_lim", [lambda: g.scalar.dma_start(T.LIMI[:], T.lim[:])], (), b("LIMI")[1])
     dma("y", "d_xs", [lambda: g.sync.dma_start(T.XB[:, NAT:PAD], T.xs[:])], (), b("XB", NAT, PAD)[1])
-    for j in range(4):
-        dma("y", "d_nb%d" % j, [lambda: g.sync.dma_start(T.NB[:, NAT + 640 * j:NAT + 640 * j + 640], T.nb[:, 640 * j:640 * j + 640])],
-            (), b("NB", NAT + 640 * j, NAT + 640 * j + 640)[1])
+    for j, (a, e) in enumerate(PIECES):
+        dma("y", "d_nb%d" % j, [lambda: g.sync.dma_start(T.NB[:, NAT + 16 * a:NAT + 16 * e], T.nb[:, 16 * a:16 * e])],
+            (), b("NB", NAT + 16 * a, NAT + 16 * e)[1])
 
     iota(b("TCI", 0, 1), [[1, 1]], 0, 1)
     fill(b("ONES"), 1.0)
@@ -187,10 +192,9 @@ def rank_program(g, core, T, topo):
     iota(b("TR"), [[16, 4]], 0, 0)
     iota(b("CC"), [[1, 4], [256, LS]], NAT - 1024, 0)
     iota(b("CST"), [[0, 4], [1, 64]], -64, 0)
-    iota(b("EXPI"), [[1, 64]], 0, 0)
     iota(b("SCR", 0, 160), [[16, 160]], NAT, 0)
-    iota(b("VN"), [[4, 640]], r, 0)
     iota(b("LANE"), [[1, 176]], 0, 0)
+    iota(b("VN"), [[16, 160]], 4 + r, 0)
     iota(b("MK1", 0, 64), [[0, 4], [1, 16]], 0, 0)
     iota(b("MK1", 64, 320), [[-16, 4], [1, 64]], 0, 0)
     for name, n, x in (("RK", 512, 128), ("RN", 512, 0), ("RST", 512, 0), ("RD", 256, 0)):
@@ -210,6 +214,8 @@ def rank_program(g, core, T, topo):
     for name, x in (("D1", MAGIC), ("OC", float(V)), ("QL4", 0.0)):
         fill(b(name, 160, 176), x)
     ts(b("THR"), b("LIMF"), 0.3, A.add)
+    for j in range(N):
+        act(b("MB", SM * j, SM * j + 64), b("ZERO", 0, 64))
     for j in range(N * R):
         act(b("MB", SM * j + 224, SM * j + SM), b("ZERO", 0, 32))
     ts(col(7), e1, 64.0, A.mult, e0, A.add)
@@ -224,12 +230,16 @@ def rank_program(g, core, T, topo):
         ts(col(12 + t), e1, -float(B0 // 64 + 1 + 4 * t + r), A.mult, e0, A.add)
     ts(b("TC", 8, 12), b("TR"), -64.5, A.add)
     ts(b("O16"), b("ONES"), 1.0 / 16.0, A.mult)
+    fill(b("ONE"), 1.0)
+    fill(b("RL"), 1.0)
     fill(b("W1"), 0.0)
     fill(b("RM"), 1.0)
     tt(col(18), e0, e4, A.add)
     ts(col(19), e4, 32.0, A.mult)
     tt(col(20), e1, e5, A.add)
     tt(col(37), e4, e5, A.add)
+    fill(b("RL", 160, 161), 0.0)
+    fill(b("RM", 0, 1024, 16), 0.0)
     ts(col(36), pm, 16.0, A.mult)
     for j in (4, 5):
         ts(b("W1", j, 128, 16), b("GG", j, 128, 16), -2048.0, A.mult)
@@ -242,45 +252,22 @@ def rank_program(g, core, T, topo):
     for q in range(N):
         ts(b("CST", 64 * q, 64 * q + 64), b("CST", 64 * q, 64 * q + 64), col(18), A.mult, col(22 + q), A.add)
     ts(b("KT", PAD, B0), b("ZERO", 0, B0 - PAD), col(37), A.add, -4096.0, A.mult)
-    for name, x in (("IDN", -8192.0), ("IDX", -1.0 / TINY), ("IDB", 4096.0), ("IDC", -4096.0)):
+    for name, x in (("IDN", -8192.0), ("IDX", -1.0 / TINY), ("IDB", 4096.0), ("IDC", -4096.0), ("ID16", 16.0)):
         act(b(name), b("ID"), scale=x)
     ts(b("TR8"), b("TR"), 8192.0, A.add)
-    cp(b("EXPL"), b("EXPI"))
     ts(b("GJ"), b("GG"), col(17), A.mult)
     ts(b("UU"), b("SCR"), pm, A.add)
-    fill(b("ST", 68, 72), 0.0)
 
     def masks():
         ts(b("MSK", 0, 64), b("MK1", 0, 64), pm, A.not_equal, -16384.0, A.mult)
         ts(b("MSK", 64, 320), b("MK1", 64, 320), pm, A.is_ge, 4096.0, A.mult)
-        for name, c0, n, st, y in (("RM", 0, 1024, 16, 0.0), ("RK", 0, 512, 16, -2.0 ** 24), ("RN", 0, 512, 16, 8192.0),
-                                   ("RD", 0, 256, 64, 16384.0), ("RST", 15, 512, 16, 8192.0)):
+        for name, c0, n, st, y in (("RK", 0, 512, 16, -2.0 ** 24), ("RN", 0, 512, 16, 8192.0),
+                                   ("RD", 0, 256, 64, 1.0), ("RST", 15, 512, 16, 8192.0)):
             fill(b(name, c0, n, st), y)
         ts(b("MSK"), b("MSK"), 8192.0 - DUMP - 32, A.add)
 
     def qf(k, name="QF", a=0, e=160):
         return b(name, 160 * k + a, 160 * k + e) if name == "QP" else b(name, 4 * a + k, 4 * e, 4)
-
-    def quarter(name, j):
-        return b(name, 160 * j, 160 * j + 160)
-
-    def names(j):
-        act(quarter("QF", j), b("NB", NAT + 640 * j + r, NAT + 640 * j + 640, 4))
-
-    def own(j):
-        tt(b("NE"), quarter("QF", j), quarter("VN", j), A.is_equal)
-
-    def but_own(j):
-        ts(b("QB"), b("NE"), float(V), A.mult)
-        tt(quarter("QM", j), quarter("QF", j), b("QB"), A.max)
-
-    def columns():
-        act(b("QN"), b("QF"), scale=1.0 / 16.0, bias=64.0)
-        cp(b("QI"), b("QF"))
-        ts(b("QI2"), b("QI"), 15, A.bitwise_and)
-        ts(b("QA"), b("QI2"), SM - 1.0 / 16.0, A.mult)
-        tt(b("QW"), b("QN"), b("QA"), A.add)
-        act(b("QN"), b("QF"), bias=float(NAT))
 
     def places(t):
         ts(qf(t % 4, "QP"), qf(t % 4, "QW"), float(SM * 4 * t - 32), A.min)
@@ -304,19 +291,18 @@ def rank_program(g, core, T, topo):
     for t in range(R):
         for q in range(N):
             if q != r:
-                arrive("a1_%d_%d" % (t, q), neng, mb(t, q, 0, 224)[1])
-                arrive("a2_%d_%d" % (t, q), neng, cu(t, q, 0, 68 if t < 4 else 128)[1])
-                if t == 4:
-                    arrive("a3_%d_%d" % (t, q), neng, cu(t, q, 128, SC)[1])
-                    arrive("a4_%d_%d" % (t, q), neng, b("LB", 256 * q, 256 * q + 256)[1])
+                arrive("a1_%d_%d" % (t, q), neng, mb(t, q, 0 if t else 64, 224)[1])
+                arrive("a2_%d_%d" % (t, q), neng, cu(t, q, 0, (64, 68, 68, 68, 132)[t])[1])
+                if t in (0, 4):
+                    arrive("a3_%d_%d" % (t, q), neng, (b("LB", 256 * q, 256 * q + 256) if t else sized(t, q))[1])
 
     def claims(name, t, q, src):
-        cp(by(b(name, DUMP, B0 + 256 * t), cu(t, q, 64, 68) if t < 4 else cu(t, q, 128, 132)), src)
+        cp(by(b(name, DUMP, B0 + 256 * t), cu(t, q, 64, 68)), src)
 
     def keys(t):
         pe(b("pK", 0, 256), [(b("ID"), b("CST"))], True, False)
         for q in range(N):
-            pe(b("pK", 64 * q, 64 * q + 64), [(b("W1"), mb(t, q, 0, 64))], False, q == N - 1)
+            pe(b("pK", 64 * q, 64 * q + 64), [(b("W1"), sized(t, q))], False, q == N - 1)
         act(blk("KT", t, 0, 4), b("pK", 0, 256), F.Identity, bias=col(31 + t))
 
     def outputs(out, table, t, on="ssss"):
@@ -324,10 +310,10 @@ def rank_program(g, core, T, topo):
             move(on[q], b(out, (4 * t + q) % 16, V, 16), by(b(table, 0, B0 + 256 * (t + 1)), b("LO", LS * q + 4, LS * q + 14)))
 
     def spots(t):
-        lists(b("pZ", 256, 256 + 4 * LS), "MB", SM * 4 * t, SM * 4 * (t + 1))
+        lists(b("pC", 256, 256 + 4 * LS), "MB", SM * 4 * t, SM * 4 * (t + 1))
 
     def spots_or_own():
-        tt(b("LO4"), b("pZ", 256, 256 + 4 * LS), b("CC"), A.max)
+        tt(b("LO4"), b("pC", 256, 256 + 4 * LS), b("CC"), A.max)
 
     def slots(t, step):
         j, k = int(step[1]), t % 4
@@ -343,11 +329,18 @@ def rank_program(g, core, T, topo):
             act(b("QL4", a, e), x, F.Relu, bias=-float(PAD))
         else:
             tt(b("QX", a, e), x, qf(k, "QN", a, e), A.max)
-            tt(b("QM2", a, e), x, qf(k, "QM", a, e), A.max)
 
-    def follow(t, js):
+    def but_own(t, j):
+        if t < R:
+            [lambda: tt(b("QA", 0, 160), qf(t % 4), b("VN"), A.is_equal), lambda: ts(b("QB", 0, 160), b("QA", 0, 160), float(V), A.mult),
+             lambda: tt(b("QM", 160 * (t % 2), 160 * (t % 2) + 160), qf(t % 4), b("QB", 0, 160), A.max)][j]()
+
+    def limits(j):
+        [lambda: cp(b("AI"), b("pK", 500, 501)), lambda: ts(b("AJ"), b("AI"), 7, A.bitwise_and), lambda: tt(b("THR"), b("LIMF"), b("AJ"), A.add)][j]()
+
+    def follow(t, js, on="s"):
         for j in js:
-            act(b("MB", SM * j + 64, SM * j + 224), by(b("KT", PAD, B0 + 256 * t), b("JL", LS * j + 4, LS * j + 14)))
+            move(on, b("MB", SM * j + 64, SM * j + 224), by(b("KT", PAD, B0 + 256 * t), b("JL", LS * j + 4, LS * j + 14)))
 
     def variables(js):
         for j in js:
@@ -355,11 +348,16 @@ def rank_program(g, core, T, topo):
 
     def again(out, table):
         for q in range(N):
-            act(b(table, NAT + q, PAD, 16), b(out, q, V, 16))
+            select(b(table, NAT + q, PAD, 16), b(out, q, V, 16), [[0, 160]], A.is_ge, 0.0, 0, 0)
 
     def pristine(t):
         for q in range(N):
-            act(blk("XO", t, q), mb(t, q, 0, 64), scale=-1.0, bias=255.0)
+            act(blk("XO", t, q), sized(t, q), scale=-1.0, bias=255.0)
+
+    def new_sizes(t):
+        for q in range(N):
+            act(blk("XB", t, q), sized(t, q), scale=TINY, bias=-255.0 * TINY)
+        keys(t)
 
     ORDER = [r] + [q for q in (3, 2, 1, 0) if q != r]
     for t in range(R):
@@ -367,33 +365,25 @@ def rank_program(g, core, T, topo):
         top = B0 + 256 * t
         qe = "QEB" if t % 2 else "QEA"
         if t == 0:
-            for j in range(4):
-                a = 40 * j
-                ts(b("XL", a, a + 40), b("NB", NAT + 16 * a + r, NAT + 16 * a + 640, 16), float(NAT), A.add)
-                if j < 3:
-                    names(j)
+            for j, (a, e) in enumerate(PIECES):
+                m = (a + e) // 2
+                ts(b("XL", a, e), b("NB", NAT + 16 * a + r, NAT + 16 * e, 16), float(NAT), A.add)
+                act(b("XG", 16 * a, 16 * m), by(b("XB", 0, B0), b("XL", a, m)))
+                cp(b("XG", 16 * m, 16 * e), by(b("XB", 0, B0), b("XL", m, e)))
                 if j:
-                    own(j - 1)
-                act(b("XG", 16 * a, 16 * a + 320), by(b("XB", 0, B0), b("XL", a, a + 20)))
-                cp(b("XG", 16 * a + 320, 16 * a + 640), by(b("XB", 0, B0), b("XL", a + 20, a + 40)))
-                if j % 2:
-                    pe(b("pD", a - 40, a + 40), [(b("ID"), b("XG", 16 * a - 640 + i, 16 * a + 640, 16)) for i in range(16)])
-                if j < 3:
-                    act(b("XO", NAT + 860 * j, min(NAT + 860 * j + 860, PAD)), b("XB", NAT + 860 * j, min(NAT + 860 * j + 860, PAD)))
-                if j:
-                    but_own(j - 1)
-            names(3)
-            own(3)
-            but_own(3)
-            act(b("OC", 0, 160), qf(0, "QM"))
-            expand(1, range(3))
+                    a0 = a if j > 1 else 0
+                    pe(b("pD", a0, e), [(b("ID"), b("XG", 16 * a0 + i, 16 * e, 16)) for i in range(16)])
+                act(b("QF", 4 * a, 4 * e), b("NB", NAT + 16 * a + r, NAT + 16 * e, 4))
+            cp(b("OC", 0, 160), qf(0))
+            act(b("QW"), b("QF"), bias=-7.5)
+            act(b("QA"), b("QW"), scale=1.0 / 16.0, bias=MAGIC)
+            expand(1, range(E0))
         else:
-            for q in ORDER:
-                cp(blk("NB", t - 1, q), cu(t - 1, q, 0, 64))
             if t < 4:
                 expand(t + 1, range(16))
+                iota(b("VN"), [[16, 160]], 4 * ((t + 1) % 4) + r, 0)
             else:
-                send(4, t, b("LB", 256 * r, 256 * r + 256))
+                send(3, t, b("LB", 256 * r, 256 * r + 256))
                 iota(b("VR", 0, B0), [[1, B0]], -NAT, 0)
             banks = ("pZ", "pN0", "pN1")
 
@@ -402,6 +392,8 @@ def rank_program(g, core, T, topo):
                 tt(b("EQ", 16 * a, 16 * e), by(b("NB", PAD, top), b("QL", a, e)), b(qe, 16 * a, 16 * e), A.not_equal if j in ZV else A.is_equal)
                 if j not in ZV:
                     pe(b(banks[j], a, e), [(b("ID"), b("ELB", a, e))] + [(b("IDN"), b("EQ", 16 * a + i, 16 * e, 16)) for i in range(16)])
+                if j == 0 and t > 1:
+                    lists(b("pK", 256, 256 + 4 * LS * (t - 1)), "MB", 0, SM * 4 * (t - 1))
 
             def uncovered(j):
                 a, e = COVER[j]
@@ -421,8 +413,7 @@ def rank_program(g, core, T, topo):
             def sizes(j):
                 a, e = COVER[j]
                 cp(b("XL", a, e), b("XL4", a, e))
-                for a, e, q in SIZES[j]:
-                    move(q, b("XG", 16 * a, 16 * e), by(b("XB", 0, top), b("XL", a, e)))
+                move("v" if j in ZV and t == 1 else "s", b("XG", 16 * a, 16 * e), by(b("XB", 0, top), b("XL", a, e)))
 
             def sums(j):
                 a, e = COVER[j]
@@ -434,26 +425,34 @@ def rank_program(g, core, T, topo):
                 if t > 1:
                     claims(name, t - 1, q, cu(t - 1, q, 0, 64) if name == "NB" else blk(name, t - 1, q))
 
+            def last_names():
+                outputs("YN", "NB", t - 1)
+
             def last_sizes():
                 outputs("YX", "XO", t - 1)
                 act(b("CC"), b("CC"), bias=4.0 if t < 4 else -12.0)
 
             def covered_rows():
-                act(b("XT"), b("XL4"), F.Sign, bias=0.5, scale=-1.0)
-                act(b("CV"), b("XT"), F.Relu, scale=float(V))
+                act(b("XU"), b("XL4"), F.Abs, bias=-1296.0)
+                act(b("XS"), b("XL4"), F.Sign, bias=0.5, scale=-1.0)
+                act(b("CW"), b("XU"), F.Relu, scale=float(V), bias=-1288.0 * V)
+                act(b("CV"), b("XS"), F.Relu, scale=float(V))
 
             def roots():
                 if t > 1:
-                    ts(b("JL", 0, 4 * LS * (t - 1)), b("pK", 0, 4 * LS * (t - 1)), float(PAD), A.max, float(PAD), A.subtract)
-            for step in PLAN.split():
+                    ts(b("JL", 0, 4 * LS * (t - 1)), b("pK", 256, 256 + 4 * LS * (t - 1)), float(PAD), A.max, float(PAD), A.subtract)
+            for step in (PLAN if t > 1 else PLAN1).split():
                 if step[0] in "lqs":
                     slots(t, step)
+                elif step[0] == "n":
+                    cp(blk("NB", t - 1, ORDER[int(step[1])]), cu(t - 1, ORDER[int(step[1])], 0, 64))
                 elif step[0] in "fxk":
                     claimed_by({"f": "NB", "x": "XB", "k": "KT"}[step[0]], int(step[1]))
                 elif step[1:].isdigit():
-                    {"c": cover, "u": uncovered, "w": kept_names, "p": pick, "g": sizes, "m": sums}[step[0]](int(step[1]))
+                    {"c": cover, "u": uncovered, "w": kept_names, "p": pick, "g": sizes, "m": sums,
+                     "h": lambda j: but_own(t + 1, j), "a": limits}[step[0]](int(step[1]))
                 else:
-                    {"o": lambda: outputs("YN", "NB", t - 1), "y": last_sizes, "cv": covered_rows, "jl": roots}[step]()
+                    {"o": last_names, "z": lambda: new_sizes(0), "y": last_sizes, "cv": covered_rows, "jl": roots}[step]()
             if t == 2:
                 again("YN", "NB")
             if t == 3:
@@ -465,33 +464,47 @@ def rank_program(g, core, T, topo):
         if t:
             pe(b("pM", 0, 320), [(b("ID"), b("MSK"))], True, False)
             for i in range(2):
+                pe(b(("pZ", "pL")[i]), [(b("IDK"), b("ONE"))], True, False)
+            for i in range(2):
                 pe(b("pN%d" % i), [(b("ID"), b("RST"))], True, False)
         act(b("D1", 0, 160), b("pD", 0, 160), bias=MAGIC)
         if t:
-            tt(b("OC", 0, 160), b("QM2"), b("CV"), A.max)
+            tt(b("OC", 0, 160), b("QM", 160 * (t % 2), 160 * (t % 2) + 160), b("CW"), A.max)
         ts(b("HH"), b("pC", 0, 160), 8.5, A.is_ge)
         scan(b("RR"), b("HH"), b("ZERO"), A.add, A.min, -65.0)
-        for s in range(4):
+        for s in range(2):
             act(b("SG", 160 * s, 160 * s + 160), b("RR"), F.Sign, bias=col(8 + s), scale=-1.0, total=b("ACC", s, s + 1))
+        for s in (2, 3):
+            ts(b("SG", 160 * s, 160 * s + 160), b("RR"), col(8 + s), A.is_le)
         tt(b("YY"), b("HH"), b("RR"), A.mult)
+        scan(b("SH"), b("RL"), b("SG", 320, 640), A.mult, A.add)
+        ts(mb(t, r, 64, 224), b("YY"), col(6), A.max, col(12 + t), A.mult)
+        if t == 0:
+            send(1, t, mb(t, r, 64, 224))
+        ts(b("LN", 0, 2), b("ACC"), 0.5, A.mult, 80.0, A.add)
+        cp(b("LN", 2, 4), b("SH", 159, 320, 160))
         if t < 4:
             ts(b("TM"), b("RR", 159, 160), 65.0, A.add, 64.0, A.min)
-            pe(b("pC", 200, 201), [(b("O16"), b("TM"))])
-        ts(mb(t, r, 64, 224), b("YY"), col(6), A.max, col(12 + t), A.mult)
-        if t:
-            for q in KD:
-                claimed_by("KT", q)
-        ts(b("LN"), b("ACC"), 0.5, A.mult, 80.0, A.add)
+            pe(b("pK", 500, 501), [(b("O16"), b("TM"))])
         ln = b("LN")
-        if t:
-            cp(b("QC"), by(b("QL4"), ln))
-        act(mb(t, r, 0, 64), by(b("D1"), ln), F.Relu, bias=MAGIC + 255.0, scale=-1.0)
-        send(1, t, mb(t, r, 0, 224))
         if t == 0:
-            cp(cu(t, r, 64, 68), b("TR"))
-            cp(cu(t, r, 0, 64), by(b("OC"), ln))
-            send(2, t, cu(t, r, 0, 68))
+            act(b("QB"), b("QF"), scale=float(SM), bias=64.0)
+            ts(b("QA"), b("QA"), MAGIC, A.subtract, 1.0 - 16.0 * SM, A.mult)
         else:
+            cp(b("QC"), by(b("QL4"), ln))
+        act(sized(t, r), by(b("D1"), ln), F.Relu, bias=MAGIC + 255.0, scale=-1.0)
+        if t == 0:
+            act(b("LV"), by(b("LANE"), ln), scale=16.0, bias=float(r))
+            act(b("OCC"), by(b("OC"), ln))
+            tt(b("NE"), b("OCC"), b("LV"), A.is_equal)
+            act(b("NF"), b("NE"), scale=4096.0, bias=8192.0)
+            tt(b("OC8"), b("OCC"), b("NF"), A.add)
+            ts(cu(t, r, 0, 64), b("OC8"), 8192.0, A.subtract, float(V), A.min)
+            send(2, t, cu(t, r, 0, 64))
+            send(3, t, sized(t, r))
+        else:
+            send(1, t, mb(t, r, 0, 224))
+
             def gather(name, table, on):
                 for i in range(2):
                     move(on[i], b(name, 512 * i, 512 * i + 512), by(b(table, PAD, top), b("QC", 32 * i, 32 * i + 32)))
@@ -513,16 +526,16 @@ def rank_program(g, core, T, topo):
             def first():
                 for s in range(4):
                     ew = b("EWS", 16 * s + 15, 16 * s + 16)
-                    ts(b("DC", 64 * s, 64 * s + 64), b("pM", 64 * s + 64, 64 * s + 128), ew, A.not_equal, ew, A.mult)
+                    ts(b("DC", 64 * s, 64 * s + 64), b("pM", 64 * s + 64, 64 * s + 128), ew, A.not_equal)
 
             def alone():
                 scan(b("DS"), b("RD"), b("DC"), A.max, A.min)
 
             def kept():
-                tt(b("ST", 64, 68), b("DS", 63, 256, 64), b("TR8"), A.max)
+                tt(b("ST", 64, 68), b("EK"), b("TR8"), A.max)
 
             def mine(j):
-                tt(b("MM", 256 * j, 256 * j + 256), by(b("LV"), b("EXPL", 16 * j, 16 * j + 16)), b("QG", 256 * j, 256 * j + 256), A.is_equal)
+                tt(b("MM", 256 * j, 256 * j + 256), b(("pZ", "pL")[j // 2], 256 * (j % 2), 256 * (j % 2) + 256), b("QG", 256 * j, 256 * j + 256), A.is_equal)
 
             def steps(j):
                 a, e, bank, c0 = 256 * j, 256 * j + 256, "pN%d" % (j // 2), 256 * (j % 2)
@@ -534,7 +547,7 @@ def rank_program(g, core, T, topo):
                 scan(b("NS", 512 * i, 512 * i + 512), b("QG", 512 * i, 512 * i + 512), b("pN%d" % i), A.min, A.add, 8192.0)
 
             def new_names():
-                tt(b("ST", 0, 64), b("NS", 15, 1024, 16), b("OCC"), A.min)
+                tt(b("ST", 0, 64), b("NS", 15, 1024, 16), b("OC8"), A.min)
 
             def covered():
                 if t == 4:
@@ -542,67 +555,60 @@ def rank_program(g, core, T, topo):
                 x = b("NB", NAT + 4 * k + r, PAD, 16)
                 tt(x, x, b("CV"), A.max)
 
-            def pivots():
-                act(b("LV"), by(b("LANE"), ln), scale=16.0, bias=float(4 * k + r))
-                act(b("OCC"), by(b("OC"), ln), bias=8192.0)
-            if t < 4:
-                gather("KG", "KT", "vs")
-                pivots()
-                gather("QG", "NB", "ss")
-                best(0)
-                best(1)
-                rounded()
-                for j, f in enumerate((claimed, diagonal, first, alone)):
-                    mine(j)
-                    if j:
-                        steps(j)
-                    f()
-                    if not j:
-                        steps(j)
-                least(0)
-                kept()
-                least(1)
-                new_names()
-                ts(cu(t, r, 0, 68), b("ST", 0, 68), 8192.0, A.subtract, float(V), A.min)
-                send(2, t, cu(t, r, 0, 68))
-                follow(t, range(4 * (t - 1)))
-            else:
-                pivots()
-                gather("QG", "NB", "vs")
-                gather("KG", "KT", "ss")
-                for j in range(4):
-                    mine(j)
-                    steps(j)
-                follow(t, range(12))
-                cp(cu(t, r, 64, 128), by(b("LANE"), ln))
-                for i in range(2):
-                    least(i)
-                    best(i)
-                new_names()
-                rounded()
-                ts(cu(t, r, 0, 64), b("ST", 0, 64), 8192.0, A.subtract, float(V), A.min)
-                send(2, t, cu(t, r, 0, 128))
-                claimed()
-                spots(t)
-                covered()
-                diagonal()
-                spots_or_own()
-                first()
-                cp(b("LO"), b("LO4"))
+            name, c0 = ("LB", 256 * r + 64 * t) if t < 4 else ("LC", 0)
+            act(b(name, c0, c0 + 64), by(b("LANE"), ln))
+            for i in range(2):
+                for j in range(16):
+                    pe(b(("pZ", "pL")[i], j, 512, 16), [(b("ID16"), b(name, c0 + 32 * i, c0 + 32 * i + 32))], False, j == 15)
+            gather("KG", "KT", "vs")
+            gather("QG", "NB", "ss")
+            act(b("OC8"), by(b("OC"), ln), bias=8192.0)
+            best(0)
+            best(1)
+            if t == 4:
+                cp(cu(t, r, 68, 132), by(b("LANE"), ln))
+            rounded()
+            mine(0)
+            claimed()
+            steps(0)
+            for j in (1, 2, 3):
+                if j == 3:
+                    diagonal()
+                mine(j)
+                steps(j)
+            first()
+            least(0)
+            alone()
+            if t == 4:
+                follow(t, range(5))
                 pristine(t)
-                outputs("YX", "XO", t)
-                pe(b("pL", 0, 160), [(b("JM", 128 * c, 128 * c + 128), b("MB", SM * c + 64, SM * c + 224)) for c in range(16)])
-                alone()
-                kept()
-                ts(cu(t, r, 128, SC), b("ST", 64, 72), 8192.0, A.subtract)
-                send(3, t, cu(t, r, 128, SC))
-        if t == 4:
-            break
-        act(b("LB", 256 * r + 64 * t, 256 * r + 64 * t + 64), by(b("LANE"), ln))
+                spots(t)
+                follow(t, range(5, 12))
+                pe(b("pD", 0, 160), [(b("JM", 128 * c, 128 * c + 128), b("MB", SM * c + 64, SM * c + 224)) for c in range(16)])
+            tt(b("EK"), b("DS", 63, 256, 64), b("EWS", 15, 64, 16), A.mult)
+            least(1)
+            kept()
+            new_names()
+            ts(cu(t, r, 0, 68), b("ST"), 8192.0, A.subtract, float(V), A.min)
+            send(2, t, cu(t, r, 0, 68 if t < 4 else 132))
+            if t == 4:
+                break
+            if t == 1:
+                pristine(0)
+                last_names()
+                last_sizes()
+            follow(t, range(4 * (t - 1)))
         if t == 0:
-            expand(1, range(3, 16))
-            columns()
+            act(b("LB", 256 * r, 256 * r + 64), by(b("LANE"), ln))
+        act(b("IDK"), b("ID"), scale=float(4 * ((t + 1) % 4) + r))
+        if t == 0:
+            expand(1, range(E0, E1))
+            tt(b("QW"), b("QA"), b("QB"), A.add)
+            act(b("QN"), b("QF"), bias=float(NAT))
             places(1)
+            for j in range(E1, 16):
+                act(b("QEB", j, V, 16), qf(1))
+            act(b("XO", NAT, PAD), b("XB", NAT, PAD))
             masks()
             ts(b("DEAD"), b("YY"), -0.5, A.is_lt, -16.0, A.mult)
             ts(b("LIVE"), b("YY"), -0.5, A.is_ge)
@@ -610,41 +616,53 @@ def rank_program(g, core, T, topo):
                 places(j)
 
         def gather_map(on):
-            for a, e, q in LISTS:
+            for a, e, q in ((0, 64, "s"), (128, 160, "s"), (64, 128 - SHARE[t], "s"), (128 - SHARE[t], 128, "v")) if t else LISTS0:
                 if q == on:
                     move(q, b("GM", 16 * a, 16 * e), by(b("MB", 0, SM * 4 * (t + 1)), qf((t + 1) % 4, "QP", a, e)))
-        gather_map("s")
-        for q in range(N):
-            act(blk("XB", t, q), mb(t, q, 0, 64), scale=TINY, bias=-255.0 * TINY)
-        spots(t)
-        keys(t)
-        gather_map("v")
-        for j in LORD:
-            a, e = COVER[j]
-            lists(b(("pL", "pD", "pM")[j], a, e), "GM", 16 * a, 16 * e)
-        if t:
-            lists(b("pK", 0, 4 * LS * t), "MB", 0, SM * 4 * t)
-        pristine(t)
-        cp(b("AI"), b("pC", 200, 201))
-        spots_or_own()
-        ts(b("AJ"), b("AI"), 7, A.bitwise_and)
-        cp(b("LO"), b("LO4"))
-        tt(b("THR"), b("LIMF"), b("AJ"), A.add)
         if t:
             covered()
-    dma("y", "d_yx", [lambda: g.sync.dma_start(T.yx[:], T.YX[:])], b("YX")[1], ())
-    variables(range(8, 16))
-    tt(b("OL4"), b("pL", 0, 160), b("UU"), A.max)
+        else:
+            for j in range(3):
+                but_own(1, j)
+        gather_map("s")
+        spots(t)
+        gather_map("v")
+        for j in LORD if t else range(3):
+            a, e = COVER[j]
+            lists(b(("pL", "pD", "pM")[j], a, e), "GM", 16 * a, 16 * e)
+        spots_or_own()
+        slots(t + 1, "l0")
+        cp(b("LO"), b("LO4"))
+        for step in ("q0", "s0"):
+            slots(t + 1, step)
+        if t:
+            new_sizes(t)
+            pristine(t)
+    def last_variables(q):
+        ts(blk("VR", 4, q), cu(4, q, 68, 132), 16.0, A.mult, float(q), A.add)
+    spots_or_own()
     cp(blk("NB", 4, r), cu(4, r, 0, 64))
-    cp(b("OL"), b("OL4"))
+    cp(b("LO"), b("LO4"))
+    last_variables(r)
+    outputs("YX", "XO", 4, "vvss")
+    dma("y", "d_yx", [lambda: g.sync.dma_start(T.yx[:], T.YX[:])], b("YX")[1], ())
+    covered()
+    variables(range(8, 16))
     for q in ORDER[1:]:
         cp(blk("NB", 4, q), cu(4, q, 0, 64))
-    outputs("YN", "NB", 4, "svsv")
-    dma("y", "d_yn", [lambda: g.sync.dma_start(T.yn[:], T.YN[:])], b("YN")[1], ())
-    for q in (3, 2, 1, 0):
-        ts(blk("VR", 4, q), cu(4, q, 64, 128), 16.0, A.mult, float(q), A.add)
-    for q in (3, 2, 1, 0):
-        claims("VR", 4, q, blk("VR", 4, q))
+    for a, e, sem in ((0, 6, "d_yn"), (6, 10, "d_yo")):
+        for q in range(N):
+            move("v" if a == 0 and q < 2 else "s", b("YN", 256 * a + q, 256 * e, 16), by(b("NB"), b("LO", LS * q + 4 + a, LS * q + 4 + e)))
+        dma("y", sem, [lambda: g.sync.dma_start(T.yn[:, 256 * a:256 * e], T.YN[:, 256 * a:256 * e])], b("YN", 256 * a, 256 * e)[1], ())
+    for q in (4, 3, 2, 1, 0):
+        if q and q - 1 != r:
+            last_variables(q - 1)
+        if q < 4:
+            claims("VR", 4, q, blk("VR", 4, q))
+        if q == 3:
+            tt(b("OL4"), b("pD", 0, 160), b("UU"), A.max)
+        if q == 1:
+            cp(b("OL"), b("OL4"))
     cp(b("YJ", 0, 1280), by(b("VR", 0, B0 + 1024), b("OL", 0, 80)))
     act(b("YJ", 1280, V), by(b("VR", 0, B0 + 1024), b("OL", 80, 160)))
     dma("s", "d_yj", [lambda: g.scalar.dma_start(T.yj[:], T.YJ[0:128:16, :])], b("YJ")[1], ())

from concourse.bass import DstId, RemoteDMATransfer
from concourse.mybir import AluOpType, ActivationFunctionType

A = AluOpType
F = ActivationFunctionType
V, N, R = 2560, 4, 5
NAT, PAD, DUMP, B0 = 16, 2576, 2592, 2688
TW = B0 + 64 * N * R
SM, SC = 256, 136
LS = SM // 16
MAGIC = 1.5 * 2.0 ** 23
MAGIC128 = 1.5 * 2.0 ** 30
TINY = 2.0 ** -14
COVER = ((0, 64), (64, 128), (128, 160))
SHARE = (0, 24, 32, 48)
LORD = (0, 2, 1)
PLAN = "n0 f3 n1 f2 n2 l2 f1 n3 q2 s2 f0 o c0 x3 l1 x2 q1 s1 x1 p0 x0 g0 y c1 c2 jl u2 p1 w2 g1 p2 k3 g2 cv m0 k2 a0 k1 a1 h0 m1 a2 h1 m2 k0 h2"
PLAN1 = "n0 n1 n2 n3 c0 l1 q1 s1 l2 q2 s2 z c1 p0 g0 c2 p1 u2 g1 w2 p2 g2 cv m0 a0 m2 a1 h0 a2 m1 h1 h2"
LISTS0 = ((0, 32, "s"), (64, 96, "s"), (128, 160, "s"), (32, 64, "v"), (96, 128, "v"))
ZV = (2,)
PIECES = ((0, 44), (44, 88), (88, 132), (132, 160))
E0, E1 = 4, 10

SCRATCH = {}
for _d, _spec in (
    ("float32", "NB:%d KT:%d VR:%d YN:2560 YJ:2560 QEA:2560 QEB:2560 QF:640 QN:640 QW:640 QL4:176 QX:160 XL4:160 CV:160 CW:160 OC:176 "
     "D1:176 LANE:176 ACC:2 LV:64 OCC:64 KG:1024 QG:1024 TS:1024 NS:1024 RK1:64 EWS:64 EK:4 ST:68 TR:4 TR8:4 CC:64 LO4:64 UU:160 "
     "OL4:160 LIMF:1 THR:1 TC:48 QA:640 QB:640 NE:64 NF:64 OC8:64 QM:320 VN:160 SCR:160 QLA:160 XT:160 XU:160 XS:160" % (TW, TW, TW)),
    ("bfloat16", "XB:%d XO:%d MB:%d YX:2560 EQ:2560 XG:2560 MXS:2560 GM:2560 RM:1024 RK:512 RN:512 RD:256 DC:256 DS:256 MM:1024 JM:2048 ELB:160 OK:160 "
     "HH:160 RR:160 YY:160 ZERO:160 DEAD:160 LIVE:160 TF:64 TM:1 ONES:128 O16:128 ID:128 G1:128 GG:128 GW:128 IDN:128 IDX:128 IDB:128 GJ:128 "
     "W1:128 LB:1024 SB:256 CST:256 MSK:320 MK1:320 SG:640 SH:320 RL:320 IDC:128 IDK:128 ID16:128 ONE:512 LC:64 RST:512 UN:512" % (TW, TW, SM * N * R)),
    ("int32", "LIMI:1 AI:1 AJ:1 TCI:2"),
    ("uint16", "CU:%d QL:160 XL:160 QP:640 LN:4 QC:64 JL:192 LO:64 OL:160" % (SC * N * R)),
):
    for _e in _spec.split():
        SCRATCH[_e.split(":")[0]] = ("sbuf", [128, int(_e.split(":")[1])], _d)
for _e in "pZ pD pC pL pN0 pN1 pM pK".split():
    SCRATCH[_e] = ("psum", [128, 512], "float32")
SEMAPHORES = ["v", "s", "t", "p", "lo", "d_xs", "d_lim", "d_yn", "d_yo", "d_yx", "d_yj"] + ["d_nb%d" % j for j in range(4)] + [
    "a%d_%d_%d" % (k, t, q) for k in (1, 2) for t in range(R) for q in range(N)] + ["a3_%d_%d" % (t, q) for t in (0, 4) for q in range(N)]


def queues(g, T):
    eng = {"v": g.vector, "s": g.scalar, "t": g.tensor, "p": g, "y": g.sync}
    cnt = {"v": 0, "s": 0, "t": 0, "p": 0}
    know = {q: {} for q in eng}
    seen, total = {}, {}

    def meet(x, y):
        return x[1] < y[2] and y[1] < x[2] and not (x[3] == y[3] and x[3] > 1 and (x[1] - y[1]) % x[3])

    def before(q, R_, W_):
        need = []
        for pcs, w in ((R_, False), (W_, True)):
            for x in pcs:
                bank = x[0][0] == "p"
                for y, w2, tok in seen.get(x[0], []):
                    if tok[3] == q == "t":
                        continue
                    if (bank and tok[3] != q) or ((w or w2) and meet(x, y)):
                        need.append(tok)
        for sem, val, clock, _ in sorted(need, key=lambda z: -z[1]):
            if know[q].get(sem, 0) < val:
                eng[q].wait_ge(T.sem[sem], val)
                know[q][sem] = val
            for k, n in clock.items():
                if know[q].get(k, 0) < n:
                    know[q][k] = n

    def after(tok, R_, W_):
        for pcs, w in ((R_, False), (W_, True)):
            for x in pcs:
                old = seen.get(x[0], [])
                if w and x[3] == 1:
                    old = [e for e in old if not (x[1] <= e[0][1] and e[0][2] <= x[2])]
                old = [e for e in old if not (e[0] == x and e[1] == w and e[2][0] == tok[0])]
                seen[x[0]] = old + [(x, w, tok)]

    def op(q, fns, R_, W_):
        before(q, R_, W_)
        for f in fns:
            ins = f()
        cnt[q] += 1
        ins.then_inc(T.sem[q], 1)
        after((q, cnt[q], dict(know[q]), q), R_, W_)

    def dma(q, sem, fns, R_, W_):
        before(q, R_, W_)
        for f in fns:
            total[sem] = total.get(sem, 0) + 16
            f().then_inc(T.sem[sem], 16)
        after((sem, total[sem], dict(know[q]), "dma"), R_, W_)

    def arrive(sem, n, W_):
        total[sem] = n
        after((sem, n, {}, "far"), (), W_)

    def finish(extra):
        for sem, n in list(cnt.items()) + list(total.items()) + extra:
            if n and know["y"].get(sem, 0) < n:
                g.sync.wait_ge(T.sem[sem], n)

    return op, dma, arrive, finish, before


def rank_program(g, core, T, topo):
    r = T.rank_of(core)
    if r is None:
        return
    vec, sca, ten = g.vector, g.scalar, g.tensor
    op, dma, arrive, finish, before = queues(g, T)
    others = [d for d in T.cores if d != core]

    def b(name, c0=0, c1=None, st=1):
        c1 = SCRATCH[name][1][1] if c1 is None else c1
        return (T[name][:, c0:c1:st], [(name, c0, c1 - (c1 - c0 - 1) % st, st)])

    def by(win, off):
        return (win[0].indirect(off[0]), win[1], off[1])

    def call(q, f, out, ins, more=()):
        aps = [x[0] if isinstance(x, tuple) else x for x in ins]
        R_ = [pc for x in ins if isinstance(x, tuple) for part in x[1:] for pc in part] + (out[2] if len(out) > 2 else [])
        op(q, [lambda: f(out[0], *aps)], R_, out[1] + [pc for x in more for pc in x[1]])

    def cp(out, x):
        call("v", lambda o, i: vec.tensor_copy(out=o, in_=i), out, [x])

    def tt(out, x, y, o1):
        call("v", lambda o, i, j: vec.tensor_tensor(out=o, in0=i, in1=j, op=o1), out, [x, y])

    def ts(out, x, s1, o1, s2=None, o2=None):
        if o2 is None:
            call("v", lambda o, i, u: vec.tensor_scalar(out=o, in0=i, scalar1=u, scalar2=None, op0=o1), out, [x, s1])
        else:
            call("v", lambda o, i, u, w: vec.tensor_scalar(out=o, in0=i, scalar1=u, scalar2=w, op0=o1, op1=o2), out, [x, s1, s2])

    def scan(out, d0, d1, o0, o1, first=0.0):
        call("v", lambda o, i, j: vec.tensor_tensor_scan(out=o, data0=i, data1=j, initial=first, op0=o0, op1=o1), out, [d0, d1])

    def fill(out, x):
        call("v", lambda o: vec.memset(o, x), out, [])

    def act(out, x, func=F.Copy, bias=0.0, scale=1.0, total=None):
        if total is None:
            call("s", lambda o, i, u, w: sca.activation(o, i, func, bias=u, scale=w), out, [x, bias, scale])
        else:
            call("s", lambda o, i, u, w: sca.activation(o, i, func, bias=u, scale=w, accum_out=total[0]), out, [x, bias, scale], [total])

    def move(q, out, x):
        (act if q == "s" else cp)(out, x)

    def iota(out, pattern, base, cm):
        call("p", lambda o: g.iota(o, pattern, base, cm, allow_small_or_imprecise_dtypes=True), out, [])

    def select(out, x, pattern, cmp_, other, base, cm):
        call("p", lambda o, i: g.affine_select(o, i, pattern, cmp_, other, base, cm), out, [x])

    def pe(out, terms, start=True, stop=True):
        fns = [lambda j=j, l=l, x=x: ten.matmul(out[0], l[0], x[0], start and j == 0, stop and j == len(terms) - 1) for j, (l, x) in enumerate(terms)]
        op("t", fns, [pc for l, x in terms for pc in l[1] + x[1]], out[1])

    def lists(out, name, c0, c1):
        pe(out, [(b("JM", 128 * m, 128 * m + 128), b(name, c0 + m, c1, 16)) for m in range(16)])

    def blk(name, t, q, n=1):
        return b(name, B0 + 64 * (4 * t + q), B0 + 64 * (4 * t + q + n))

    def mb(t, q, c0, c1):
        return b("MB", SM * (4 * t + q) + c0, SM * (4 * t + q) + c1)

    def sized(t, q):
        return mb(t, q, 0, 64) if t else b("SB", 64 * q, 64 * q + 64)

    def cu(t, q, c0, c1):
        return b("CU", SC * (4 * t + q) + c0, SC * (4 * t + q) + c1)

    def col(j):
        return b("TC", j, j + 1)

    dma("s", "d_lim", [lambda: g.scalar.dma_start(T.LIMI[:], T.lim[:])], (), b("LIMI")[1])
    dma("y", "d_xs", [lambda: g.sync.dma_start(T.XB[:, NAT:PAD], T.xs[:])], (), b("XB", NAT, PAD)[1])
    for j, (a, e) in enumerate(PIECES):
        dma("y", "d_nb%d" % j, [lambda: g.sync.dma_start(T.NB[:, NAT + 16 * a:NAT + 16 * e], T.nb[:, 16 * a:16 * e])],
            (), b("NB", NAT + 16 * a, NAT + 16 * e)[1])

    iota(b("TCI", 0, 1), [[1, 1]], 0, 1)
    fill(b("ONES"), 1.0)
    select(b("ID"), b("ONES"), [[-1, 128]], A.is_equal, 0.0, 0, 1)
    select(b("G1"), b("ONES"), [[-16, 8], [0, 16]], A.is_ge, 0.0, 0, 1)
    select(b("GG"), b("G1"), [[16, 8], [0, 16]], A.is_ge, 0.0, 15, -1)
    iota(b("TR"), [[16, 4]], 0, 0)
    iota(b("CC"), [[1, 4], [256, LS]], NAT - 1024, 0)
    iota(b("CST"), [[0, 4], [1, 64]], -64, 0)
    iota(b("SCR", 0, 160), [[16, 160]], NAT, 0)
    iota(b("LANE"), [[1, 176]], 0, 0)
    iota(b("VN"), [[16, 160]], 4 + r, 0)
    iota(b("MK1", 0, 64), [[0, 4], [1, 16]], 0, 0)
    iota(b("MK1", 64, 320), [[-16, 4], [1, 64]], 0, 0)
    for name, n, x in (("RK", 512, 128), ("RN", 512, 0), ("RST", 512, 0), ("RD", 256, 0)):
        iota(b(name), [[0, n]], x, 0)
    fill(b("ZERO"), 0.0)
    ts(b("TCI", 1, 2), b("TCI", 0, 1), 15, A.bitwise_and)
    fill(b("JM"), 0.0)
    pm = col(0)
    cp(pm, b("TCI", 1, 2))
    for name, x in (("XB", 0.0), ("XO", 0.0), ("NB", float(V))):
        fill(b(name, 0, NAT), x)
        fill(b(name, PAD, B0), x)
    e0, e1, e4, e5 = col(1), col(2), col(3), col(4)
    for c_, j in ((e0, 0), (e1, 1), (e4, 4), (e5, 5)):
        ts(c_, pm, float(j), A.is_equal)
    cp(b("LIMF"), b("LIMI"))
    for name, x in (("D1", MAGIC), ("OC", float(V)), ("QL4", 0.0)):
        fill(b(name, 160, 176), x)
    ts(b("THR"), b("LIMF"), 0.3, A.add)
    for j in range(N):
        act(b("MB", SM * j, SM * j + 64), b("ZERO", 0, 64))
    for j in range(N * R):
        act(b("MB", SM * j + 224, SM * j + SM), b("ZERO", 0, 32))
    ts(col(7), e1, 64.0, A.mult, e0, A.add)
    ts(col(17), e5, 64.0, A.mult, e4, A.add)
    ts(b("LIMF"), b("LIMF"), 0.3, A.add)
    ts(col(6), e0, -63.0, A.mult, -1.0, A.add)
    ts(b("GW"), b("GG"), col(7), A.mult)
    for m in range(16):
        act(b("JM", 128 * m + m, 128 * m + 128, 16), b("GW", m, 128, 16))
    ts(b("TR"), b("TR"), pm, A.add)
    for t in range(R):
        ts(col(12 + t), e1, -float(B0 // 64 + 1 + 4 * t + r), A.mult, e0, A.add)
    ts(b("TC", 8, 12), b("TR"), -64.5, A.add)
    ts(b("O16"), b("ONES"), 1.0 / 16.0, A.mult)
    fill(b("ONE"), 1.0)
    fill(b("RL"), 1.0)
    fill(b("W1"), 0.0)
    fill(b("RM"), 1.0)
    tt(col(18), e0, e4, A.add)
    ts(col(19), e4, 32.0, A.mult)
    tt(col(20), e1, e5, A.add)
    tt(col(37), e4, e5, A.add)
    fill(b("RL", 160, 161), 0.0)
    fill(b("RM", 0, 1024, 16), 0.0)
    ts(col(36), pm, 16.0, A.mult)
    for j in (4, 5):
        ts(b("W1", j, 128, 16), b("GG", j, 128, 16), -2048.0, A.mult)
    ts(col(38), col(37), 4080.0 * 2048.0, A.mult)
    for q in range(N):
        ts(col(22 + q), col(20), float(q), A.mult, col(19), A.add)
    ts(b("CC"), b("CC"), col(36), A.add)
    for t in range(R - 1):
        ts(col(31 + t), col(20), float(B0 // 64 + 1 + 4 * t), A.mult, col(38), A.add)
    for q in range(N):
        ts(b("CST", 64 * q, 64 * q + 64), b("CST", 64 * q, 64 * q + 64), col(18), A.mult, col(22 + q), A.add)
    ts(b("KT", PAD, B0), b("ZERO", 0, B0 - PAD), col(37), A.add, -4096.0, A.mult)
    for name, x in (("IDN", -8192.0), ("IDX", -1.0 / TINY), ("IDB", 4096.0), ("IDC", -4096.0), ("ID16", 16.0)):
        act(b(name), b("ID"), scale=x)
    ts(b("TR8"), b("TR"), 8192.0, A.add)
    ts(b("GJ"), b("GG"), col(17), A.mult)
    ts(b("UU"), b("SCR"), pm, A.add)

    def masks():
        ts(b("MSK", 0, 64), b("MK1", 0, 64), pm, A.not_equal, -16384.0, A.mult)
        ts(b("MSK", 64, 320), b("MK1", 64, 320), pm, A.is_ge, 4096.0, A.mult)
        for name, c0, n, st, y in (("RK", 0, 512, 16, -2.0 ** 24), ("RN", 0, 512, 16, 8192.0),
                                   ("RD", 0, 256, 64, 1.0), ("RST", 15, 512, 16, 8192.0)):
            fill(b(name, c0, n, st), y)
        ts(b("MSK"), b("MSK"), 8192.0 - DUMP - 32, A.add)

    def qf(k, name="QF", a=0, e=160):
        return b(name, 160 * k + a, 160 * k + e) if name == "QP" else b(name, 4 * a + k, 4 * e, 4)

    def places(t):
        ts(qf(t % 4, "QP"), qf(t % 4, "QW"), float(SM * 4 * t - 32), A.min)

    def expand(t, js):
        for j in js:
            select(b("QEB" if t % 2 else "QEA", j, V, 16), qf(t % 4), [[0, 160]], A.is_ge, 0.0, 0, 0)

    mask = topo.mask(core, others[0])
    for d in others:
        mask &= topo.mask(core, d)
    neng = len([e for e in topo.engines(core, others[0]) if mask >> e & 1])
    ids = [DstId(rid=topo.addr(d)[0], pnc=topo.addr(d)[1]) for d in others]
    nsend = [0]

    def send(kind, t, x):
        before("p", x[1], ())
        g.remote_dma_fused([RemoteDMATransfer(dst_ids=ids, dma_engine_mask=mask, remote_sem=T.sem["a%d_%d_%d" % (kind, t, r)],
                                              srcs=[x[0]], dsts=[x[0] for d in others])], local_sem=T.sem["lo"])
        nsend[0] += neng
    for t in range(R):
        for q in range(N):
            if q != r:
                arrive("a1_%d_%d" % (t, q), neng, mb(t, q, 0 if t else 64, 224)[1])
                arrive("a2_%d_%d" % (t, q), neng, cu(t, q, 0, (64, 68, 68, 68, 132)[t])[1])
                if t in (0, 4):
                    arrive("a3_%d_%d" % (t, q), neng, (b("LB", 256 * q, 256 * q + 256) if t else sized(t, q))[1])

    def claims(name, t, q, src):
        cp(by(b(name, DUMP, B0 + 256 * t), cu(t, q, 64, 68)), src)

    def keys(t):
        pe(b("pK", 0, 256), [(b("ID"), b("CST"))], True, False)
        for q in range(N):
            pe(b("pK", 64 * q, 64 * q + 64), [(b("W1"), sized(t, q))], False, q == N - 1)
        act(blk("KT", t, 0, 4), b("pK", 0, 256), F.Identity, bias=col(31 + t))

    def outputs(out, table, t, on="ssss"):
        for q in range(N):
            move(on[q], b(out, (4 * t + q) % 16, V, 16), by(b(table, 0, B0 + 256 * (t + 1)), b("LO", LS * q + 4, LS * q + 14)))

    def spots(t):
        lists(b("pC", 256, 256 + 4 * LS), "MB", SM * 4 * t, SM * 4 * (t + 1))

    def spots_or_own():
        tt(b("LO4"), b("pC", 256, 256 + 4 * LS), b("CC"), A.max)

    def slots(t, step):
        j, k = int(step[1]), t % 4
        a, e = COVER[j]
        x = b(("pL", "pD", "pM")[j], a, e)
        if step[0] == "l":
            ts(b("QL", a, e), x, float(PAD), A.max, float(PAD), A.subtract)
        elif step[0] == "s":
            if j in ZV:
                act(b("QLA", a, e), x)
            else:
                act(b("ELB", a, e), x, scale=128.0, bias=8192.0)
            act(b("QL4", a, e), x, F.Relu, bias=-float(PAD))
        else:
            tt(b("QX", a, e), x, qf(k, "QN", a, e), A.max)

    def but_own(t, j):
        if t < R:
            [lambda: tt(b("QA", 0, 160), qf(t % 4), b("VN"), A.is_equal), lambda: ts(b("QB", 0, 160), b("QA", 0, 160), float(V), A.mult),
             lambda: tt(b("QM", 160 * (t % 2), 160 * (t % 2) + 160), qf(t % 4), b("QB", 0, 160), A.max)][j]()

    def limits(j):
        [lambda: cp(b("AI"), b("pK", 500, 501)), lambda: ts(b("AJ"), b("AI"), 7, A.bitwise_and), lambda: tt(b("THR"), b("LIMF"), b("AJ"), A.add)][j]()

    def follow(t, js, on="s"):
        for j in js:
            move(on, b("MB", SM * j + 64, SM * j + 224), by(b("KT", PAD, B0 + 256 * t), b("JL", LS * j + 4, LS * j + 14)))

    def variables(js):
        for j in js:
            act(blk("VR", 0, j), b("LB", 256 * (j % 4) + 64 * (j // 4), 256 * (j % 4) + 64 * (j // 4) + 64), scale=16.0, bias=float(j))

    def again(out, table):
        for q in range(N):
            select(b(table, NAT + q, PAD, 16), b(out, q, V, 16), [[0, 160]], A.is_ge, 0.0, 0, 0)

    def pristine(t):
        for q in range(N):
            act(blk("XO", t, q), sized(t, q), scale=-1.0, bias=255.0)

    def new_sizes(t):
        for q in range(N):
            act(blk("XB", t, q), sized(t, q), scale=TINY, bias=-255.0 * TINY)
        keys(t)

    ORDER = [r] + [q for q in (3, 2, 1, 0) if q != r]
    for t in range(R):
        k = t % 4
        top = B0 + 256 * t
        qe = "QEB" if t % 2 else "QEA"
        if t == 0:
            for j, (a, e) in enumerate(PIECES):
                m = (a + e) // 2
                ts(b("XL", a, e), b("NB", NAT + 16 * a + r, NAT + 16 * e, 16), float(NAT), A.add)
                act(b("XG", 16 * a, 16 * m), by(b("XB", 0, B0), b("XL", a, m)))
                cp(b("XG", 16 * m, 16 * e), by(b("XB", 0, B0), b("XL", m, e)))
                if j:
                    a0 = a if j > 1 else 0
                    pe(b("pD", a0, e), [(b("ID"), b("XG", 16 * a0 + i, 16 * e, 16)) for i in range(16)])
                act(b("QF", 4 * a, 4 * e), b("NB", NAT + 16 * a + r, NAT + 16 * e, 4))
            cp(b("OC", 0, 160), qf(0))
            act(b("QW"), b("QF"), bias=-7.5)
            act(b("QA"), b("QW"), scale=1.0 / 16.0, bias=MAGIC)
            expand(1, range(E0))
        else:
            if t < 4:
                expand(t + 1, range(16))
                iota(b("VN"), [[16, 160]], 4 * ((t + 1) % 4) + r, 0)
            else:
                send(3, t, b("LB", 256 * r, 256 * r + 256))
                iota(b("VR", 0, B0), [[1, B0]], -NAT, 0)
            banks = ("pZ", "pN0", "pN1")

            def cover(j):
                a, e = COVER[j]
                tt(b("EQ", 16 * a, 16 * e), by(b("NB", PAD, top), b("QL", a, e)), b(qe, 16 * a, 16 * e), A.not_equal if j in ZV else A.is_equal)
                if j not in ZV:
                    pe(b(banks[j], a, e), [(b("ID"), b("ELB", a, e))] + [(b("IDN"), b("EQ", 16 * a + i, 16 * e, 16)) for i in range(16)])
                if j == 0 and t > 1:
                    lists(b("pK", 256, 256 + 4 * LS * (t - 1)), "MB", 0, SM * 4 * (t - 1))

            def uncovered(j):
                a, e = COVER[j]
                scan(b("UN", 0, 16 * (e - a)), b("RN", 0, 16 * (e - a)), b("EQ", 16 * a, 16 * e), A.max, A.min)

            def kept_names(j):
                a, e = COVER[j]
                tt(b("XT", a, e), b("UN", 15, 16 * (e - a), 16), b("QX", a, e), A.mult)

            def pick(j):
                a, e = COVER[j]
                if j in ZV:
                    tt(b("XL4", a, e), b("XT", a, e), b("QLA", a, e), A.max)
                else:
                    tt(b("XL4", a, e), b(banks[j], a, e), b("QX", a, e), A.min)

            def sizes(j):
                a, e = COVER[j]
                cp(b("XL", a, e), b("XL4", a, e))
                move("v" if j in ZV and t == 1 else "s", b("XG", 16 * a, 16 * e), by(b("XB", 0, top), b("XL", a, e)))

            def sums(j):
                a, e = COVER[j]
                pe(b("pD", a, e), [(b("ID"), b("XG", 16 * a + i, 16 * e, 16)) for i in range(16)], True, False)
                scan(b("MXS", 16 * a, 16 * e), b("RM", 0, 16 * (e - a)), b("XG", 16 * a, 16 * e), A.mult, A.min)
                pe(b("pD", a, e), [(b("IDX"), b("MXS", 16 * a + 15, 16 * e, 16))], False, True)

            def claimed_by(name, q):
                if t > 1:
                    claims(name, t - 1, q, cu(t - 1, q, 0, 64) if name == "NB" else blk(name, t - 1, q))

            def last_names():
                outputs("YN", "NB", t - 1)

            def last_sizes():
                outputs("YX", "XO", t - 1)
                act(b("CC"), b("CC"), bias=4.0 if t < 4 else -12.0)

            def covered_rows():
                act(b("XU"), b("XL4"), F.Abs, bias=-1296.0)
                act(b("XS"), b("XL4"), F.Sign, bias=0.5, scale=-1.0)
                act(b("CW"), b("XU"), F.Relu, scale=float(V), bias=-1288.0 * V)
                act(b("CV"), b("XS"), F.Relu, scale=float(V))

            def roots():
                if t > 1:
                    ts(b("JL", 0, 4 * LS * (t - 1)), b("pK", 256, 256 + 4 * LS * (t - 1)), float(PAD), A.max, float(PAD), A.subtract)
            for step in (PLAN if t > 1 else PLAN1).split():
                if step[0] in "lqs":
                    slots(t, step)
                elif step[0] == "n":
                    cp(blk("NB", t - 1, ORDER[int(step[1])]), cu(t - 1, ORDER[int(step[1])], 0, 64))
                elif step[0] in "fxk":
                    claimed_by({"f": "NB", "x": "XB", "k": "KT"}[step[0]], int(step[1]))
                elif step[1:].isdigit():
                    {"c": cover, "u": uncovered, "w": kept_names, "p": pick, "g": sizes, "m": sums,
                     "h": lambda j: but_own(t + 1, j), "a": limits}[step[0]](int(step[1]))
                else:
                    {"o": last_names, "z": lambda: new_sizes(0), "y": last_sizes, "cv": covered_rows, "jl": roots}[step]()
            if t == 2:
                again("YN", "NB")
            if t == 3:
                again("YX", "XO")
            if t == 4:
                variables(range(8))
        ts(b("OK"), b("pD", 0, 160), b("THR"), A.is_le)
        pe(b("pC", 0, 160), ([(b("ID"), b("DEAD"))] if t == 4 else []) + [(b("GG"), b("OK"))])
        if t:
            pe(b("pM", 0, 320), [(b("ID"), b("MSK"))], True, False)
            for i in range(2):
                pe(b(("pZ", "pL")[i]), [(b("IDK"), b("ONE"))], True, False)
            for i in range(2):
                pe(b("pN%d" % i), [(b("ID"), b("RST"))], True, False)
        act(b("D1", 0, 160), b("pD", 0, 160), bias=MAGIC)
        if t:
            tt(b("OC", 0, 160), b("QM", 160 * (t % 2), 160 * (t % 2) + 160), b("CW"), A.max)
        ts(b("HH"), b("pC", 0, 160), 8.5, A.is_ge)
        scan(b("RR"), b("HH"), b("ZERO"), A.add, A.min, -65.0)
        for s in range(2):
            act(b("SG", 160 * s, 160 * s + 160), b("RR"), F.Sign, bias=col(8 + s), scale=-1.0, total=b("ACC", s, s + 1))
        for s in (2, 3):
            ts(b("SG", 160 * s, 160 * s + 160), b("RR"), col(8 + s), A.is_le)
        tt(b("YY"), b("HH"), b("RR"), A.mult)
        scan(b("SH"), b("RL"), b("SG", 320, 640), A.mult, A.add)
        ts(mb(t, r, 64, 224), b("YY"), col(6), A.max, col(12 + t), A.mult)
        if t == 0:
            send(1, t, mb(t, r, 64, 224))
        ts(b("LN", 0, 2), b("ACC"), 0.5, A.mult, 80.0, A.add)
        cp(b("LN", 2, 4), b("SH", 159, 320, 160))
        if t < 4:
            ts(b("TM"), b("RR", 159, 160), 65.0, A.add, 64.0, A.min)
            pe(b("pK", 500, 501), [(b("O16"), b("TM"))])
        ln = b("LN")
        if t == 0:
            act(b("QB"), b("QF"), scale=float(SM), bias=64.0)
            ts(b("QA"), b("QA"), MAGIC, A.subtract, 1.0 - 16.0 * SM, A.mult)
        else:
            cp(b("QC"), by(b("QL4"), ln))
        act(sized(t, r), by(b("D1"), ln), F.Relu, bias=MAGIC + 255.0, scale=-1.0)
        if t == 0:
            act(b("LV"), by(b("LANE"), ln), scale=16.0, bias=float(r))
            act(b("OCC"), by(b("OC"), ln))
            tt(b("NE"), b("OCC"), b("LV"), A.is_equal)
            act(b("NF"), b("NE"), scale=4096.0, bias=8192.0)
            tt(b("OC8"), b("OCC"), b("NF"), A.add)
            ts(cu(t, r, 0, 64), b("OC8"), 8192.0, A.subtract, float(V), A.min)
            send(2, t, cu(t, r, 0, 64))
            send(3, t, sized(t, r))
        else:
            send(1, t, mb(t, r, 0, 224))

            def gather(name, table, on):
                for i in range(2):
                    move(on[i], b(name, 512 * i, 512 * i + 512), by(b(table, PAD, top), b("QC", 32 * i, 32 * i + 32)))

            def best(i):
                scan(b("TS", 512 * i, 512 * i + 512), b("RK"), b("KG", 512 * i, 512 * i + 512), A.add, A.max)

            def rounded():
                ts(b("RK1"), b("TS", 15, 1024, 16), MAGIC128, A.add, MAGIC128, A.subtract)

            def claimed():
                tt(b("TF"), b("TS", 15, 1024, 16), b("RK1"), A.subtract)
                for s in range(5):
                    pe(b("pM", 64 * s, 64 * s + 64), [(b("GJ"), b("TF"))], False, s == 4)

            def diagonal():
                scan(b("EWS"), b("RM", 0, 64), b("pM", 0, 64), A.mult, A.max)

            def first():
                for s in range(4):
                    ew = b("EWS", 16 * s + 15, 16 * s + 16)
                    ts(b("DC", 64 * s, 64 * s + 64), b("pM", 64 * s + 64, 64 * s + 128), ew, A.not_equal)

            def alone():
                scan(b("DS"), b("RD"), b("DC"), A.max, A.min)

            def kept():
                tt(b("ST", 64, 68), b("EK"), b("TR8"), A.max)

            def mine(j):
                tt(b("MM", 256 * j, 256 * j + 256), b(("pZ", "pL")[j // 2], 256 * (j % 2), 256 * (j % 2) + 256), b("QG", 256 * j, 256 * j + 256), A.is_equal)

            def steps(j):
                a, e, bank, c0 = 256 * j, 256 * j + 256, "pN%d" % (j // 2), 256 * (j % 2)
                pe(b(bank, c0, c0 + 256), [(b("IDB"), b("MM", a, e))], False, False)
                pe(b(bank, c0, c0 + 255), [(b("IDC"), b("MM", a + 1, e))], False, False)
                pe(b(bank, c0 + 15, c0 + 255, 16), [(b("IDB"), b("MM", a + 16, e, 16))], False, j % 2 == 1)

            def least(i):
                scan(b("NS", 512 * i, 512 * i + 512), b("QG", 512 * i, 512 * i + 512), b("pN%d" % i), A.min, A.add, 8192.0)

            def new_names():
                tt(b("ST", 0, 64), b("NS", 15, 1024, 16), b("OC8"), A.min)

            def covered():
                if t == 4:
                    tt(b("CV"), b("CV"), b("LIVE"), A.mult)
                x = b("NB", NAT + 4 * k + r, PAD, 16)
                tt(x, x, b("CV"), A.max)

            name, c0 = ("LB", 256 * r + 64 * t) if t < 4 else ("LC", 0)
            act(b(name, c0, c0 + 64), by(b("LANE"), ln))
            for i in range(2):
                for j in range(16):
                    pe(b(("pZ", "pL")[i], j, 512, 16), [(b("ID16"), b(name, c0 + 32 * i, c0 + 32 * i + 32))], False, j == 15)
            gather("KG", "KT", "vs")
            gather("QG", "NB", "ss")
            act(b("OC8"), by(b("OC"), ln), bias=8192.0)
            best(0)
            best(1)
            if t == 4:
                cp(cu(t, r, 68, 132), by(b("LANE"), ln))
            rounded()
            mine(0)
            claimed()
            steps(0)
            for j in (1, 2, 3):
                if j == 3:
                    diagonal()
                mine(j)
                steps(j)
            first()
            least(0)
            alone()
            if t == 4:
                follow(t, range(5))
                pristine(t)
                spots(t)
                follow(t, range(5, 12))
                pe(b("pD", 0, 160), [(b("JM", 128 * c, 128 * c + 128), b("MB", SM * c + 64, SM * c + 224)) for c in range(16)])
            tt(b("EK"), b("DS", 63, 256, 64), b("EWS", 15, 64, 16), A.mult)
            least(1)
            kept()
            new_names()
            ts(cu(t, r, 0, 68), b("ST"), 8192.0, A.subtract, float(V), A.min)
            send(2, t, cu(t, r, 0, 68 if t < 4 else 132))
            if t == 4:
                break
            if t == 1:
                pristine(0)
                last_names()
                last_sizes()
            follow(t, range(4 * (t - 1)))
        if t == 0:
            act(b("LB", 256 * r, 256 * r + 64), by(b("LANE"), ln))
        act(b("IDK"), b("ID"), scale=float(4 * ((t + 1) % 4) + r))
        if t == 0:
            expand(1, range(E0, E1))
            tt(b("QW"), b("QA"), b("QB"), A.add)
            act(b("QN"), b("QF"), bias=float(NAT))
            places(1)
            for j in range(E1, 16):
                act(b("QEB", j, V, 16), qf(1))
            act(b("XO", NAT, PAD), b("XB", NAT, PAD))
            masks()
            ts(b("DEAD"), b("YY"), -0.5, A.is_lt, -16.0, A.mult)
            ts(b("LIVE"), b("YY"), -0.5, A.is_ge)
            for j in (2, 3, 4):
                places(j)

        def gather_map(on):
            for a, e, q in ((0, 64, "s"), (128, 160, "s"), (64, 128 - SHARE[t], "s"), (128 - SHARE[t], 128, "v")) if t else LISTS0:
                if q == on:
                    move(q, b("GM", 16 * a, 16 * e), by(b("MB", 0, SM * 4 * (t + 1)), qf((t + 1) % 4, "QP", a, e)))
        if t:
            covered()
        else:
            for j in range(3):
                but_own(1, j)
        gather_map("s")
        spots(t)
        gather_map("v")
        for j in LORD if t else range(3):
            a, e = COVER[j]
            lists(b(("pL", "pD", "pM")[j], a, e), "GM", 16 * a, 16 * e)
        spots_or_own()
        slots(t + 1, "l0")
        cp(b("LO"), b("LO4"))
        for step in ("q0", "s0"):
            slots(t + 1, step)
        if t:
            new_sizes(t)
            pristine(t)
    def last_variables(q):
        ts(blk("VR", 4, q), cu(4, q, 68, 132), 16.0, A.mult, float(q), A.add)
    spots_or_own()
    cp(blk("NB", 4, r), cu(4, r, 0, 64))
    cp(b("LO"), b("LO4"))
    last_variables(r)
    outputs("YX", "XO", 4, "vvss")
    dma("y", "d_yx", [lambda: g.sync.dma_start(T.yx[:], T.YX[:])], b("YX")[1], ())
    covered()
    variables(range(8, 16))
    for q in ORDER[1:]:
        cp(blk("NB", 4, q), cu(4, q, 0, 64))
    for a, e, sem in ((0, 6, "d_yn"), (6, 10, "d_yo")):
        for q in range(N):
            move("v" if a == 0 and q < 2 else "s", b("YN", 256 * a + q, 256 * e, 16), by(b("NB"), b("LO", LS * q + 4 + a, LS * q + 4 + e)))
        dma("y", sem, [lambda: g.sync.dma_start(T.yn[:, 256 * a:256 * e], T.YN[:, 256 * a:256 * e])], b("YN", 256 * a, 256 * e)[1], ())
    for q in (4, 3, 2, 1, 0):
        if q and q - 1 != r:
            last_variables(q - 1)
        if q < 4:
            claims("VR", 4, q, blk("VR", 4, q))
        if q == 3:
            tt(b("OL4"), b("pD", 0, 160), b("UU"), A.max)
        if q == 1:
            cp(b("OL"), b("OL4"))
    cp(b("YJ", 0, 1280), by(b("VR", 0, B0 + 1024), b("OL", 0, 80)))
    act(b("YJ", 1280, V), by(b("VR", 0, B0 + 1024), b("OL", 80, 160)))
    dma("s", "d_yj", [lambda: g.scalar.dma_start(T.yj[:], T.YJ[0:128:16, :])], b("YJ")[1], ())
    finish([("lo", nsend[0])])
